import numpy as np
import ml_dtypes


def mxq(x, axis, fmt="e4m3"):
    dtype, down = {"e4m3": (ml_dtypes.float8_e4m3fn, 7), "e5m2": (ml_dtypes.float8_e5m2, 14)}[fmt]
    v = np.moveaxis(np.asarray(x, np.float32).astype(ml_dtypes.bfloat16).astype(np.float64), axis, -1)
    blocks = v.reshape(v.shape[:-1] + (-1, 32))
    amax = np.abs(blocks).max(-1, keepdims=True)
    byte = np.maximum(np.where(amax > 0, np.frexp(amax)[1] - 1 + 127, 0) - down, 1)
    scale = np.exp2(byte - 127.0)
    codes = (blocks / scale).astype(np.float32).astype(dtype).astype(np.float64)
    return np.moveaxis((codes * scale).reshape(v.shape), -1, axis)


WIDE = False


def mx_kscale(k):
    if not WIDE:
        return np.ones(k)
    levels = np.array([10, -10, 5, -5, 0])
    if k % 512:
        return np.exp2(np.random.permutation(np.resize(levels, k // 32))).repeat(32)
    a = np.empty((k // 512, 16))
    for p in range(k // 512):
        a[p, :8] = np.random.permutation(np.resize(levels, 8))
        for g in range(8):
            far = levels[np.abs(levels - a[p, g]) >= 10]
            a[p, g + 8] = far[np.random.randint(len(far))]
    return np.exp2(a.ravel()).repeat(32)


def f64(x):
    return np.asarray(x).astype(np.float64)


def striped(idx):
    return np.tile(idx.reshape(-1, 16).T, (8, 1)).astype(np.uint16)


def unstriped(offs):
    return offs[:16].T.reshape(-1).astype(np.int64)


E2M1 = np.array([0.0, 0.5, 1.0, 1.5, 2.0, 3.0, 4.0, 6.0, -0.0, -0.5, -1.0, -1.5, -2.0, -3.0, -4.0, -6.0])


def pack_weight(w, fmt):
    k, n = w.shape
    w = f64(np.asarray(w, np.float32).astype(ml_dtypes.bfloat16)).reshape(k // 32, 32, n)
    amax = np.abs(w).max(1)
    if fmt == "e4m3":
        byte = np.frexp(amax)[1] - 1 + 127 - 7
    else:
        mant, ex = np.frexp(amax / 6.0)
        byte = np.where(mant > 0.5, ex, ex - 1) + 127
    byte = np.clip(np.where(amax > 0, byte, 1), 1, 254)
    scaled = (w * np.exp2(127.0 - byte)[:, None, :]).reshape(k, n).astype(np.float32)
    by_word = np.ascontiguousarray(scaled.reshape(k // 512, 128, 4, n).transpose(0, 1, 3, 2))
    if fmt == "e4m3":
        words = by_word.astype(ml_dtypes.float8_e4m3fn).view(np.uint8)
    else:
        c = by_word.astype(ml_dtypes.float4_e2m1fn).view(np.uint8) & 0xF
        words = (c[..., 0::2] | (c[..., 1::2] << 4)).reshape(k // 512, 128, 2 * n)
    return np.ascontiguousarray(words), np.ascontiguousarray(byte.astype(np.uint8).reshape(k // 512, 16, n))


def unpack_weight(words, scales, fmt):
    g, _, n = scales.shape
    words = np.ascontiguousarray(words).reshape(g, 128, n, -1)
    if fmt == "e4m3":
        vals = words.view(ml_dtypes.float8_e4m3fn).astype(np.float64)
    else:
        nib = np.empty((g, 128, n, 4), np.uint8)
        nib[..., 0::2] = words & 0xF
        nib[..., 1::2] = words >> 4
        vals = E2M1[nib]
    vals = vals * np.repeat(np.exp2(scales.astype(np.float64) - 127.0), 8, axis=1)[..., None]
    return vals.transpose(0, 1, 3, 2).reshape(g * 512, n)


def silu(v):
    return v / (1.0 + np.exp(-np.maximum(v, -700.0)))


K, T, E, C, F, D, H = 1024, 1024, 8, 128, 2, 256, 512
N = 512


def by_expert(wq, xq, E, C):
    return np.concatenate([wq[e].T @ xq[:, e * C:(e + 1) * C] for e in range(E)], axis=1)


def setup_inputs():
    n = np.random.standard_normal
    s = mx_kscale(K)
    u = mx_kscale(H)
    slot_token = np.random.permutation(T)[:E * C]
    slots2 = np.random.permutation(T)[:F * D]
    x = pack_weight(n((K, T)) * s[:, None], "e4m3")
    w = [pack_weight(m, "e4m3") for m in n((E, K, N)) / np.sqrt(K) / s[None, :, None]]
    wa = [pack_weight(m, "e2m1") for m in n((F, K, H)) / np.sqrt(K) / s[None, :, None] * u]
    wb = [pack_weight(m, "e2m1") for m in n((F, H, N)) / np.sqrt(H) / u[None, :, None]]
    return {
        "x_words": x[0],
        "x_scales": x[1],
        "w_words": np.stack([m[0] for m in w]),
        "w_scales": np.stack([m[1] for m in w]),
        "wa_words": np.stack([m[0] for m in wa]),
        "wa_scales": np.stack([m[1] for m in wa]),
        "wb_words": np.stack([m[0] for m in wb]),
        "wb_scales": np.stack([m[1] for m in wb]),
        "gate": np.tile(np.random.uniform(0.2, 1.0, E * C), (128, 1)).astype(np.float32),
        "gate2": (np.tile(np.random.uniform(0.2, 1.0, F * D), (128, 1))).astype(np.float32),
        "offs": striped(slot_token),
        "offs2": striped(slots2),
    }


def reference(x_words, x_scales, w_words, w_scales, wa_words, wa_scales, wb_words, wb_scales, gate, gate2, offs, offs2):
    w = np.stack([unpack_weight(w_words[e], w_scales[e], "e4m3") for e in range(E)])
    wa = np.stack([unpack_weight(wa_words[e], wa_scales[e], "e2m1") for e in range(F)])
    wb = np.stack([unpack_weight(wb_words[e], wb_scales[e], "e2m1") for e in range(F)])
    idx, idx2 = unstriped(offs), unstriped(offs2)
    x = unpack_weight(x_words, x_scales, "e4m3")
    y = by_expert(w, x[:, idx], E, C)
    h = silu(by_expert(wa, x[:, idx2], F, D))
    z = by_expert(wb, mxq(h, 0, "e4m3"), F, D)
    out = np.zeros((N, T))
    out[:, idx] = f64(gate[:1]) * y
    out[:, idx2] += f64(gate2[:1]) * z
    return out

@@ -1,0 +1,224 @@
+from contextlib import ExitStack
+
+import concourse.mybir as mybir
+from concourse.masks import make_identity
+
+K, T, E, C, F, D, H, N = 1024, 1024, 8, 128, 2, 256, 512, 512
+FLOPS = 2 * (K * N * E * C + K * H * F * D + H * N * F * D)
+
+F32 = mybir.dt.float32
+BF16 = mybir.dt.bfloat16
+I32 = mybir.dt.int32
+U32 = mybir.dt.uint32
+U16 = mybir.dt.uint16
+U8 = mybir.dt.uint8
+FP8X4 = mybir.dt.float8_e4m3fn_x4
+FP4X4 = mybir.dt.float4_e2m1fn_x4
+COPY = mybir.ActivationFunctionType.Copy
+SILU = mybir.ActivationFunctionType.Silu
+ADD = mybir.AluOpType.add
+
+P = 128
+PASSES = K // 512
+QUADS = 4
+ROWS = 4
+GROUP = 512
+NT = N // P
+
+
+def tile_moe_mlr_silu_kernel(
+    tc, x_words, x_scales, w_words, w_scales, wa_words, wa_scales, wb_words, wb_scales, gate, gate2, offs, offs2, out
+):
+    nc = tc.nc
+    with ExitStack() as ctx:
+        keep = ctx.enter_context(tc.tile_pool(name="keep", bufs=1))
+        ring = ctx.enter_context(tc.tile_pool(name="ring", bufs=3))
+        mm_ps = ctx.enter_context(tc.psum_pool(name="mm_ps", bufs=3))
+        tr_ps = ctx.enter_context(tc.psum_pool(name="tr_ps", bufs=3))
+        h_ps = ctx.enter_context(tc.psum_pool(name="h_ps", bufs=2))
+
+        offs_sb = keep.tile([P, T // 16], U16, name="offs_sb")
+        offs2_sb = keep.tile([P, F * D // 16], U16, name="offs2_sb")
+        x_sb = [keep.tile([P, T], I32, name="x_sb%d" % s, align_bytes=64) for s in range(PASSES)]
+        xs_both = keep.tile([P, T], U8, name="xs_both", align_bytes=64)
+        xs_last = keep.tile([P, T], U8, name="xs_last", align_bytes=64)
+        w_sb = [keep.tile([P, PASSES, 4 * N], U8, name="w_sb%d" % e, align_bytes=64) for e in range(E)]
+        ws_sb = keep.tile([P, E * PASSES, N], U8, name="ws_sb", align_bytes=64)
+        wa_sb = keep.tile([P, F * PASSES, 2 * H], U8, name="wa_sb", align_bytes=64)
+        was_sb = keep.tile([P, F * PASSES, H], U8, name="was_sb", align_bytes=64)
+        wb_sb = keep.tile([P, F, 2 * N], U8, name="wb_sb", align_bytes=64)
+        wbs_sb = keep.tile([P, F, N], U8, name="wbs_sb", align_bytes=64)
+        gate_rows = keep.tile([P, P], F32, name="gate_rows")
+        gate_cols = keep.tile([P, 16], F32, name="gate_cols")
+        ident32 = keep.tile([P, P], F32, name="ident32")
+        ident16 = keep.tile([P, P], BF16, name="ident16")
+        o_sb = [keep.tile([P, T], F32, name="o_sb%d" % j) for j in range(NT)]
+        z_sb = [keep.tile([P, T], F32, name="z_sb%d" % j) for j in range(NT)]
+
+        def zero(tile_ap):
+            nc.vector.memset(tile_ap.bitcast(I32), 0)
+
+        zero(xs_both[:])
+        zero(ws_sb[:].rearrange("p a n -> p (a n)"))
+        zero(xs_last[:])
+        zero(was_sb[:].rearrange("p a n -> p (a n)"))
+        zero(wbs_sb[:].rearrange("p a n -> p (a n)"))
+        nc.gpsimd.memset(gate_rows[:], 0.0)
+        make_identity(nc, ident32[:])
+        make_identity(nc, ident16[:])
+        for j in range(NT):
+            nc.gpsimd.memset(z_sb[j][:], 0.0)
+
+        def load_x(s):
+            nc.sync.dma_start(x_sb[s][:], x_words[s].rearrange("p t d -> p (t d)").bitcast(I32))
+
+        def load_planes(dst, src):
+            for q in range(QUADS):
+                nc.sync.dma_start(
+                    dst[32 * q : 32 * q + ROWS, :, :].bitcast(I32),
+                    src[:, ROWS * q : ROWS * (q + 1), :].rearrange("a r n -> r a n").bitcast(I32),
+                )
+
+        def load_w(e):
+            nc.sync.dma_start(w_sb[e][:].bitcast(I32), w_words[e].rearrange("s p n d -> p s (n d)").bitcast(I32))
+
+        nc.sync.dma_start(offs_sb[:], offs)
+        load_x(0)
+        load_x(1)
+        for q in range(QUADS):
+            nc.sync.dma_start(
+                xs_both[32 * q : 32 * q + PASSES * ROWS, :].bitcast(I32),
+                x_scales[:, ROWS * q : ROWS * (q + 1), :].bitcast(I32),
+            )
+        nc.sync.dma_start(offs2_sb[:], offs2)
+        load_planes(ws_sb, w_scales.rearrange("e s b n -> (e s) b n"))
+        for e in range(E // 2):
+            load_w(e)
+        nc.sync.dma_start(gate_rows[0:E, :], gate[0].rearrange("(e p) -> e p", p=P))
+        nc.sync.dma_start(gate_rows[E : E + 4, :], gate2[0].rearrange("(e p) -> e p", p=P))
+        for q in range(QUADS):
+            nc.sync.dma_start(
+                xs_last[32 * q : 32 * q + ROWS, :].bitcast(I32),
+                x_scales[1, ROWS * q : ROWS * (q + 1), :].bitcast(I32),
+            )
+        for e in range(E // 2, E):
+            load_w(e)
+        load_planes(was_sb, wa_scales.rearrange("f s b n -> (f s) b n"))
+        nc.sync.dma_start(wa_sb[:].bitcast(I32), wa_words.rearrange("f s p n -> p (f s) n").bitcast(I32))
+        load_planes(wbs_sb, wb_scales.rearrange("f s b n -> (f s) b n"))
+        nc.sync.dma_start(wb_sb[:].bitcast(I32), wb_words.rearrange("f s p n -> p (f s) n").bitcast(I32))
+
+        g_ps = tr_ps.tile([P, NT, P], F32, name="turned", tag="turned")
+        nc.tensor.transpose(g_ps[:, 0, :], gate_rows[:], ident32[:])
+        nc.scalar.copy(gate_cols[:], g_ps[:, 0, 0:16])
+
+        def gather_words(name, offsets):
+            tiles = []
+            for s in range(PASSES):
+                g = keep.tile([P, GROUP], U32, name="%s_words%d" % (name, s), align_bytes=64)
+                nc.vector.tensor_copy(g[:], x_sb[s][:].bitcast(U32).indirect(offsets))
+                tiles.append(g)
+            return tiles
+
+        def gather_bytes(name, window, offsets):
+            g = keep.tile([P, GROUP], U8, name=name, align_bytes=64)
+            nc.vector.tensor_copy(g[:], window[:].indirect(offsets))
+            return g
+
+        def turn_gated(acc, gate_col, dst, u):
+            gated = ring.tile([P, N], F32, name="gated")
+            nc.scalar.activation(gated[:], acc[:], COPY, scale=gate_cols[:, gate_col : gate_col + 1])
+            turned = tr_ps.tile([P, NT, P], F32, name="turned", tag="turned")
+            for j in range(NT):
+                nc.tensor.transpose(turned[:, j, :], gated[:, j * P : (j + 1) * P], ident32[:])
+            nc.scalar.copy(dst[:, :, u * P : (u + 1) * P], turned[:])
+
+        def experts(half, words, scales):
+            y = keep.tile([P, NT, GROUP], F32, name="y%d" % half)
+            for u in range(GROUP // C):
+                e = half * (GROUP // C) + u
+                cols = slice(u * C, (u + 1) * C)
+                acc = mm_ps.tile([P, N], F32, name="acc", tag="acc")
+                for s in range(PASSES):
+                    nc.tensor.matmul_mx(
+                        out=acc[:],
+                        lhsT=words[s][:, cols].bitcast(FP8X4),
+                        lhsT_scale=scales[ROWS * s : P, cols],
+                        rhs=w_sb[e][:, s, :].bitcast(FP8X4),
+                        rhs_scale=ws_sb[:, e * PASSES + s, :],
+                        start=(s == 0),
+                        stop=(s == PASSES - 1),
+                    )
+                turn_gated(acc, e, y, u)
+            return y
+
+        half_offs = [offs_sb[:, 0:32], offs_sb[:, 32:64]]
+        e_words = []
+        e_scales = []
+        for half in range(2):
+            e_words.append(gather_words("e%d" % half, half_offs[half]))
+            e_scales.append(gather_bytes("e%d_bytes" % half, xs_both, half_offs[half]))
+        a_words = gather_words("a", offs2_sb[:])
+        a_scales = [gather_bytes("a_bytes0", xs_both, offs2_sb[:]), gather_bytes("a_bytes1", xs_last, offs2_sb[:])]
+
+        y0 = experts(0, e_words[0], e_scales[0])
+        y1 = experts(1, e_words[1], e_scales[1])
+
+        h_in = keep.tile([P, GROUP, 4], BF16, name="h_in", align_bytes=64)
+        for u in range(GROUP // P):
+            f = u * P // D
+            cols = slice(u * P, (u + 1) * P)
+            acc = mm_ps.tile([P, N], F32, name="acc", tag="acc")
+            for s in range(PASSES):
+                nc.tensor.matmul_mx(
+                    out=acc[:],
+                    lhsT=a_words[s][:, cols].bitcast(FP8X4),
+                    lhsT_scale=a_scales[s][:, cols],
+                    rhs=wa_sb[:, f * PASSES + s, :].bitcast(FP4X4),
+                    rhs_scale=was_sb[:, f * PASSES + s, :],
+                    start=(s == 0),
+                    stop=(s == PASSES - 1),
+                )
+            h_rows = ring.tile([P, 4, P], BF16, name="h_rows")
+            nc.scalar.activation(h_rows[:], acc[:].rearrange("m (p t) -> m t p", t=4), SILU)
+            h_turned = h_ps.tile([P, 4, P], BF16, name="h_turned")
+            for t in range(4):
+                nc.tensor.transpose(h_turned[:, t, :], h_rows[:, t, :], ident16[:])
+            nc.scalar.copy(h_in[:, cols, :], h_turned[:].rearrange("p t m -> p m t"))
+
+        def scatter_y(j, half, y):
+            nc.vector.tensor_copy(o_sb[j][:].indirect(half_offs[half]), y[:, j, :])
+
+        scatter_y(0, 0, y0)
+        scatter_y(1, 0, y0)
+
+        h_codes = keep.tile([P, GROUP], U32, name="h_codes", align_bytes=64)
+        h_scales = keep.tile([P, GROUP], U8, name="h_scales", align_bytes=64)
+        nc.vector.quantize_mx(
+            out=h_codes[:].bitcast(FP8X4), scales=h_scales[:], in_=h_in[:].rearrange("p m t -> p (m t)")
+        )
+        z = keep.tile([P, NT, GROUP], F32, name="z")
+        for u in range(GROUP // P):
+            f = u * P // D
+            cols = slice(u * P, (u + 1) * P)
+            acc = mm_ps.tile([P, N], F32, name="acc", tag="acc")
+            nc.tensor.matmul_mx(
+                out=acc[:],
+                lhsT=h_codes[:, cols].bitcast(FP8X4),
+                lhsT_scale=h_scales[:, cols],
+                rhs=wb_sb[:, f, :].bitcast(FP4X4),
+                rhs_scale=wbs_sb[:, f, :],
+                start=True,
+                stop=True,
+            )
+            turn_gated(acc, E + u, z, u)
+
+        scatter_y(2, 0, y0)
+        scatter_y(3, 0, y0)
+        for j in range(NT):
+            scatter_y(j, 1, y1)
+            nc.vector.tensor_copy(z_sb[j][:].indirect(offs2_sb[:]), z[:, j, :])
+            for c in range(2):
+                cols = slice(c * T // 2, (c + 1) * T // 2)
+                nc.vector.tensor_tensor(o_sb[j][:, cols], o_sb[j][:, cols], z_sb[j][:, cols], ADD)
+                nc.sync.dma_start(out[j * P : (j + 1) * P, cols], o_sb[j][:, cols])

@@ -24,6 +24,7 @@ QUADS = 4
 ROWS = 4
 GROUP = 512
 NT = N // P
+BANKS = 3
 
 
 def tile_moe_mlr_silu_kernel(
@@ -32,16 +33,13 @@ def tile_moe_mlr_silu_kernel(
     nc = tc.nc
     with ExitStack() as ctx:
         keep = ctx.enter_context(tc.tile_pool(name="keep", bufs=1))
-        ring = ctx.enter_context(tc.tile_pool(name="ring", bufs=3))
-        mm_ps = ctx.enter_context(tc.psum_pool(name="mm_ps", bufs=3))
-        tr_ps = ctx.enter_context(tc.psum_pool(name="tr_ps", bufs=3))
-        h_ps = ctx.enter_context(tc.psum_pool(name="h_ps", bufs=2))
+        psum = ctx.enter_context(tc.psum_pool(name="psum", bufs=1))
 
         offs_sb = keep.tile([P, T // 16], U16, name="offs_sb")
         offs2_sb = keep.tile([P, F * D // 16], U16, name="offs2_sb")
         x_sb = [keep.tile([P, T], I32, name="x_sb%d" % s, align_bytes=64) for s in range(PASSES)]
         xs_both = keep.tile([P, T], U8, name="xs_both", align_bytes=64)
-        xs_last = keep.tile([P, T], U8, name="xs_last", align_bytes=64)
+        a_bytes1 = keep.tile([P, GROUP], U8, name="a_bytes1", align_bytes=64)
         w_sb = [keep.tile([P, PASSES, 4 * N], U8, name="w_sb%d" % e, align_bytes=64) for e in range(E)]
         ws_sb = keep.tile([P, E * PASSES, N], U8, name="ws_sb", align_bytes=64)
         wa_sb = keep.tile([P, F * PASSES, 2 * H], U8, name="wa_sb", align_bytes=64)
@@ -54,23 +52,33 @@ def tile_moe_mlr_silu_kernel(
         ident16 = keep.tile([P, P], BF16, name="ident16")
         o_sb = [keep.tile([P, T], F32, name="o_sb%d" % j) for j in range(NT)]
         z_sb = [keep.tile([P, T], F32, name="z_sb%d" % j) for j in range(NT)]
+        y = keep.tile([P, NT, E * C], F32, name="y")
+        z = keep.tile([P, NT, F * D], F32, name="z")
+        gated = [keep.tile([P, N], F32, name="gated%d" % b) for b in range(BANKS)]
+        h_rows = [keep.tile([P, 4, P], BF16, name="h_rows%d" % b) for b in range(2)]
+        h_in = keep.tile([P, GROUP, 4], BF16, name="h_in", align_bytes=64)
+        h_codes = keep.tile([P, GROUP], U32, name="h_codes", align_bytes=64)
+        h_scales = keep.tile([P, GROUP], U8, name="h_scales", align_bytes=64)
+        sums = [psum.tile([P, N], F32, name="sums%d" % b) for b in range(BANKS)]
+        turned = [psum.tile([P, NT, P], F32, name="turned%d" % b) for b in range(BANKS)]
+        h_turned = [psum.tile([P, 4, P], BF16, name="h_turned%d" % b) for b in range(2)]
 
         def zero(tile_ap):
             nc.vector.memset(tile_ap.bitcast(I32), 0)
 
         zero(xs_both[:])
-        zero(ws_sb[:].rearrange("p a n -> p (a n)"))
-        zero(xs_last[:])
+        zero(ws_sb[:, 0:4, :].rearrange("p a n -> p (a n)"))
         zero(was_sb[:].rearrange("p a n -> p (a n)"))
-        zero(wbs_sb[:].rearrange("p a n -> p (a n)"))
+        zero(a_bytes1[:])
         nc.gpsimd.memset(gate_rows[:], 0.0)
+        nc.gpsimd.dma_start(gate_rows[0:E, :], gate[0].rearrange("(e p) -> e p", p=P))
+        nc.gpsimd.dma_start(gate_rows[E : E + 4, :], gate2[0].rearrange("(e p) -> e p", p=P))
         make_identity(nc, ident32[:])
+        nc.gpsimd.memset(ws_sb[:, 4:, :].rearrange("p a n -> p (a n)").bitcast(I32), 0)
         make_identity(nc, ident16[:])
+        nc.gpsimd.memset(wbs_sb[:].rearrange("p a n -> p (a n)").bitcast(I32), 0)
         for j in range(NT):
             nc.gpsimd.memset(z_sb[j][:], 0.0)
-
-        def load_x(s):
-            nc.sync.dma_start(x_sb[s][:], x_words[s].rearrange("p t d -> p (t d)").bitcast(I32))
 
         def load_planes(dst, src):
             for q in range(QUADS):
@@ -82,36 +90,6 @@ def tile_moe_mlr_silu_kernel(
         def load_w(e):
             nc.sync.dma_start(w_sb[e][:].bitcast(I32), w_words[e].rearrange("s p n d -> p s (n d)").bitcast(I32))
 
-        nc.sync.dma_start(offs_sb[:], offs)
-        load_x(0)
-        load_x(1)
-        for q in range(QUADS):
-            nc.sync.dma_start(
-                xs_both[32 * q : 32 * q + PASSES * ROWS, :].bitcast(I32),
-                x_scales[:, ROWS * q : ROWS * (q + 1), :].bitcast(I32),
-            )
-        nc.sync.dma_start(offs2_sb[:], offs2)
-        load_planes(ws_sb, w_scales.rearrange("e s b n -> (e s) b n"))
-        for e in range(E // 2):
-            load_w(e)
-        nc.sync.dma_start(gate_rows[0:E, :], gate[0].rearrange("(e p) -> e p", p=P))
-        nc.sync.dma_start(gate_rows[E : E + 4, :], gate2[0].rearrange("(e p) -> e p", p=P))
-        for q in range(QUADS):
-            nc.sync.dma_start(
-                xs_last[32 * q : 32 * q + ROWS, :].bitcast(I32),
-                x_scales[1, ROWS * q : ROWS * (q + 1), :].bitcast(I32),
-            )
-        for e in range(E // 2, E):
-            load_w(e)
-        load_planes(was_sb, wa_scales.rearrange("f s b n -> (f s) b n"))
-        nc.sync.dma_start(wa_sb[:].bitcast(I32), wa_words.rearrange("f s p n -> p (f s) n").bitcast(I32))
-        load_planes(wbs_sb, wb_scales.rearrange("f s b n -> (f s) b n"))
-        nc.sync.dma_start(wb_sb[:].bitcast(I32), wb_words.rearrange("f s p n -> p (f s) n").bitcast(I32))
-
-        g_ps = tr_ps.tile([P, NT, P], F32, name="turned", tag="turned")
-        nc.tensor.transpose(g_ps[:, 0, :], gate_rows[:], ident32[:])
-        nc.scalar.copy(gate_cols[:], g_ps[:, 0, 0:16])
-
         def gather_words(name, offsets):
             tiles = []
             for s in range(PASSES):
@@ -120,58 +98,77 @@ def tile_moe_mlr_silu_kernel(
                 tiles.append(g)
             return tiles
 
-        def gather_bytes(name, window, offsets):
+        def gather_bytes(name, offsets):
             g = keep.tile([P, GROUP], U8, name=name, align_bytes=64)
-            nc.vector.tensor_copy(g[:], window[:].indirect(offsets))
+            nc.vector.tensor_copy(g[:], xs_both[:].indirect(offsets))
             return g
 
-        def turn_gated(acc, gate_col, dst, u):
-            gated = ring.tile([P, N], F32, name="gated")
-            nc.scalar.activation(gated[:], acc[:], COPY, scale=gate_cols[:, gate_col : gate_col + 1])
-            turned = tr_ps.tile([P, NT, P], F32, name="turned", tag="turned")
-            for j in range(NT):
-                nc.tensor.transpose(turned[:, j, :], gated[:, j * P : (j + 1) * P], ident32[:])
-            nc.scalar.copy(dst[:, :, u * P : (u + 1) * P], turned[:])
-
-        def experts(half, words, scales):
-            y = keep.tile([P, NT, GROUP], F32, name="y%d" % half)
-            for u in range(GROUP // C):
-                e = half * (GROUP // C) + u
-                cols = slice(u * C, (u + 1) * C)
-                acc = mm_ps.tile([P, N], F32, name="acc", tag="acc")
-                for s in range(PASSES):
-                    nc.tensor.matmul_mx(
-                        out=acc[:],
-                        lhsT=words[s][:, cols].bitcast(FP8X4),
-                        lhsT_scale=scales[ROWS * s : P, cols],
-                        rhs=w_sb[e][:, s, :].bitcast(FP8X4),
-                        rhs_scale=ws_sb[:, e * PASSES + s, :],
-                        start=(s == 0),
-                        stop=(s == PASSES - 1),
-                    )
-                turn_gated(acc, e, y, u)
-            return y
+        nc.sync.dma_start(offs_sb[:], offs)
+        for q in range(QUADS):
+            nc.sync.dma_start(
+                xs_both[32 * q : 32 * q + PASSES * ROWS, :].bitcast(I32),
+                x_scales[:, ROWS * q : ROWS * (q + 1), :].bitcast(I32),
+            )
+        nc.sync.dma_start(offs2_sb[:], offs2)
+        for s in range(PASSES):
+            nc.sync.dma_start(x_sb[s][:], x_words[s].rearrange("p t d -> p (t d)").bitcast(I32))
+        ws_rows = w_scales.rearrange("e s b n -> (e s) b n")
+        load_planes(ws_sb[:, 0:4, :], ws_rows[0:4])
+        load_w(0)
+        load_w(1)
+        nc.sync.dma_start(wa_sb[:].bitcast(I32), wa_words.rearrange("f s p n -> p (f s) n").bitcast(I32))
+        load_planes(was_sb[:], wa_scales.rearrange("f s b n -> (f s) b n"))
 
         half_offs = [offs_sb[:, 0:32], offs_sb[:, 32:64]]
-        e_words = []
-        e_scales = []
-        for half in range(2):
-            e_words.append(gather_words("e%d" % half, half_offs[half]))
-            e_scales.append(gather_bytes("e%d_bytes" % half, xs_both, half_offs[half]))
+        e_scales = [gather_bytes("e0_bytes", half_offs[0])]
+        a_bytes0 = gather_bytes("a_bytes0", offs2_sb[:])
+        for q in range(QUADS):
+            nc.sync.dma_start(
+                a_bytes1[32 * q : 32 * q + ROWS, :].bitcast(I32),
+                a_bytes0[32 * q + ROWS : 32 * q + 2 * ROWS, :].bitcast(I32),
+            )
+        a_scales = [a_bytes0, a_bytes1]
+        e_words = [gather_words("e0", half_offs[0])]
         a_words = gather_words("a", offs2_sb[:])
-        a_scales = [gather_bytes("a_bytes0", xs_both, offs2_sb[:]), gather_bytes("a_bytes1", xs_last, offs2_sb[:])]
+        e_scales.append(gather_bytes("e1_bytes", half_offs[1]))
+        e_words.append(gather_words("e1", half_offs[1]))
 
-        y0 = experts(0, e_words[0], e_scales[0])
-        y1 = experts(1, e_words[1], e_scales[1])
+        load_planes(ws_sb[:, 4:, :], ws_rows[4:])
+        for e in range(2, E):
+            load_w(e)
+        load_planes(wbs_sb[:], wb_scales.rearrange("f s b n -> (f s) b n"))
+        nc.sync.dma_start(wb_sb[:].bitcast(I32), wb_words.rearrange("f s p n -> p (f s) n").bitcast(I32))
 
-        h_in = keep.tile([P, GROUP, 4], BF16, name="h_in", align_bytes=64)
-        for u in range(GROUP // P):
-            f = u * P // D
-            cols = slice(u * P, (u + 1) * P)
-            acc = mm_ps.tile([P, N], F32, name="acc", tag="acc")
+        nc.tensor.transpose(turned[BANKS - 1][:, 0, :], gate_rows[:], ident32[:])
+        nc.scalar.copy(gate_cols[:], turned[BANKS - 1][:, 0, 0:16])
+
+        def turn_gated(b, gate_col, dst, u):
+            nc.scalar.activation(gated[b][:], sums[b][:], COPY, scale=gate_cols[:, gate_col : gate_col + 1])
+            for j in range(NT):
+                nc.tensor.transpose(turned[b][:, j, :], gated[b][:, j * P : (j + 1) * P], ident32[:])
+            nc.scalar.copy(dst[:, :, u * P : (u + 1) * P], turned[b][:])
+
+        def expert(e, b):
+            half, u = divmod(e, GROUP // C)
+            cols = slice(u * C, (u + 1) * C)
             for s in range(PASSES):
                 nc.tensor.matmul_mx(
-                    out=acc[:],
+                    out=sums[b][:],
+                    lhsT=e_words[half][s][:, cols].bitcast(FP8X4),
+                    lhsT_scale=e_scales[half][ROWS * s : P, cols],
+                    rhs=w_sb[e][:, s, :].bitcast(FP8X4),
+                    rhs_scale=ws_sb[:, e * PASSES + s, :],
+                    start=(s == 0),
+                    stop=(s == PASSES - 1),
+                )
+            turn_gated(b, e, y, e)
+
+        def adapter_in(u, b):
+            f = u * P // D
+            cols = slice(u * P, (u + 1) * P)
+            for s in range(PASSES):
+                nc.tensor.matmul_mx(
+                    out=sums[b][:],
                     lhsT=a_words[s][:, cols].bitcast(FP8X4),
                     lhsT_scale=a_scales[s][:, cols],
                     rhs=wa_sb[:, f * PASSES + s, :].bitcast(FP4X4),
@@ -179,31 +176,16 @@ def tile_moe_mlr_silu_kernel(
                     start=(s == 0),
                     stop=(s == PASSES - 1),
                 )
-            h_rows = ring.tile([P, 4, P], BF16, name="h_rows")
-            nc.scalar.activation(h_rows[:], acc[:].rearrange("m (p t) -> m t p", t=4), SILU)
-            h_turned = h_ps.tile([P, 4, P], BF16, name="h_turned")
+            nc.scalar.activation(h_rows[u % 2][:], sums[b][:].rearrange("m (p t) -> m t p", t=4), SILU)
             for t in range(4):
-                nc.tensor.transpose(h_turned[:, t, :], h_rows[:, t, :], ident16[:])
-            nc.scalar.copy(h_in[:, cols, :], h_turned[:].rearrange("p t m -> p m t"))
+                nc.tensor.transpose(h_turned[u % 2][:, t, :], h_rows[u % 2][:, t, :], ident16[:])
+            nc.scalar.copy(h_in[:, cols, :], h_turned[u % 2][:].rearrange("p t m -> p m t"))
 
-        def scatter_y(j, half, y):
-            nc.vector.tensor_copy(o_sb[j][:].indirect(half_offs[half]), y[:, j, :])
-
-        scatter_y(0, 0, y0)
-        scatter_y(1, 0, y0)
-
-        h_codes = keep.tile([P, GROUP], U32, name="h_codes", align_bytes=64)
-        h_scales = keep.tile([P, GROUP], U8, name="h_scales", align_bytes=64)
-        nc.vector.quantize_mx(
-            out=h_codes[:].bitcast(FP8X4), scales=h_scales[:], in_=h_in[:].rearrange("p m t -> p (m t)")
-        )
-        z = keep.tile([P, NT, GROUP], F32, name="z")
-        for u in range(GROUP // P):
+        def adapter_out(u, b):
             f = u * P // D
             cols = slice(u * P, (u + 1) * P)
-            acc = mm_ps.tile([P, N], F32, name="acc", tag="acc")
             nc.tensor.matmul_mx(
-                out=acc[:],
+                out=sums[b][:],
                 lhsT=h_codes[:, cols].bitcast(FP8X4),
                 lhsT_scale=h_scales[:, cols],
                 rhs=wb_sb[:, f, :].bitcast(FP4X4),
@@ -211,14 +193,31 @@ def tile_moe_mlr_silu_kernel(
                 start=True,
                 stop=True,
             )
-            turn_gated(acc, E + u, z, u)
+            turn_gated(b, E + u, z, u)
 
-        scatter_y(2, 0, y0)
-        scatter_y(3, 0, y0)
+        def scatter_y(j, first, last):
+            nc.vector.tensor_copy(
+                o_sb[j][:].indirect(offs_sb[:, first * C // 16 : last * C // 16]), y[:, j, first * C : last * C]
+            )
+
+        work = [(expert, 0), (expert, 1)] + [(adapter_in, u) for u in range(4)] + [(expert, e) for e in range(2, E)]
+        for n, (step, arg) in enumerate(work):
+            step(arg, n % BANKS)
         for j in range(NT):
-            scatter_y(j, 1, y1)
+            scatter_y(j, 0, 2)
+        nc.vector.quantize_mx(
+            out=h_codes[:].bitcast(FP8X4), scales=h_scales[:], in_=h_in[:].rearrange("p m t -> p (m t)")
+        )
+        for u in range(4):
+            adapter_out(u, (len(work) + u) % BANKS)
+        for j in range(NT):
+            scatter_y(j, 2, 4)
+        for j in range(NT):
+            scatter_y(j, 4, E)
+        for j in range(NT):
             nc.vector.tensor_copy(z_sb[j][:].indirect(offs2_sb[:]), z[:, j, :])
+            adder = nc.vector if j == NT - 1 else nc.gpsimd
             for c in range(2):
                 cols = slice(c * T // 2, (c + 1) * T // 2)
-                nc.vector.tensor_tensor(o_sb[j][:, cols], o_sb[j][:, cols], z_sb[j][:, cols], ADD)
+                adder.tensor_tensor(o_sb[j][:, cols], o_sb[j][:, cols], z_sb[j][:, cols], ADD)
                 nc.sync.dma_start(out[j * P : (j + 1) * P, cols], o_sb[j][:, cols])

@@ -66,7 +66,7 @@ def tile_moe_mlr_silu_kernel(
         def zero(tile_ap):
             nc.vector.memset(tile_ap.bitcast(I32), 0)
 
-        zero(xs_both[:])
+        nc.gpsimd.memset(xs_both[:].bitcast(I32), 0)
         zero(ws_sb[:, 0:4, :].rearrange("p a n -> p (a n)"))
         zero(was_sb[:].rearrange("p a n -> p (a n)"))
         zero(a_bytes1[:])
@@ -109,18 +109,20 @@ def tile_moe_mlr_silu_kernel(
                 xs_both[32 * q : 32 * q + PASSES * ROWS, :].bitcast(I32),
                 x_scales[:, ROWS * q : ROWS * (q + 1), :].bitcast(I32),
             )
-        nc.sync.dma_start(offs2_sb[:], offs2)
         for s in range(PASSES):
             nc.sync.dma_start(x_sb[s][:], x_words[s].rearrange("p t d -> p (t d)").bitcast(I32))
+        nc.sync.dma_start(offs2_sb[:], offs2)
         ws_rows = w_scales.rearrange("e s b n -> (e s) b n")
         load_planes(ws_sb[:, 0:4, :], ws_rows[0:4])
         load_w(0)
         load_w(1)
-        nc.sync.dma_start(wa_sb[:].bitcast(I32), wa_words.rearrange("f s p n -> p (f s) n").bitcast(I32))
-        load_planes(was_sb[:], wa_scales.rearrange("f s b n -> (f s) b n"))
+        load_planes(ws_sb[:, 4:, :], ws_rows[4:])
+        for e in range(2, 5):
+            load_w(e)
 
         half_offs = [offs_sb[:, 0:32], offs_sb[:, 32:64]]
-        e_scales = [gather_bytes("e0_bytes", half_offs[0])]
+        e_scales = [gather_bytes("e%d_bytes" % half, half_offs[half]) for half in range(2)]
+        e_words = [gather_words("e%d" % half, half_offs[half]) for half in range(2)]
         a_bytes0 = gather_bytes("a_bytes0", offs2_sb[:])
         for q in range(QUADS):
             nc.sync.dma_start(
@@ -128,13 +130,11 @@ def tile_moe_mlr_silu_kernel(
                 a_bytes0[32 * q + ROWS : 32 * q + 2 * ROWS, :].bitcast(I32),
             )
         a_scales = [a_bytes0, a_bytes1]
-        e_words = [gather_words("e0", half_offs[0])]
         a_words = gather_words("a", offs2_sb[:])
-        e_scales.append(gather_bytes("e1_bytes", half_offs[1]))
-        e_words.append(gather_words("e1", half_offs[1]))
 
-        load_planes(ws_sb[:, 4:, :], ws_rows[4:])
-        for e in range(2, E):
+        load_planes(was_sb[:], wa_scales.rearrange("f s b n -> (f s) b n"))
+        nc.sync.dma_start(wa_sb[:].bitcast(I32), wa_words.rearrange("f s p n -> p (f s) n").bitcast(I32))
+        for e in range(5, E):
             load_w(e)
         load_planes(wbs_sb[:], wb_scales.rearrange("f s b n -> (f s) b n"))
         nc.sync.dma_start(wb_sb[:].bitcast(I32), wb_words.rearrange("f s p n -> p (f s) n").bitcast(I32))
@@ -200,24 +200,24 @@ def tile_moe_mlr_silu_kernel(
                 o_sb[j][:].indirect(offs_sb[:, first * C // 16 : last * C // 16]), y[:, j, first * C : last * C]
             )
 
-        work = [(expert, 0), (expert, 1)] + [(adapter_in, u) for u in range(4)] + [(expert, e) for e in range(2, E)]
+        work = [(expert, e) for e in range(5)] + [(adapter_in, u) for u in range(4)] + [(expert, e) for e in range(5, E)]
         for n, (step, arg) in enumerate(work):
             step(arg, n % BANKS)
         for j in range(NT):
             scatter_y(j, 0, 2)
+        for j in range(NT):
+            scatter_y(j, 2, 5)
         nc.vector.quantize_mx(
             out=h_codes[:].bitcast(FP8X4), scales=h_scales[:], in_=h_in[:].rearrange("p m t -> p (m t)")
         )
         for u in range(4):
             adapter_out(u, (len(work) + u) % BANKS)
         for j in range(NT):
-            scatter_y(j, 2, 4)
-        for j in range(NT):
-            scatter_y(j, 4, E)
+            scatter_y(j, 5, E)
         for j in range(NT):
             nc.vector.tensor_copy(z_sb[j][:].indirect(offs2_sb[:]), z[:, j, :])
             adder = nc.vector if j == NT - 1 else nc.gpsimd
-            for c in range(2):
-                cols = slice(c * T // 2, (c + 1) * T // 2)
-                adder.tensor_tensor(o_sb[j][:, cols], o_sb[j][:, cols], z_sb[j][:, cols], ADD)
-                nc.sync.dma_start(out[j * P : (j + 1) * P, cols], o_sb[j][:, cols])
+            edges = [0, 512, 768, T] if j == NT - 1 else [0, 512, T]
+            for lo, hi in zip(edges[:-1], edges[1:]):
+                adder.tensor_tensor(o_sb[j][:, lo:hi], o_sb[j][:, lo:hi], z_sb[j][:, lo:hi], ADD)
+                nc.sync.dma_start(out[j * P : (j + 1) * P, lo:hi], o_sb[j][:, lo:hi])

@@ -48,6 +48,7 @@ def tile_moe_mlr_silu_kernel(
         wbs_sb = keep.tile([P, F, N], U8, name="wbs_sb", align_bytes=64)
         gate_rows = keep.tile([P, P], F32, name="gate_rows")
         gate_cols = keep.tile([P, 16], F32, name="gate_cols")
+        zero_col = keep.tile([P, 1], F32, name="zero_col")
         ident32 = keep.tile([P, P], F32, name="ident32")
         ident16 = keep.tile([P, P], BF16, name="ident16")
         o_sb = [keep.tile([P, T], F32, name="o_sb%d" % j) for j in range(NT)]
@@ -67,18 +68,19 @@ def tile_moe_mlr_silu_kernel(
             nc.vector.memset(tile_ap.bitcast(I32), 0)
 
         nc.gpsimd.memset(xs_both[:].bitcast(I32), 0)
+        nc.vector.memset(zero_col[:], 0.0)
         zero(ws_sb[:, 0:4, :].rearrange("p a n -> p (a n)"))
+        zero(ws_sb[:, 4:, :].rearrange("p a n -> p (a n)"))
         zero(was_sb[:].rearrange("p a n -> p (a n)"))
         zero(a_bytes1[:])
+        zero(wbs_sb[:].rearrange("p a n -> p (a n)"))
         nc.gpsimd.memset(gate_rows[:], 0.0)
-        nc.gpsimd.dma_start(gate_rows[0:E, :], gate[0].rearrange("(e p) -> e p", p=P))
-        nc.gpsimd.dma_start(gate_rows[E : E + 4, :], gate2[0].rearrange("(e p) -> e p", p=P))
+        nc.scalar.dma_start(gate_rows[0:E, :], gate[0].rearrange("(e p) -> e p", p=P))
+        nc.scalar.dma_start(gate_rows[E : E + 4, :], gate2[0].rearrange("(e p) -> e p", p=P))
         make_identity(nc, ident32[:])
-        nc.gpsimd.memset(ws_sb[:, 4:, :].rearrange("p a n -> p (a n)").bitcast(I32), 0)
         make_identity(nc, ident16[:])
-        nc.gpsimd.memset(wbs_sb[:].rearrange("p a n -> p (a n)").bitcast(I32), 0)
         for j in range(NT):
-            nc.gpsimd.memset(z_sb[j][:], 0.0)
+            nc.scalar.copy(z_sb[j][:], zero_col[:].to_broadcast([P, T]))
 
         def load_planes(dst, src):
             for q in range(QUADS):
@@ -90,27 +92,27 @@ def tile_moe_mlr_silu_kernel(
         def load_w(e):
             nc.sync.dma_start(w_sb[e][:].bitcast(I32), w_words[e].rearrange("s p n d -> p s (n d)").bitcast(I32))
 
-        def gather_words(name, offsets):
-            tiles = []
-            for s in range(PASSES):
-                g = keep.tile([P, GROUP], U32, name="%s_words%d" % (name, s), align_bytes=64)
-                nc.vector.tensor_copy(g[:], x_sb[s][:].bitcast(U32).indirect(offsets))
-                tiles.append(g)
-            return tiles
+        def gather_words(name, s, offsets):
+            g = keep.tile([P, GROUP], U32, name="%s_words%d" % (name, s), align_bytes=64)
+            nc.vector.tensor_copy(g[:], x_sb[s][:].bitcast(U32).indirect(offsets))
+            return g
 
         def gather_bytes(name, offsets):
             g = keep.tile([P, GROUP], U8, name=name, align_bytes=64)
             nc.vector.tensor_copy(g[:], xs_both[:].indirect(offsets))
             return g
 
+        def load_x(s):
+            nc.sync.dma_start(x_sb[s][:], x_words[s].rearrange("p t d -> p (t d)").bitcast(I32))
+
         nc.sync.dma_start(offs_sb[:], offs)
+        load_x(0)
         for q in range(QUADS):
             nc.sync.dma_start(
                 xs_both[32 * q : 32 * q + PASSES * ROWS, :].bitcast(I32),
                 x_scales[:, ROWS * q : ROWS * (q + 1), :].bitcast(I32),
             )
-        for s in range(PASSES):
-            nc.sync.dma_start(x_sb[s][:], x_words[s].rearrange("p t d -> p (t d)").bitcast(I32))
+        load_x(1)
         nc.sync.dma_start(offs2_sb[:], offs2)
         ws_rows = w_scales.rearrange("e s b n -> (e s) b n")
         load_planes(ws_sb[:, 0:4, :], ws_rows[0:4])
@@ -121,8 +123,12 @@ def tile_moe_mlr_silu_kernel(
             load_w(e)
 
         half_offs = [offs_sb[:, 0:32], offs_sb[:, 32:64]]
-        e_scales = [gather_bytes("e%d_bytes" % half, half_offs[half]) for half in range(2)]
-        e_words = [gather_words("e%d" % half, half_offs[half]) for half in range(2)]
+        e_scales = []
+        e_words = []
+        for half in range(2):
+            first = gather_words("e%d" % half, 0, half_offs[half])
+            e_scales.append(gather_bytes("e%d_bytes" % half, half_offs[half]))
+            e_words.append([first, gather_words("e%d" % half, 1, half_offs[half])])
         a_bytes0 = gather_bytes("a_bytes0", offs2_sb[:])
         for q in range(QUADS):
             nc.sync.dma_start(
@@ -130,7 +136,7 @@ def tile_moe_mlr_silu_kernel(
                 a_bytes0[32 * q + ROWS : 32 * q + 2 * ROWS, :].bitcast(I32),
             )
         a_scales = [a_bytes0, a_bytes1]
-        a_words = gather_words("a", offs2_sb[:])
+        a_words = [gather_words("a", s, offs2_sb[:]) for s in range(PASSES)]
 
         load_planes(was_sb[:], wa_scales.rearrange("f s b n -> (f s) b n"))
         nc.sync.dma_start(wa_sb[:].bitcast(I32), wa_words.rearrange("f s p n -> p (f s) n").bitcast(I32))
@@ -203,10 +209,9 @@ def tile_moe_mlr_silu_kernel(
         work = [(expert, e) for e in range(5)] + [(adapter_in, u) for u in range(4)] + [(expert, e) for e in range(5, E)]
         for n, (step, arg) in enumerate(work):
             step(arg, n % BANKS)
-        for j in range(NT):
-            scatter_y(j, 0, 2)
-        for j in range(NT):
-            scatter_y(j, 2, 5)
+        for first, last in ((0, 1), (1, 3), (3, 5)):
+            for j in range(NT):
+                scatter_y(j, first, last)
         nc.vector.quantize_mx(
             out=h_codes[:].bitcast(FP8X4), scales=h_scales[:], in_=h_in[:].rearrange("p m t -> p (m t)")
         )

@@ -17,6 +17,7 @@ FP4X4 = mybir.dt.float4_e2m1fn_x4
 COPY = mybir.ActivationFunctionType.Copy
 SILU = mybir.ActivationFunctionType.Silu
 ADD = mybir.AluOpType.add
+MULT = mybir.AluOpType.mult
 
 P = 128
 PASSES = K // 512
@@ -37,17 +38,18 @@ def tile_moe_mlr_silu_kernel(
 
         offs_sb = keep.tile([P, T // 16], U16, name="offs_sb")
         offs2_sb = keep.tile([P, F * D // 16], U16, name="offs2_sb")
-        x_sb = [keep.tile([P, T], I32, name="x_sb%d" % s, align_bytes=64) for s in range(PASSES)]
+        x_sb = keep.tile([P, PASSES, T], I32, name="x_sb", align_bytes=64)
         xs_both = keep.tile([P, T], U8, name="xs_both", align_bytes=64)
         a_bytes1 = keep.tile([P, GROUP], U8, name="a_bytes1", align_bytes=64)
         w_sb = [keep.tile([P, PASSES, 4 * N], U8, name="w_sb%d" % e, align_bytes=64) for e in range(E)]
-        ws_sb = keep.tile([P, E * PASSES, N], U8, name="ws_sb", align_bytes=64)
+        ws_sb = keep.tile([P, E, N], U8, name="ws_sb", align_bytes=64)
         wa_sb = keep.tile([P, F * PASSES, 2 * H], U8, name="wa_sb", align_bytes=64)
         was_sb = keep.tile([P, F * PASSES, H], U8, name="was_sb", align_bytes=64)
         wb_sb = keep.tile([P, F, 2 * N], U8, name="wb_sb", align_bytes=64)
         wbs_sb = keep.tile([P, F, N], U8, name="wbs_sb", align_bytes=64)
         gate_rows = keep.tile([P, P], F32, name="gate_rows")
         gate_cols = keep.tile([P, 16], F32, name="gate_cols")
+        gate_sb = keep.tile([P, E * C], F32, name="gate_sb")
         zero_col = keep.tile([P, 1], F32, name="zero_col")
         ident32 = keep.tile([P, P], F32, name="ident32")
         ident16 = keep.tile([P, P], BF16, name="ident16")
@@ -64,23 +66,20 @@ def tile_moe_mlr_silu_kernel(
         turned = [psum.tile([P, NT, P], F32, name="turned%d" % b) for b in range(BANKS)]
         h_turned = [psum.tile([P, 4, P], BF16, name="h_turned%d" % b) for b in range(2)]
 
-        def zero(tile_ap):
-            nc.vector.memset(tile_ap.bitcast(I32), 0)
+        def zero(engine, tile_ap):
+            engine.memset(tile_ap.bitcast(I32), 0)
 
-        nc.gpsimd.memset(xs_both[:].bitcast(I32), 0)
+        zero(nc.gpsimd, xs_both[:])
         nc.vector.memset(zero_col[:], 0.0)
-        zero(ws_sb[:, 0:4, :].rearrange("p a n -> p (a n)"))
-        zero(ws_sb[:, 4:, :].rearrange("p a n -> p (a n)"))
-        zero(was_sb[:].rearrange("p a n -> p (a n)"))
-        zero(a_bytes1[:])
-        zero(wbs_sb[:].rearrange("p a n -> p (a n)"))
+        zero(nc.vector, ws_sb[:].rearrange("p a n -> p (a n)"))
         nc.gpsimd.memset(gate_rows[:], 0.0)
-        nc.scalar.dma_start(gate_rows[0:E, :], gate[0].rearrange("(e p) -> e p", p=P))
-        nc.scalar.dma_start(gate_rows[E : E + 4, :], gate2[0].rearrange("(e p) -> e p", p=P))
         make_identity(nc, ident32[:])
+        zero(nc.gpsimd, a_bytes1[:])
+        zero(nc.gpsimd, was_sb[:].rearrange("p a n -> p (a n)"))
         make_identity(nc, ident16[:])
+        zero(nc.gpsimd, wbs_sb[:].rearrange("p a n -> p (a n)"))
         for j in range(NT):
-            nc.scalar.copy(z_sb[j][:], zero_col[:].to_broadcast([P, T]))
+            nc.scalar.activation(z_sb[j][:], zero_col[:].to_broadcast([P, T]), SILU)
 
         def load_planes(dst, src):
             for q in range(QUADS):
@@ -94,7 +93,7 @@ def tile_moe_mlr_silu_kernel(
 
         def gather_words(name, s, offsets):
             g = keep.tile([P, GROUP], U32, name="%s_words%d" % (name, s), align_bytes=64)
-            nc.vector.tensor_copy(g[:], x_sb[s][:].bitcast(U32).indirect(offsets))
+            nc.vector.tensor_copy(g[:], x_sb[:, s, :].bitcast(U32).indirect(offsets))
             return g
 
         def gather_bytes(name, offsets):
@@ -102,51 +101,50 @@ def tile_moe_mlr_silu_kernel(
             nc.vector.tensor_copy(g[:], xs_both[:].indirect(offsets))
             return g
 
-        def load_x(s):
-            nc.sync.dma_start(x_sb[s][:], x_words[s].rearrange("p t d -> p (t d)").bitcast(I32))
-
         nc.sync.dma_start(offs_sb[:], offs)
-        load_x(0)
+        nc.sync.dma_start(offs2_sb[:], offs2)
         for q in range(QUADS):
             nc.sync.dma_start(
                 xs_both[32 * q : 32 * q + PASSES * ROWS, :].bitcast(I32),
                 x_scales[:, ROWS * q : ROWS * (q + 1), :].bitcast(I32),
             )
-        load_x(1)
-        nc.sync.dma_start(offs2_sb[:], offs2)
-        ws_rows = w_scales.rearrange("e s b n -> (e s) b n")
-        load_planes(ws_sb[:, 0:4, :], ws_rows[0:4])
+        nc.sync.dma_start(x_sb[:], x_words.rearrange("s p t d -> p s (t d)").bitcast(I32))
+        for s in range(PASSES):
+            for q in range(QUADS):
+                nc.sync.dma_start(
+                    ws_sb[32 * q + ROWS * s : 32 * q + ROWS * (s + 1), :, :].bitcast(I32),
+                    w_scales[:, s, ROWS * q : ROWS * (q + 1), :].rearrange("a r n -> r a n").bitcast(I32),
+                )
         load_w(0)
         load_w(1)
-        load_planes(ws_sb[:, 4:, :], ws_rows[4:])
-        for e in range(2, 5):
-            load_w(e)
+        nc.sync.dma_start(gate_sb[:], gate)
+        load_w(2)
+        load_w(3)
+        nc.sync.dma_start(gate_rows[0:4, :], gate2[0].rearrange("(e p) -> e p", p=P))
+        load_planes(was_sb[:], wa_scales.rearrange("f s b n -> (f s) b n"))
+        nc.sync.dma_start(wa_sb[:].bitcast(I32), wa_words.rearrange("f s p n -> p (f s) n").bitcast(I32))
 
-        half_offs = [offs_sb[:, 0:32], offs_sb[:, 32:64]]
-        e_scales = []
-        e_words = []
-        for half in range(2):
-            first = gather_words("e%d" % half, 0, half_offs[half])
-            e_scales.append(gather_bytes("e%d_bytes" % half, half_offs[half]))
-            e_words.append([first, gather_words("e%d" % half, 1, half_offs[half])])
-        a_bytes0 = gather_bytes("a_bytes0", offs2_sb[:])
+        lists = [offs_sb[:, 0:32], offs2_sb[:], offs_sb[:, 32:64]]
+        scales = [gather_bytes("g%d_bytes" % i, lists[i]) for i in range(3)]
+        pass0 = []
+        pass1 = []
+        for i in range(3):
+            pass0.append(gather_words("g%d" % i, 0, lists[i]))
+            pass1.append(gather_words("g%d" % i, 1, lists[i]))
+        e_scales = [scales[0], scales[2]]
+        e_words = [[pass0[i], pass1[i]] for i in (0, 2)]
+        a_words = [pass0[1], pass1[1]]
+        a_bytes0 = scales[1]
         for q in range(QUADS):
             nc.sync.dma_start(
                 a_bytes1[32 * q : 32 * q + ROWS, :].bitcast(I32),
                 a_bytes0[32 * q + ROWS : 32 * q + 2 * ROWS, :].bitcast(I32),
             )
         a_scales = [a_bytes0, a_bytes1]
-        a_words = [gather_words("a", s, offs2_sb[:]) for s in range(PASSES)]
-
-        load_planes(was_sb[:], wa_scales.rearrange("f s b n -> (f s) b n"))
-        nc.sync.dma_start(wa_sb[:].bitcast(I32), wa_words.rearrange("f s p n -> p (f s) n").bitcast(I32))
-        for e in range(5, E):
+        for e in range(4, E):
             load_w(e)
         load_planes(wbs_sb[:], wb_scales.rearrange("f s b n -> (f s) b n"))
         nc.sync.dma_start(wb_sb[:].bitcast(I32), wb_words.rearrange("f s p n -> p (f s) n").bitcast(I32))
-
-        nc.tensor.transpose(turned[BANKS - 1][:, 0, :], gate_rows[:], ident32[:])
-        nc.scalar.copy(gate_cols[:], turned[BANKS - 1][:, 0, 0:16])
 
         def turn_gated(b, gate_col, dst, u):
             nc.scalar.activation(gated[b][:], sums[b][:], COPY, scale=gate_cols[:, gate_col : gate_col + 1])
@@ -157,17 +155,18 @@ def tile_moe_mlr_silu_kernel(
         def expert(e, b):
             half, u = divmod(e, GROUP // C)
             cols = slice(u * C, (u + 1) * C)
-            for s in range(PASSES):
-                nc.tensor.matmul_mx(
-                    out=sums[b][:],
-                    lhsT=e_words[half][s][:, cols].bitcast(FP8X4),
-                    lhsT_scale=e_scales[half][ROWS * s : P, cols],
-                    rhs=w_sb[e][:, s, :].bitcast(FP8X4),
-                    rhs_scale=ws_sb[:, e * PASSES + s, :],
-                    start=(s == 0),
-                    stop=(s == PASSES - 1),
-                )
-            turn_gated(b, e, y, e)
+            for j in range(NT):
+                for s in range(PASSES):
+                    nc.tensor.matmul_mx(
+                        out=sums[b][:, j * P : (j + 1) * P],
+                        lhsT=w_sb[e][:, s, 4 * j * P : 4 * (j + 1) * P].bitcast(FP8X4),
+                        lhsT_scale=ws_sb[ROWS * s : P, e, j * P : (j + 1) * P],
+                        rhs=e_words[half][s][:, cols].bitcast(FP8X4),
+                        rhs_scale=e_scales[half][ROWS * s : P, cols],
+                        start=(s == 0),
+                        stop=(s == PASSES - 1),
+                    )
+            nc.scalar.copy(y[:, :, e * C : (e + 1) * C], sums[b][:].rearrange("p (j m) -> p j m", j=NT))
 
         def adapter_in(u, b):
             f = u * P // D
@@ -199,30 +198,36 @@ def tile_moe_mlr_silu_kernel(
                 start=True,
                 stop=True,
             )
-            turn_gated(b, E + u, z, u)
+            turn_gated(b, u, z, u)
 
         def scatter_y(j, first, last):
-            nc.vector.tensor_copy(
-                o_sb[j][:].indirect(offs_sb[:, first * C // 16 : last * C // 16]), y[:, j, first * C : last * C]
+            cols = slice(first * C, last * C)
+            nc.vector.tensor_tensor(
+                o_sb[j][:].indirect(offs_sb[:, first * C // 16 : last * C // 16]), y[:, j, cols], gate_sb[:, cols], MULT
             )
 
-        work = [(expert, e) for e in range(5)] + [(adapter_in, u) for u in range(4)] + [(expert, e) for e in range(5, E)]
+        nc.tensor.transpose(turned[BANKS - 1][:, 0, :], gate_rows[:], ident32[:])
+        nc.scalar.copy(gate_cols[:], turned[BANKS - 1][:, 0, 0:16])
+        work = [(expert, e) for e in range(4)] + [(adapter_in, u) for u in range(4)] + [(expert, e) for e in range(4, E)]
         for n, (step, arg) in enumerate(work):
             step(arg, n % BANKS)
-        for first, last in ((0, 1), (1, 3), (3, 5)):
-            for j in range(NT):
-                scatter_y(j, first, last)
+        scatter_y(0, 0, 2)
+        for j in range(1, NT):
+            scatter_y(j, 0, 4)
         nc.vector.quantize_mx(
             out=h_codes[:].bitcast(FP8X4), scales=h_scales[:], in_=h_in[:].rearrange("p m t -> p (m t)")
         )
         for u in range(4):
             adapter_out(u, (len(work) + u) % BANKS)
-        for j in range(NT):
-            scatter_y(j, 5, E)
+        scatter_y(0, 2, 6)
+        scatter_y(1, 4, E)
+        scatter_y(0, 6, E)
+        for j in range(2, NT):
+            scatter_y(j, 4, E)
         for j in range(NT):
             nc.vector.tensor_copy(z_sb[j][:].indirect(offs2_sb[:]), z[:, j, :])
             adder = nc.vector if j == NT - 1 else nc.gpsimd
-            edges = [0, 512, 768, T] if j == NT - 1 else [0, 512, T]
+            edges = [0, 384, 704, 896, T] if j == NT - 1 else [0, 512, T]
             for lo, hi in zip(edges[:-1], edges[1:]):
                 adder.tensor_tensor(o_sb[j][:, lo:hi], o_sb[j][:, lo:hi], z_sb[j][:, lo:hi], ADD)
                 nc.sync.dma_start(out[j * P : (j + 1) * P, lo:hi], o_sb[j][:, lo:hi])

@@ -39,10 +39,14 @@ def tile_moe_mlr_silu_kernel(
         offs_sb = keep.tile([P, T // 16], U16, name="offs_sb")
         offs2_sb = keep.tile([P, F * D // 16], U16, name="offs2_sb")
         x_sb = keep.tile([P, PASSES, T], I32, name="x_sb", align_bytes=64)
+        xs_rows = keep.tile([P, T], U8, name="xs_rows", align_bytes=64)
         xs_both = keep.tile([P, T], U8, name="xs_both", align_bytes=64)
-        a_bytes1 = keep.tile([P, GROUP], U8, name="a_bytes1", align_bytes=64)
+        first_planes = keep.tile([P, GROUP], U8, name="first_planes", align_bytes=64)
+        slot_rows = keep.tile([P, 2 * GROUP], U8, name="slot_rows", align_bytes=64)
+        planes = [keep.tile([P, 2 * GROUP], U8, name="planes%d" % s, align_bytes=64) for s in range(PASSES)]
         w_sb = [keep.tile([P, PASSES, 4 * N], U8, name="w_sb%d" % e, align_bytes=64) for e in range(E)]
-        ws_sb = keep.tile([P, E, N], U8, name="ws_sb", align_bytes=64)
+        ws_first = keep.tile([P, N], U8, name="ws_first", align_bytes=64)
+        ws_sb = keep.tile([P, E - 2, N], U8, name="ws_sb", align_bytes=64)
         wa_sb = keep.tile([P, F * PASSES, 2 * H], U8, name="wa_sb", align_bytes=64)
         was_sb = keep.tile([P, F * PASSES, H], U8, name="was_sb", align_bytes=64)
         wb_sb = keep.tile([P, F, 2 * N], U8, name="wb_sb", align_bytes=64)
@@ -70,16 +74,22 @@ def tile_moe_mlr_silu_kernel(
             engine.memset(tile_ap.bitcast(I32), 0)
 
         zero(nc.gpsimd, xs_both[:])
+        zero(nc.gpsimd, ws_first[:])
+        zero(nc.vector, xs_rows[32:64, :])
+        zero(nc.vector, xs_rows[64:P, :])
         nc.vector.memset(zero_col[:], 0.0)
         zero(nc.vector, ws_sb[:].rearrange("p a n -> p (a n)"))
+        for s in range(PASSES):
+            zero(nc.gpsimd, planes[s][:])
         nc.gpsimd.memset(gate_rows[:], 0.0)
         make_identity(nc, ident32[:])
-        zero(nc.gpsimd, a_bytes1[:])
         zero(nc.gpsimd, was_sb[:].rearrange("p a n -> p (a n)"))
         make_identity(nc, ident16[:])
         zero(nc.gpsimd, wbs_sb[:].rearrange("p a n -> p (a n)"))
-        for j in range(NT):
+        for j in range(2):
             nc.scalar.activation(z_sb[j][:], zero_col[:].to_broadcast([P, T]), SILU)
+        for j in range(2, NT):
+            nc.gpsimd.memset(z_sb[j][:], 0.0)
 
         def load_planes(dst, src):
             for q in range(QUADS):
@@ -96,51 +106,53 @@ def tile_moe_mlr_silu_kernel(
             nc.vector.tensor_copy(g[:], x_sb[:, s, :].bitcast(U32).indirect(offsets))
             return g
 
-        def gather_bytes(name, offsets):
-            g = keep.tile([P, GROUP], U8, name=name, align_bytes=64)
-            nc.vector.tensor_copy(g[:], xs_both[:].indirect(offsets))
-            return g
-
-        nc.sync.dma_start(offs_sb[:], offs)
         nc.sync.dma_start(offs2_sb[:], offs2)
+        nc.sync.dma_start(xs_rows[0:32, :].bitcast(I32), x_scales.rearrange("s b t -> (s b) t").bitcast(I32))
+        nc.sync.dma_start(offs_sb[:], offs)
         for q in range(QUADS):
             nc.sync.dma_start(
-                xs_both[32 * q : 32 * q + PASSES * ROWS, :].bitcast(I32),
+                xs_both[32 * q + 2 * ROWS : 32 * q + 4 * ROWS, :].bitcast(I32),
                 x_scales[:, ROWS * q : ROWS * (q + 1), :].bitcast(I32),
             )
         nc.sync.dma_start(x_sb[:], x_words.rearrange("s p t d -> p s (t d)").bitcast(I32))
+        load_w(0)
+        ws_rows = w_scales.rearrange("e s b n -> (e s) b n")
+        for q in range(QUADS):
+            nc.sync.dma_start(
+                ws_first[32 * q : 32 * q + 4 * ROWS, :].bitcast(I32),
+                ws_rows[0:4, ROWS * q : ROWS * (q + 1), :].bitcast(I32),
+            )
+        lists = [offs_sb[:, 0:32], offs2_sb[:], offs_sb[:, 32:64]]
+        for i in range(2):
+            nc.vector.tensor_copy(slot_rows[:, i * GROUP : (i + 1) * GROUP], xs_rows[:].indirect(lists[1 + i]))
+        nc.vector.tensor_copy(first_planes[:], xs_both[:].indirect(lists[0]))
+        nc.sync.dma_start(gate_sb[:, 0:GROUP], gate[:, 0:GROUP])
+        load_w(1)
         for s in range(PASSES):
             for q in range(QUADS):
                 nc.sync.dma_start(
                     ws_sb[32 * q + ROWS * s : 32 * q + ROWS * (s + 1), :, :].bitcast(I32),
-                    w_scales[:, s, ROWS * q : ROWS * (q + 1), :].rearrange("a r n -> r a n").bitcast(I32),
+                    w_scales[2:, s, ROWS * q : ROWS * (q + 1), :].rearrange("a r n -> r a n").bitcast(I32),
                 )
-        load_w(0)
-        load_w(1)
-        nc.sync.dma_start(gate_sb[:], gate)
         load_w(2)
         load_w(3)
+        for q in range(QUADS):
+            for s in range(PASSES):
+                row = 16 * s + ROWS * q
+                nc.sync.dma_start(
+                    planes[s][32 * q : 32 * q + ROWS, :].bitcast(I32), slot_rows[row : row + ROWS, :].bitcast(I32)
+                )
         nc.sync.dma_start(gate_rows[0:4, :], gate2[0].rearrange("(e p) -> e p", p=P))
         load_planes(was_sb[:], wa_scales.rearrange("f s b n -> (f s) b n"))
         nc.sync.dma_start(wa_sb[:].bitcast(I32), wa_words.rearrange("f s p n -> p (f s) n").bitcast(I32))
-
-        lists = [offs_sb[:, 0:32], offs2_sb[:], offs_sb[:, 32:64]]
-        scales = [gather_bytes("g%d_bytes" % i, lists[i]) for i in range(3)]
         pass0 = []
         pass1 = []
         for i in range(3):
             pass0.append(gather_words("g%d" % i, 0, lists[i]))
             pass1.append(gather_words("g%d" % i, 1, lists[i]))
-        e_scales = [scales[0], scales[2]]
         e_words = [[pass0[i], pass1[i]] for i in (0, 2)]
         a_words = [pass0[1], pass1[1]]
-        a_bytes0 = scales[1]
-        for q in range(QUADS):
-            nc.sync.dma_start(
-                a_bytes1[32 * q : 32 * q + ROWS, :].bitcast(I32),
-                a_bytes0[32 * q + ROWS : 32 * q + 2 * ROWS, :].bitcast(I32),
-            )
-        a_scales = [a_bytes0, a_bytes1]
+        nc.sync.dma_start(gate_sb[:, GROUP:], gate[:, GROUP:])
         for e in range(4, E):
             load_w(e)
         load_planes(wbs_sb[:], wb_scales.rearrange("f s b n -> (f s) b n"))
@@ -152,6 +164,9 @@ def tile_moe_mlr_silu_kernel(
                 nc.tensor.transpose(turned[b][:, j, :], gated[b][:, j * P : (j + 1) * P], ident32[:])
             nc.scalar.copy(dst[:, :, u * P : (u + 1) * P], turned[b][:])
 
+        def w_plane(e, s):
+            return ws_first[ROWS * (PASSES * e + s) : P, :] if e < 2 else ws_sb[ROWS * s : P, e - 2, :]
+
         def expert(e, b):
             half, u = divmod(e, GROUP // C)
             cols = slice(u * C, (u + 1) * C)
@@ -160,9 +175,9 @@ def tile_moe_mlr_silu_kernel(
                     nc.tensor.matmul_mx(
                         out=sums[b][:, j * P : (j + 1) * P],
                         lhsT=w_sb[e][:, s, 4 * j * P : 4 * (j + 1) * P].bitcast(FP8X4),
-                        lhsT_scale=ws_sb[ROWS * s : P, e, j * P : (j + 1) * P],
+                        lhsT_scale=w_plane(e, s)[:, j * P : (j + 1) * P],
                         rhs=e_words[half][s][:, cols].bitcast(FP8X4),
-                        rhs_scale=e_scales[half][ROWS * s : P, cols],
+                        rhs_scale=(planes[s][:, GROUP:] if half else first_planes[ROWS * (2 + s) : P, :])[:, cols],
                         start=(s == 0),
                         stop=(s == PASSES - 1),
                     )
@@ -175,7 +190,7 @@ def tile_moe_mlr_silu_kernel(
                 nc.tensor.matmul_mx(
                     out=sums[b][:],
                     lhsT=a_words[s][:, cols].bitcast(FP8X4),
-                    lhsT_scale=a_scales[s][:, cols],
+                    lhsT_scale=planes[s][:, cols],
                     rhs=wa_sb[:, f * PASSES + s, :].bitcast(FP4X4),
                     rhs_scale=was_sb[:, f * PASSES + s, :],
                     start=(s == 0),
@@ -211,18 +226,20 @@ def tile_moe_mlr_silu_kernel(
         work = [(expert, e) for e in range(4)] + [(adapter_in, u) for u in range(4)] + [(expert, e) for e in range(4, E)]
         for n, (step, arg) in enumerate(work):
             step(arg, n % BANKS)
-        scatter_y(0, 0, 2)
-        for j in range(1, NT):
-            scatter_y(j, 0, 4)
+        scatter_y(0, 0, 1)
+        scatter_y(1, 0, 1)
+        scatter_y(2, 0, 2)
+        scatter_y(3, 0, 2)
+        scatter_y(0, 1, 4)
+        scatter_y(1, 1, 4)
+        scatter_y(2, 2, 4)
+        scatter_y(3, 2, 4)
         nc.vector.quantize_mx(
             out=h_codes[:].bitcast(FP8X4), scales=h_scales[:], in_=h_in[:].rearrange("p m t -> p (m t)")
         )
         for u in range(4):
             adapter_out(u, (len(work) + u) % BANKS)
-        scatter_y(0, 2, 6)
-        scatter_y(1, 4, E)
-        scatter_y(0, 6, E)
-        for j in range(2, NT):
+        for j in range(NT):
             scatter_y(j, 4, E)
         for j in range(NT):
             nc.vector.tensor_copy(z_sb[j][:].indirect(offs2_sb[:]), z[:, j, :])

@@ -70,26 +70,24 @@ def tile_moe_mlr_silu_kernel(
         turned = [psum.tile([P, NT, P], F32, name="turned%d" % b) for b in range(BANKS)]
         h_turned = [psum.tile([P, 4, P], BF16, name="h_turned%d" % b) for b in range(2)]
 
-        def zero(engine, tile_ap):
-            engine.memset(tile_ap.bitcast(I32), 0)
+        def zero(tile_ap):
+            nc.gpsimd.memset(tile_ap.bitcast(I32), 0)
 
-        zero(nc.gpsimd, xs_both[:])
-        zero(nc.gpsimd, ws_first[:])
-        zero(nc.vector, xs_rows[32:64, :])
-        zero(nc.vector, xs_rows[64:P, :])
-        nc.vector.memset(zero_col[:], 0.0)
-        zero(nc.vector, ws_sb[:].rearrange("p a n -> p (a n)"))
+        zero(xs_both[:])
+        zero(xs_rows[32:64, :])
+        zero(xs_rows[64:P, :])
+        zero(ws_first[:])
+        nc.gpsimd.memset(zero_col[:], 0.0)
+        zero(ws_sb[:].rearrange("p a n -> p (a n)"))
         for s in range(PASSES):
-            zero(nc.gpsimd, planes[s][:])
+            zero(planes[s][:])
         nc.gpsimd.memset(gate_rows[:], 0.0)
+        zero(was_sb[:].rearrange("p a n -> p (a n)"))
         make_identity(nc, ident32[:])
-        zero(nc.gpsimd, was_sb[:].rearrange("p a n -> p (a n)"))
         make_identity(nc, ident16[:])
-        zero(nc.gpsimd, wbs_sb[:].rearrange("p a n -> p (a n)"))
-        for j in range(2):
+        zero(wbs_sb[:].rearrange("p a n -> p (a n)"))
+        for j in range(NT):
             nc.scalar.activation(z_sb[j][:], zero_col[:].to_broadcast([P, T]), SILU)
-        for j in range(2, NT):
-            nc.gpsimd.memset(z_sb[j][:], 0.0)
 
         def load_planes(dst, src):
             for q in range(QUADS):

@@ -23,9 +23,10 @@ P = 128
 PASSES = K // 512
 QUADS = 4
 ROWS = 4
-GROUP = 512
+M = F * D
 NT = N // P
 BANKS = 3
+WIDE = 1376
 
 
 def tile_moe_mlr_silu_kernel(
@@ -37,54 +38,57 @@ def tile_moe_mlr_silu_kernel(
         psum = ctx.enter_context(tc.psum_pool(name="psum", bufs=1))
 
         offs_sb = keep.tile([P, T // 16], U16, name="offs_sb")
-        offs2_sb = keep.tile([P, F * D // 16], U16, name="offs2_sb")
-        x_sb = keep.tile([P, PASSES, T], I32, name="x_sb", align_bytes=64)
+        offs2_sb = keep.tile([P, M // 16], U16, name="offs2_sb")
+        x_sb = keep.tile([P, T + WIDE], I32, name="x_sb", align_bytes=64)
         xs_rows = keep.tile([P, T], U8, name="xs_rows", align_bytes=64)
-        xs_both = keep.tile([P, T], U8, name="xs_both", align_bytes=64)
-        first_planes = keep.tile([P, GROUP], U8, name="first_planes", align_bytes=64)
-        slot_rows = keep.tile([P, 2 * GROUP], U8, name="slot_rows", align_bytes=64)
-        planes = [keep.tile([P, 2 * GROUP], U8, name="planes%d" % s, align_bytes=64) for s in range(PASSES)]
-        w_sb = [keep.tile([P, PASSES, 4 * N], U8, name="w_sb%d" % e, align_bytes=64) for e in range(E)]
-        ws_first = keep.tile([P, N], U8, name="ws_first", align_bytes=64)
-        ws_sb = keep.tile([P, E - 2, N], U8, name="ws_sb", align_bytes=64)
+        xs_planes = keep.tile([P, WIDE], U8, name="xs_planes", align_bytes=64)
+        a_rows = keep.tile([P, M], U8, name="a_rows", align_bytes=64)
+        e_planes = keep.tile([P, T], U8, name="e_planes", align_bytes=64)
+        a_planes = keep.tile([P, PASSES, M], U8, name="a_planes", align_bytes=64)
+        e_words = [keep.tile([P, T], U32, name="e_words%d" % s, align_bytes=64) for s in range(PASSES)]
+        a_words = [keep.tile([P, M], U32, name="a_words%d" % s, align_bytes=64) for s in range(PASSES)]
+        w_cuts = [(0, 1), (1, 2), (2, NT)]
+        w_sb = [
+            keep.tile([P, E * PASSES, 4 * P * (hi - lo)], U8, name="w_sb%d" % lo, align_bytes=64) for lo, hi in w_cuts
+        ]
+        ws_first = keep.tile([P, E * PASSES, P], U8, name="ws_first", align_bytes=64)
+        ws_rest = keep.tile([P, E * PASSES, N - P], U8, name="ws_rest", align_bytes=64)
         wa_sb = keep.tile([P, F * PASSES, 2 * H], U8, name="wa_sb", align_bytes=64)
         was_sb = keep.tile([P, F * PASSES, H], U8, name="was_sb", align_bytes=64)
         wb_sb = keep.tile([P, F, 2 * N], U8, name="wb_sb", align_bytes=64)
         wbs_sb = keep.tile([P, F, N], U8, name="wbs_sb", align_bytes=64)
         gate_rows = keep.tile([P, P], F32, name="gate_rows")
         gate_cols = keep.tile([P, 16], F32, name="gate_cols")
-        gate_sb = keep.tile([P, E * C], F32, name="gate_sb")
+        gate_sb = keep.tile([P, T], F32, name="gate_sb")
         zero_col = keep.tile([P, 1], F32, name="zero_col")
-        ident32 = keep.tile([P, P], F32, name="ident32")
-        ident16 = keep.tile([P, P], BF16, name="ident16")
-        o_sb = [keep.tile([P, T], F32, name="o_sb%d" % j) for j in range(NT)]
+        ident = keep.tile([P, P], F32, name="ident")
+        o_sb = [keep.tile([P, WIDE], F32, name="o_sb%d" % j) for j in range(NT)]
         z_sb = [keep.tile([P, T], F32, name="z_sb%d" % j) for j in range(NT)]
-        y = keep.tile([P, NT, E * C], F32, name="y")
-        z = keep.tile([P, NT, F * D], F32, name="z")
-        gated = [keep.tile([P, N], F32, name="gated%d" % b) for b in range(BANKS)]
-        h_rows = [keep.tile([P, 4, P], BF16, name="h_rows%d" % b) for b in range(2)]
-        h_in = keep.tile([P, GROUP, 4], BF16, name="h_in", align_bytes=64)
-        h_codes = keep.tile([P, GROUP], U32, name="h_codes", align_bytes=64)
-        h_scales = keep.tile([P, GROUP], U8, name="h_scales", align_bytes=64)
+        y = [keep.tile([P, T], F32, name="y%d" % j) for j in range(NT)]
+        z = [keep.tile([P, M], F32, name="z%d" % j) for j in range(NT)]
+        gated = [keep.tile([P, N], F32, name="gated%d" % u) for u in range(M // P)]
+        h_rows = [keep.tile([P, H], BF16, name="h_rows%d" % b) for b in range(2)]
+        h_in = keep.tile([P, 4 * M], BF16, name="h_in", align_bytes=64)
+        h_codes = keep.tile([P, M], U32, name="h_codes", align_bytes=64)
+        h_scales = keep.tile([P, M], U8, name="h_scales", align_bytes=64)
         sums = [psum.tile([P, N], F32, name="sums%d" % b) for b in range(BANKS)]
-        turned = [psum.tile([P, NT, P], F32, name="turned%d" % b) for b in range(BANKS)]
-        h_turned = [psum.tile([P, 4, P], BF16, name="h_turned%d" % b) for b in range(2)]
+        turned = [psum.tile([P, N], F32, name="turned%d" % b) for b in range(BANKS)]
+        h_turned = [psum.tile([P, N], F32, name="h_turned%d" % b) for b in range(2)]
 
         def zero(tile_ap):
             nc.gpsimd.memset(tile_ap.bitcast(I32), 0)
 
-        zero(xs_both[:])
+        zero(xs_planes[:])
         zero(xs_rows[32:64, :])
         zero(xs_rows[64:P, :])
-        zero(ws_first[:])
+        zero(ws_first[:].rearrange("p a n -> p (a n)"))
         nc.gpsimd.memset(zero_col[:], 0.0)
-        zero(ws_sb[:].rearrange("p a n -> p (a n)"))
-        for s in range(PASSES):
-            zero(planes[s][:])
-        nc.gpsimd.memset(gate_rows[:], 0.0)
+        nc.gpsimd.memset(x_sb[:, PASSES * T :], 0)
+        zero(ws_rest[:].rearrange("p a n -> p (a n)"))
+        zero(a_planes[:].rearrange("p a n -> p (a n)"))
         zero(was_sb[:].rearrange("p a n -> p (a n)"))
-        make_identity(nc, ident32[:])
-        make_identity(nc, ident16[:])
+        nc.gpsimd.memset(gate_rows[:], 0.0)
+        make_identity(nc, ident[:])
         zero(wbs_sb[:].rearrange("p a n -> p (a n)"))
         for j in range(NT):
             nc.scalar.activation(z_sb[j][:], zero_col[:].to_broadcast([P, T]), SILU)
@@ -96,90 +100,73 @@ def tile_moe_mlr_silu_kernel(
                     src[:, ROWS * q : ROWS * (q + 1), :].rearrange("a r n -> r a n").bitcast(I32),
                 )
 
-        def load_w(e):
-            nc.sync.dma_start(w_sb[e][:].bitcast(I32), w_words[e].rearrange("s p n d -> p s (n d)").bitcast(I32))
+        def move_planes(dst, src):
+            for s in range(PASSES):
+                for q in range(QUADS):
+                    row = 16 * s + ROWS * q
+                    nc.sync.dma_start(
+                        dst[32 * q : 32 * q + ROWS, s, :].bitcast(I32), src[row : row + ROWS, :].bitcast(I32)
+                    )
 
-        def gather_words(name, s, offsets):
-            g = keep.tile([P, GROUP], U32, name="%s_words%d" % (name, s), align_bytes=64)
-            nc.vector.tensor_copy(g[:], x_sb[:, s, :].bitcast(U32).indirect(offsets))
-            return g
+        w_rows = w_words.rearrange("e s p n d -> p (e s) (n d)")
+
+        def load_w(i):
+            lo, hi = w_cuts[i]
+            nc.sync.dma_start(w_sb[i][:].bitcast(I32), w_rows[:, :, 4 * P * lo : 4 * P * hi].bitcast(I32))
 
         nc.sync.dma_start(offs2_sb[:], offs2)
         nc.sync.dma_start(xs_rows[0:32, :].bitcast(I32), x_scales.rearrange("s b t -> (s b) t").bitcast(I32))
         nc.sync.dma_start(offs_sb[:], offs)
         for q in range(QUADS):
             nc.sync.dma_start(
-                xs_both[32 * q + 2 * ROWS : 32 * q + 4 * ROWS, :].bitcast(I32),
+                xs_planes[32 * q : 32 * q + PASSES * ROWS, 0:T].bitcast(I32),
                 x_scales[:, ROWS * q : ROWS * (q + 1), :].bitcast(I32),
             )
-        nc.sync.dma_start(x_sb[:], x_words.rearrange("s p t d -> p s (t d)").bitcast(I32))
-        load_w(0)
+        nc.sync.dma_start(
+            x_sb[:, 0 : PASSES * T].rearrange("p (s t) -> p s t", s=PASSES),
+            x_words.rearrange("s p t d -> p s (t d)").bitcast(I32),
+        )
         ws_rows = w_scales.rearrange("e s b n -> (e s) b n")
-        for q in range(QUADS):
-            nc.sync.dma_start(
-                ws_first[32 * q : 32 * q + 4 * ROWS, :].bitcast(I32),
-                ws_rows[0:4, ROWS * q : ROWS * (q + 1), :].bitcast(I32),
-            )
-        lists = [offs_sb[:, 0:32], offs2_sb[:], offs_sb[:, 32:64]]
-        for i in range(2):
-            nc.vector.tensor_copy(slot_rows[:, i * GROUP : (i + 1) * GROUP], xs_rows[:].indirect(lists[1 + i]))
-        nc.vector.tensor_copy(first_planes[:], xs_both[:].indirect(lists[0]))
-        nc.sync.dma_start(gate_sb[:, 0:GROUP], gate[:, 0:GROUP])
-        load_w(1)
+        load_planes(ws_first[:], ws_rows[:, :, 0:P])
+        load_w(0)
+        nc.sync.dma_start(gate_sb[:], gate)
+        nc.vector.tensor_copy(a_rows[:], xs_rows[:].indirect(offs2_sb[:]))
+        nc.vector.tensor_copy(e_planes[:], xs_planes[:].indirect(offs_sb[:]))
         for s in range(PASSES):
-            for q in range(QUADS):
-                nc.sync.dma_start(
-                    ws_sb[32 * q + ROWS * s : 32 * q + ROWS * (s + 1), :, :].bitcast(I32),
-                    w_scales[2:, s, ROWS * q : ROWS * (q + 1), :].rearrange("a r n -> r a n").bitcast(I32),
-                )
-        load_w(2)
-        load_w(3)
-        for q in range(QUADS):
-            for s in range(PASSES):
-                row = 16 * s + ROWS * q
-                nc.sync.dma_start(
-                    planes[s][32 * q : 32 * q + ROWS, :].bitcast(I32), slot_rows[row : row + ROWS, :].bitcast(I32)
-                )
-        nc.sync.dma_start(gate_rows[0:4, :], gate2[0].rearrange("(e p) -> e p", p=P))
+            nc.vector.tensor_copy(e_words[s][:], x_sb[:, s * T : s * T + WIDE].bitcast(U32).indirect(offs_sb[:]))
+        for s in range(PASSES):
+            nc.vector.tensor_copy(a_words[s][:], x_sb[:, s * T : (s + 1) * T].bitcast(U32).indirect(offs2_sb[:]))
+        load_planes(ws_rest[:], ws_rows[:, :, P:])
+        load_w(1)
+        move_planes(a_planes, a_rows)
         load_planes(was_sb[:], wa_scales.rearrange("f s b n -> (f s) b n"))
         nc.sync.dma_start(wa_sb[:].bitcast(I32), wa_words.rearrange("f s p n -> p (f s) n").bitcast(I32))
-        pass0 = []
-        pass1 = []
-        for i in range(3):
-            pass0.append(gather_words("g%d" % i, 0, lists[i]))
-            pass1.append(gather_words("g%d" % i, 1, lists[i]))
-        e_words = [[pass0[i], pass1[i]] for i in (0, 2)]
-        a_words = [pass0[1], pass1[1]]
-        nc.sync.dma_start(gate_sb[:, GROUP:], gate[:, GROUP:])
-        for e in range(4, E):
-            load_w(e)
+        nc.sync.dma_start(gate_rows[0:4, :], gate2[0].rearrange("(e p) -> e p", p=P))
+        load_w(2)
         load_planes(wbs_sb[:], wb_scales.rearrange("f s b n -> (f s) b n"))
         nc.sync.dma_start(wb_sb[:].bitcast(I32), wb_words.rearrange("f s p n -> p (f s) n").bitcast(I32))
 
-        def turn_gated(b, gate_col, dst, u):
-            nc.scalar.activation(gated[b][:], sums[b][:], COPY, scale=gate_cols[:, gate_col : gate_col + 1])
-            for j in range(NT):
-                nc.tensor.transpose(turned[b][:, j, :], gated[b][:, j * P : (j + 1) * P], ident32[:])
-            nc.scalar.copy(dst[:, :, u * P : (u + 1) * P], turned[b][:])
-
-        def w_plane(e, s):
-            return ws_first[ROWS * (PASSES * e + s) : P, :] if e < 2 else ws_sb[ROWS * s : P, e - 2, :]
-
-        def expert(e, b):
-            half, u = divmod(e, GROUP // C)
-            cols = slice(u * C, (u + 1) * C)
-            for j in range(NT):
-                for s in range(PASSES):
+        def experts(j, banks):
+            i = min(j, len(w_cuts) - 1)
+            first = j - w_cuts[i][0]
+            for s in range(PASSES):
+                for e in range(E):
+                    half, u = divmod(e, E // 2)
+                    cols = slice(e * C, (e + 1) * C)
+                    a = PASSES * e + s
+                    plane = ws_first[:, a, :] if j == 0 else ws_rest[:, a, (j - 1) * P : j * P]
                     nc.tensor.matmul_mx(
-                        out=sums[b][:, j * P : (j + 1) * P],
-                        lhsT=w_sb[e][:, s, 4 * j * P : 4 * (j + 1) * P].bitcast(FP8X4),
-                        lhsT_scale=w_plane(e, s)[:, j * P : (j + 1) * P],
-                        rhs=e_words[half][s][:, cols].bitcast(FP8X4),
-                        rhs_scale=(planes[s][:, GROUP:] if half else first_planes[ROWS * (2 + s) : P, :])[:, cols],
-                        start=(s == 0),
-                        stop=(s == PASSES - 1),
+                        out=banks[half][:, u * C : (u + 1) * C],
+                        lhsT=w_sb[i][:, a, 4 * P * first : 4 * P * (first + 1)].bitcast(FP8X4),
+                        lhsT_scale=plane,
+                        rhs=e_words[s][:, cols].bitcast(FP8X4),
+                        rhs_scale=e_planes[ROWS * s : P, cols],
+                        start=(s == 0 and u == 0),
+                        stop=(s == PASSES - 1 and u == E // 2 - 1),
                     )
-            nc.scalar.copy(y[:, :, e * C : (e + 1) * C], sums[b][:].rearrange("p (j m) -> p j m", j=NT))
+            for half in range(2):
+                nc.scalar.copy(y[j][:, half * N : (half + 1) * N], banks[half][:])
+            nc.vector.tensor_tensor(o_sb[j][:].indirect(offs_sb[:]), y[j][:], gate_sb[:], MULT)
 
         def adapter_in(u, b):
             f = u * P // D
@@ -188,16 +175,24 @@ def tile_moe_mlr_silu_kernel(
                 nc.tensor.matmul_mx(
                     out=sums[b][:],
                     lhsT=a_words[s][:, cols].bitcast(FP8X4),
-                    lhsT_scale=planes[s][:, cols],
+                    lhsT_scale=a_planes[:, s, cols],
                     rhs=wa_sb[:, f * PASSES + s, :].bitcast(FP4X4),
                     rhs_scale=was_sb[:, f * PASSES + s, :],
                     start=(s == 0),
                     stop=(s == PASSES - 1),
                 )
-            nc.scalar.activation(h_rows[u % 2][:], sums[b][:].rearrange("m (p t) -> m t p", t=4), SILU)
-            for t in range(4):
-                nc.tensor.transpose(h_turned[u % 2][:, t, :], h_rows[u % 2][:, t, :], ident16[:])
-            nc.scalar.copy(h_in[:, cols, :], h_turned[u % 2][:].rearrange("p t m -> p m t"))
+            nc.scalar.activation(
+                h_rows[u % 2][:].rearrange("m (v p e) -> m v p e", v=2, e=2),
+                sums[b][:].rearrange("m (p v e) -> m v p e", v=2, e=2),
+                SILU,
+            )
+            pairs = h_rows[u % 2][:].bitcast(F32)
+            for v in range(2):
+                nc.tensor.transpose(h_turned[u % 2][:, v * P : (v + 1) * P], pairs[:, v * P : (v + 1) * P], ident[:])
+            nc.scalar.copy(
+                h_in[:, 4 * u * P : 4 * (u + 1) * P].bitcast(F32).rearrange("p (m v) -> p m v", v=2),
+                h_turned[u % 2][:, 0 : 2 * P].rearrange("p (v m) -> p m v", v=2),
+            )
 
         def adapter_out(u, b):
             f = u * P // D
@@ -211,38 +206,33 @@ def tile_moe_mlr_silu_kernel(
                 start=True,
                 stop=True,
             )
-            turn_gated(b, u, z, u)
+            nc.scalar.activation(gated[u][:], sums[b][:], COPY, scale=gate_cols[:, u : u + 1])
 
-        def scatter_y(j, first, last):
-            cols = slice(first * C, last * C)
-            nc.vector.tensor_tensor(
-                o_sb[j][:].indirect(offs_sb[:, first * C // 16 : last * C // 16]), y[:, j, cols], gate_sb[:, cols], MULT
-            )
+        def turn_back(j):
+            bank = turned[j % BANKS]
+            for u in range(M // P):
+                nc.tensor.transpose(bank[:, u * P : (u + 1) * P], gated[u][:, j * P : (j + 1) * P], ident[:])
+            nc.scalar.copy(z[j][:], bank[:])
 
-        nc.tensor.transpose(turned[BANKS - 1][:, 0, :], gate_rows[:], ident32[:])
-        nc.scalar.copy(gate_cols[:], turned[BANKS - 1][:, 0, 0:16])
-        work = [(expert, e) for e in range(4)] + [(adapter_in, u) for u in range(4)] + [(expert, e) for e in range(4, E)]
-        for n, (step, arg) in enumerate(work):
-            step(arg, n % BANKS)
-        scatter_y(0, 0, 1)
-        scatter_y(1, 0, 1)
-        scatter_y(2, 0, 2)
-        scatter_y(3, 0, 2)
-        scatter_y(0, 1, 4)
-        scatter_y(1, 1, 4)
-        scatter_y(2, 2, 4)
-        scatter_y(3, 2, 4)
-        nc.vector.quantize_mx(
-            out=h_codes[:].bitcast(FP8X4), scales=h_scales[:], in_=h_in[:].rearrange("p m t -> p (m t)")
-        )
+        experts(0, [sums[0], sums[1]])
+        experts(1, [sums[2], sums[0]])
+        nc.tensor.transpose(turned[BANKS - 1][:, 0:P], gate_rows[:], ident[:])
+        nc.scalar.copy(gate_cols[:], turned[BANKS - 1][:, 0:16])
         for u in range(4):
-            adapter_out(u, (len(work) + u) % BANKS)
+            adapter_in(u, (1 + u) % BANKS)
+        nc.vector.quantize_mx(out=h_codes[:].bitcast(FP8X4), scales=h_scales[:], in_=h_in[:])
+        experts(2, h_turned)
+        for u in range(4):
+            adapter_out(u, (2 + u) % BANKS)
         for j in range(NT):
-            scatter_y(j, 4, E)
-        for j in range(NT):
-            nc.vector.tensor_copy(z_sb[j][:].indirect(offs2_sb[:]), z[:, j, :])
-            adder = nc.vector if j == NT - 1 else nc.gpsimd
-            edges = [0, 384, 704, 896, T] if j == NT - 1 else [0, 512, T]
-            for lo, hi in zip(edges[:-1], edges[1:]):
-                adder.tensor_tensor(o_sb[j][:, lo:hi], o_sb[j][:, lo:hi], z_sb[j][:, lo:hi], ADD)
-                nc.sync.dma_start(out[j * P : (j + 1) * P, lo:hi], o_sb[j][:, lo:hi])
+            turn_back(j)
+            nc.vector.tensor_copy(z_sb[j][:].indirect(offs2_sb[:]), z[j][:])
+            if j < NT - 1:
+                nc.gpsimd.tensor_tensor(o_sb[j][:, 0:T], o_sb[j][:, 0:T], z_sb[j][:], ADD)
+                nc.sync.dma_start(out[j * P : (j + 1) * P, :], o_sb[j][:, 0:T])
+        j = NT - 1
+        experts(j, [turned[2], turned[0]])
+        edges = [0, 384, 704, 896, T]
+        for lo, hi in zip(edges[:-1], edges[1:]):
+            nc.vector.tensor_tensor(o_sb[j][:, lo:hi], o_sb[j][:, lo:hi], z_sb[j][:, lo:hi], ADD)
+            nc.sync.dma_start(out[j * P : (j + 1) * P, lo:hi], o_sb[j][:, lo:hi])

@@ -40,19 +40,17 @@ def tile_moe_mlr_silu_kernel(
         offs_sb = keep.tile([P, T // 16], U16, name="offs_sb")
         offs2_sb = keep.tile([P, M // 16], U16, name="offs2_sb")
         x_sb = keep.tile([P, T + WIDE], I32, name="x_sb", align_bytes=64)
-        xs_rows = keep.tile([P, T], U8, name="xs_rows", align_bytes=64)
-        xs_planes = keep.tile([P, WIDE], U8, name="xs_planes", align_bytes=64)
-        a_rows = keep.tile([P, M], U8, name="a_rows", align_bytes=64)
-        e_planes = keep.tile([P, T], U8, name="e_planes", align_bytes=64)
-        a_planes = keep.tile([P, PASSES, M], U8, name="a_planes", align_bytes=64)
+        xs_rows = keep.tile([P, WIDE], U8, name="xs_rows", align_bytes=64)
+        slot_rows = keep.tile([P, M + T], U8, name="slot_rows", align_bytes=64)
+        planes = keep.tile([P, M + T], U8, name="planes", align_bytes=64)
+        a_plane0 = keep.tile([P, M], U8, name="a_plane0", align_bytes=64)
         e_words = [keep.tile([P, T], U32, name="e_words%d" % s, align_bytes=64) for s in range(PASSES)]
         a_words = [keep.tile([P, M], U32, name="a_words%d" % s, align_bytes=64) for s in range(PASSES)]
-        w_cuts = [(0, 1), (1, 2), (2, NT)]
-        w_sb = [
-            keep.tile([P, E * PASSES, 4 * P * (hi - lo)], U8, name="w_sb%d" % lo, align_bytes=64) for lo, hi in w_cuts
-        ]
-        ws_first = keep.tile([P, E * PASSES, P], U8, name="ws_first", align_bytes=64)
-        ws_rest = keep.tile([P, E * PASSES, N - P], U8, name="ws_rest", align_bytes=64)
+        w_01 = keep.tile([P, 2 * PASSES, 4 * N], U8, name="w_01", align_bytes=64)
+        w_2 = keep.tile([P, PASSES, 4 * N], U8, name="w_2", align_bytes=64)
+        w_3 = keep.tile([P, PASSES, 4 * N], U8, name="w_3", align_bytes=64)
+        w_late = [keep.tile([P, 4 * PASSES, 2 * N], U8, name="w_late%d" % g, align_bytes=64) for g in range(2)]
+        ws_sb = [keep.tile([P, N], U8, name="ws_sb%d" % g, align_bytes=64) for g in range(E // 2)]
         wa_sb = keep.tile([P, F * PASSES, 2 * H], U8, name="wa_sb", align_bytes=64)
         was_sb = keep.tile([P, F * PASSES, H], U8, name="was_sb", align_bytes=64)
         wb_sb = keep.tile([P, F, 2 * N], U8, name="wb_sb", align_bytes=64)
@@ -62,7 +60,7 @@ def tile_moe_mlr_silu_kernel(
         gate_sb = keep.tile([P, T], F32, name="gate_sb")
         zero_col = keep.tile([P, 1], F32, name="zero_col")
         ident = keep.tile([P, P], F32, name="ident")
-        o_sb = [keep.tile([P, WIDE], F32, name="o_sb%d" % j) for j in range(NT)]
+        o_sb = [keep.tile([P, T], F32, name="o_sb%d" % j) for j in range(NT)]
         z_sb = [keep.tile([P, T], F32, name="z_sb%d" % j) for j in range(NT)]
         y = [keep.tile([P, T], F32, name="y%d" % j) for j in range(NT)]
         z = [keep.tile([P, M], F32, name="z%d" % j) for j in range(NT)]
@@ -78,16 +76,17 @@ def tile_moe_mlr_silu_kernel(
         def zero(tile_ap):
             nc.gpsimd.memset(tile_ap.bitcast(I32), 0)
 
-        zero(xs_planes[:])
-        zero(xs_rows[32:64, :])
-        zero(xs_rows[64:P, :])
-        zero(ws_first[:].rearrange("p a n -> p (a n)"))
+        zero(ws_sb[0][:])
+        zero(xs_rows[32:64, 0:T])
+        zero(xs_rows[64:P, 0:T])
         nc.gpsimd.memset(zero_col[:], 0.0)
-        nc.gpsimd.memset(x_sb[:, PASSES * T :], 0)
-        zero(ws_rest[:].rearrange("p a n -> p (a n)"))
-        zero(a_planes[:].rearrange("p a n -> p (a n)"))
+        zero(planes[:])
+        zero(ws_sb[1][:])
+        zero(a_plane0[:])
         zero(was_sb[:].rearrange("p a n -> p (a n)"))
         nc.gpsimd.memset(gate_rows[:], 0.0)
+        zero(ws_sb[2][:])
+        zero(ws_sb[3][:])
         make_identity(nc, ident[:])
         zero(wbs_sb[:].rearrange("p a n -> p (a n)"))
         for j in range(NT):
@@ -100,73 +99,82 @@ def tile_moe_mlr_silu_kernel(
                     src[:, ROWS * q : ROWS * (q + 1), :].rearrange("a r n -> r a n").bitcast(I32),
                 )
 
-        def move_planes(dst, src):
-            for s in range(PASSES):
-                for q in range(QUADS):
-                    row = 16 * s + ROWS * q
-                    nc.sync.dma_start(
-                        dst[32 * q : 32 * q + ROWS, s, :].bitcast(I32), src[row : row + ROWS, :].bitcast(I32)
-                    )
-
         w_rows = w_words.rearrange("e s p n d -> p (e s) (n d)")
+        ws_rows = w_scales.rearrange("e s b n -> (e s) b n")
 
-        def load_w(i):
-            lo, hi = w_cuts[i]
-            nc.sync.dma_start(w_sb[i][:].bitcast(I32), w_rows[:, :, 4 * P * lo : 4 * P * hi].bitcast(I32))
+        def load_ws(g):
+            for q in range(QUADS):
+                nc.sync.dma_start(
+                    ws_sb[g][32 * q : 32 * q + 4 * ROWS, :].bitcast(I32),
+                    ws_rows[4 * g : 4 * (g + 1), ROWS * q : ROWS * (q + 1), :].bitcast(I32),
+                )
 
         nc.sync.dma_start(offs2_sb[:], offs2)
-        nc.sync.dma_start(xs_rows[0:32, :].bitcast(I32), x_scales.rearrange("s b t -> (s b) t").bitcast(I32))
-        nc.sync.dma_start(offs_sb[:], offs)
-        for q in range(QUADS):
+        for s in range(PASSES):
             nc.sync.dma_start(
-                xs_planes[32 * q : 32 * q + PASSES * ROWS, 0:T].bitcast(I32),
-                x_scales[:, ROWS * q : ROWS * (q + 1), :].bitcast(I32),
+                xs_rows[16 * (1 - s) : 16 * (2 - s), 0:T].bitcast(I32),
+                x_scales[s].rearrange("(q r) t -> r q t", r=ROWS).bitcast(I32),
             )
+        nc.sync.dma_start(offs_sb[:], offs)
         nc.sync.dma_start(
             x_sb[:, 0 : PASSES * T].rearrange("p (s t) -> p s t", s=PASSES),
             x_words.rearrange("s p t d -> p s (t d)").bitcast(I32),
         )
-        ws_rows = w_scales.rearrange("e s b n -> (e s) b n")
-        load_planes(ws_first[:], ws_rows[:, :, 0:P])
-        load_w(0)
-        nc.sync.dma_start(gate_sb[:], gate)
-        nc.vector.tensor_copy(a_rows[:], xs_rows[:].indirect(offs2_sb[:]))
-        nc.vector.tensor_copy(e_planes[:], xs_planes[:].indirect(offs_sb[:]))
+        nc.sync.dma_start(w_01[:].bitcast(I32), w_rows[:, 0:4, :].bitcast(I32))
+        load_ws(0)
+        nc.sync.dma_start(gate_sb[:, 0:N], gate[:, 0:N])
+        nc.sync.dma_start(w_2[:].bitcast(I32), w_rows[:, 4:6, :].bitcast(I32))
+        nc.vector.tensor_copy(slot_rows[:, 0:M], xs_rows[:, 0:T].indirect(offs2_sb[:]))
+        nc.vector.tensor_copy(slot_rows[:, M:], xs_rows[:].indirect(offs_sb[:]))
         for s in range(PASSES):
             nc.vector.tensor_copy(e_words[s][:], x_sb[:, s * T : s * T + WIDE].bitcast(U32).indirect(offs_sb[:]))
         for s in range(PASSES):
             nc.vector.tensor_copy(a_words[s][:], x_sb[:, s * T : (s + 1) * T].bitcast(U32).indirect(offs2_sb[:]))
-        load_planes(ws_rest[:], ws_rows[:, :, P:])
-        load_w(1)
-        move_planes(a_planes, a_rows)
+        for q in range(QUADS):
+            nc.sync.dma_start(
+                planes[32 * q : 32 * q + 2 * ROWS, :].bitcast(I32), slot_rows[q:32:QUADS, :].bitcast(I32)
+            )
+        load_ws(1)
+        nc.sync.dma_start(w_3[:].bitcast(I32), w_rows[:, 6:8, :].bitcast(I32))
+        for q in range(QUADS):
+            nc.sync.dma_start(
+                a_plane0[32 * q : 32 * q + ROWS, :].bitcast(I32), slot_rows[16 + q : 32 : QUADS, 0:M].bitcast(I32)
+            )
         load_planes(was_sb[:], wa_scales.rearrange("f s b n -> (f s) b n"))
         nc.sync.dma_start(wa_sb[:].bitcast(I32), wa_words.rearrange("f s p n -> p (f s) n").bitcast(I32))
         nc.sync.dma_start(gate_rows[0:4, :], gate2[0].rearrange("(e p) -> e p", p=P))
-        load_w(2)
+        load_ws(2)
+        load_ws(3)
+        nc.sync.dma_start(w_late[0][:].bitcast(I32), w_rows[:, 8:, 0 : 2 * N].bitcast(I32))
+        nc.sync.dma_start(gate_sb[:, N:], gate[:, N:])
+        nc.sync.dma_start(w_late[1][:].bitcast(I32), w_rows[:, 8:, 2 * N :].bitcast(I32))
         load_planes(wbs_sb[:], wb_scales.rearrange("f s b n -> (f s) b n"))
         nc.sync.dma_start(wb_sb[:].bitcast(I32), wb_words.rearrange("f s p n -> p (f s) n").bitcast(I32))
 
-        def experts(j, banks):
-            i = min(j, len(w_cuts) - 1)
-            first = j - w_cuts[i][0]
+        def w_tile(e, s, j):
+            if e >= 4:
+                return w_late[j // 2][:, PASSES * (e - 4) + s, 4 * P * (j % 2) : 4 * P * (j % 2 + 1)]
+            rows = w_01[:, PASSES * e + s, :] if e < 2 else (w_2, w_3)[e - 2][:, s, :]
+            return rows[:, 4 * P * j : 4 * P * (j + 1)]
+
+        def experts(j, first, last, bank):
             for s in range(PASSES):
-                for e in range(E):
-                    half, u = divmod(e, E // 2)
-                    cols = slice(e * C, (e + 1) * C)
-                    a = PASSES * e + s
-                    plane = ws_first[:, a, :] if j == 0 else ws_rest[:, a, (j - 1) * P : j * P]
+                for e in range(first, last):
+                    a = PASSES * (e % 2) + s
                     nc.tensor.matmul_mx(
-                        out=banks[half][:, u * C : (u + 1) * C],
-                        lhsT=w_sb[i][:, a, 4 * P * first : 4 * P * (first + 1)].bitcast(FP8X4),
-                        lhsT_scale=plane,
-                        rhs=e_words[s][:, cols].bitcast(FP8X4),
-                        rhs_scale=e_planes[ROWS * s : P, cols],
-                        start=(s == 0 and u == 0),
-                        stop=(s == PASSES - 1 and u == E // 2 - 1),
+                        out=bank[:, (e - first) * C : (e - first + 1) * C],
+                        lhsT=w_tile(e, s, j).bitcast(FP8X4),
+                        lhsT_scale=ws_sb[e // 2][ROWS * a : P, j * P : (j + 1) * P],
+                        rhs=e_words[s][:, e * C : (e + 1) * C].bitcast(FP8X4),
+                        rhs_scale=planes[ROWS * (1 - s) : P, M + e * C : M + (e + 1) * C],
+                        start=(s == 0 and e == first),
+                        stop=(s == PASSES - 1 and e == last - 1),
                     )
-            for half in range(2):
-                nc.scalar.copy(y[j][:, half * N : (half + 1) * N], banks[half][:])
-            nc.vector.tensor_tensor(o_sb[j][:].indirect(offs_sb[:]), y[j][:], gate_sb[:], MULT)
+            cols = slice(first * C, last * C)
+            nc.scalar.copy(y[j][:, cols], bank[:, 0 : (last - first) * C])
+            nc.vector.tensor_tensor(
+                o_sb[j][:].indirect(offs_sb[:, first * C // 16 : last * C // 16]), y[j][:, cols], gate_sb[:, cols], MULT
+            )
 
         def adapter_in(u, b):
             f = u * P // D
@@ -175,7 +183,7 @@ def tile_moe_mlr_silu_kernel(
                 nc.tensor.matmul_mx(
                     out=sums[b][:],
                     lhsT=a_words[s][:, cols].bitcast(FP8X4),
-                    lhsT_scale=a_planes[:, s, cols],
+                    lhsT_scale=(planes if s else a_plane0)[:, cols],
                     rhs=wa_sb[:, f * PASSES + s, :].bitcast(FP4X4),
                     rhs_scale=was_sb[:, f * PASSES + s, :],
                     start=(s == 0),
@@ -214,14 +222,17 @@ def tile_moe_mlr_silu_kernel(
                 nc.tensor.transpose(bank[:, u * P : (u + 1) * P], gated[u][:, j * P : (j + 1) * P], ident[:])
             nc.scalar.copy(z[j][:], bank[:])
 
-        experts(0, [sums[0], sums[1]])
-        experts(1, [sums[2], sums[0]])
+        early = [(0, 0, 2), (1, 0, 4), (2, 0, 4), (3, 0, 4), (0, 2, 4)]
+        for n, (j, first, last) in enumerate(early):
+            experts(j, first, last, sums[n % BANKS])
         nc.tensor.transpose(turned[BANKS - 1][:, 0:P], gate_rows[:], ident[:])
         nc.scalar.copy(gate_cols[:], turned[BANKS - 1][:, 0:16])
         for u in range(4):
-            adapter_in(u, (1 + u) % BANKS)
+            adapter_in(u, (2 + u) % BANKS)
         nc.vector.quantize_mx(out=h_codes[:].bitcast(FP8X4), scales=h_scales[:], in_=h_in[:])
-        experts(2, h_turned)
+        experts(0, 4, E, sums[0])
+        experts(1, 4, E, sums[1])
+        experts(2, 4, E, h_turned[1])
         for u in range(4):
             adapter_out(u, (2 + u) % BANKS)
         for j in range(NT):
@@ -231,7 +242,7 @@ def tile_moe_mlr_silu_kernel(
                 nc.gpsimd.tensor_tensor(o_sb[j][:, 0:T], o_sb[j][:, 0:T], z_sb[j][:], ADD)
                 nc.sync.dma_start(out[j * P : (j + 1) * P, :], o_sb[j][:, 0:T])
         j = NT - 1
-        experts(j, [turned[2], turned[0]])
+        experts(j, 4, E, turned[j % BANKS])
         edges = [0, 384, 704, 896, T]
         for lo, hi in zip(edges[:-1], edges[1:]):
             nc.vector.tensor_tensor(o_sb[j][:, lo:hi], o_sb[j][:, lo:hi], z_sb[j][:, lo:hi], ADD)

@@ -40,15 +40,14 @@ def tile_moe_mlr_silu_kernel(
         offs_sb = keep.tile([P, T // 16], U16, name="offs_sb")
         offs2_sb = keep.tile([P, M // 16], U16, name="offs2_sb")
         x_sb = keep.tile([P, T + WIDE], I32, name="x_sb", align_bytes=64)
-        xs_rows = keep.tile([P, WIDE], U8, name="xs_rows", align_bytes=64)
-        slot_rows = keep.tile([P, M + T], U8, name="slot_rows", align_bytes=64)
-        planes = keep.tile([P, M + T], U8, name="planes", align_bytes=64)
-        a_plane0 = keep.tile([P, M], U8, name="a_plane0", align_bytes=64)
+        xs_rows = keep.tile([P, T], U8, name="xs_rows", align_bytes=64)
+        xs_planes = keep.tile([P, WIDE], U8, name="xs_planes", align_bytes=64)
+        a_rows = keep.tile([P, M], U8, name="a_rows", align_bytes=64)
+        e_planes = keep.tile([P, T], U8, name="e_planes", align_bytes=64)
+        a_planes = keep.tile([P, PASSES, M], U8, name="a_planes", align_bytes=64)
         e_words = [keep.tile([P, T], U32, name="e_words%d" % s, align_bytes=64) for s in range(PASSES)]
         a_words = [keep.tile([P, M], U32, name="a_words%d" % s, align_bytes=64) for s in range(PASSES)]
-        w_01 = keep.tile([P, 2 * PASSES, 4 * N], U8, name="w_01", align_bytes=64)
-        w_2 = keep.tile([P, PASSES, 4 * N], U8, name="w_2", align_bytes=64)
-        w_3 = keep.tile([P, PASSES, 4 * N], U8, name="w_3", align_bytes=64)
+        w_early = [keep.tile([P, 2 * PASSES, 4 * N], U8, name="w_early%d" % g, align_bytes=64) for g in range(2)]
         w_late = [keep.tile([P, 4 * PASSES, 2 * N], U8, name="w_late%d" % g, align_bytes=64) for g in range(2)]
         ws_sb = [keep.tile([P, N], U8, name="ws_sb%d" % g, align_bytes=64) for g in range(E // 2)]
         wa_sb = keep.tile([P, F * PASSES, 2 * H], U8, name="wa_sb", align_bytes=64)
@@ -76,13 +75,13 @@ def tile_moe_mlr_silu_kernel(
         def zero(tile_ap):
             nc.gpsimd.memset(tile_ap.bitcast(I32), 0)
 
+        zero(xs_planes[:, 0:T])
+        zero(xs_rows[32:64, :])
+        zero(xs_rows[64:P, :])
         zero(ws_sb[0][:])
-        zero(xs_rows[32:64, 0:T])
-        zero(xs_rows[64:P, 0:T])
         nc.gpsimd.memset(zero_col[:], 0.0)
-        zero(planes[:])
         zero(ws_sb[1][:])
-        zero(a_plane0[:])
+        zero(a_planes[:].rearrange("p a n -> p (a n)"))
         zero(was_sb[:].rearrange("p a n -> p (a n)"))
         nc.gpsimd.memset(gate_rows[:], 0.0)
         zero(ws_sb[2][:])
@@ -110,36 +109,34 @@ def tile_moe_mlr_silu_kernel(
                 )
 
         nc.sync.dma_start(offs2_sb[:], offs2)
-        for s in range(PASSES):
-            nc.sync.dma_start(
-                xs_rows[16 * (1 - s) : 16 * (2 - s), 0:T].bitcast(I32),
-                x_scales[s].rearrange("(q r) t -> r q t", r=ROWS).bitcast(I32),
-            )
+        nc.sync.dma_start(xs_rows[0:32, :].bitcast(I32), x_scales.rearrange("s b t -> (s b) t").bitcast(I32))
         nc.sync.dma_start(offs_sb[:], offs)
+        for q in range(QUADS):
+            nc.sync.dma_start(
+                xs_planes[32 * q + 2 * ROWS : 32 * q + 4 * ROWS, 0:T].bitcast(I32),
+                x_scales[:, ROWS * q : ROWS * (q + 1), :].bitcast(I32),
+            )
         nc.sync.dma_start(
             x_sb[:, 0 : PASSES * T].rearrange("p (s t) -> p s t", s=PASSES),
             x_words.rearrange("s p t d -> p s (t d)").bitcast(I32),
         )
-        nc.sync.dma_start(w_01[:].bitcast(I32), w_rows[:, 0:4, :].bitcast(I32))
+        nc.sync.dma_start(w_early[0][:].bitcast(I32), w_rows[:, 0:4, :].bitcast(I32))
         load_ws(0)
         nc.sync.dma_start(gate_sb[:, 0:N], gate[:, 0:N])
-        nc.sync.dma_start(w_2[:].bitcast(I32), w_rows[:, 4:6, :].bitcast(I32))
-        nc.vector.tensor_copy(slot_rows[:, 0:M], xs_rows[:, 0:T].indirect(offs2_sb[:]))
-        nc.vector.tensor_copy(slot_rows[:, M:], xs_rows[:].indirect(offs_sb[:]))
+        nc.sync.dma_start(w_early[1][:].bitcast(I32), w_rows[:, 4:8, :].bitcast(I32))
+        load_ws(1)
+        nc.vector.tensor_copy(a_rows[:], xs_rows[:].indirect(offs2_sb[:]))
+        nc.vector.tensor_copy(e_planes[:], xs_planes[:].indirect(offs_sb[:]))
         for s in range(PASSES):
             nc.vector.tensor_copy(e_words[s][:], x_sb[:, s * T : s * T + WIDE].bitcast(U32).indirect(offs_sb[:]))
         for s in range(PASSES):
             nc.vector.tensor_copy(a_words[s][:], x_sb[:, s * T : (s + 1) * T].bitcast(U32).indirect(offs2_sb[:]))
-        for q in range(QUADS):
-            nc.sync.dma_start(
-                planes[32 * q : 32 * q + 2 * ROWS, :].bitcast(I32), slot_rows[q:32:QUADS, :].bitcast(I32)
-            )
-        load_ws(1)
-        nc.sync.dma_start(w_3[:].bitcast(I32), w_rows[:, 6:8, :].bitcast(I32))
-        for q in range(QUADS):
-            nc.sync.dma_start(
-                a_plane0[32 * q : 32 * q + ROWS, :].bitcast(I32), slot_rows[16 + q : 32 : QUADS, 0:M].bitcast(I32)
-            )
+        for s in range(PASSES):
+            for q in range(QUADS):
+                row = 16 * s + ROWS * q
+                nc.sync.dma_start(
+                    a_planes[32 * q : 32 * q + ROWS, s, :].bitcast(I32), a_rows[row : row + ROWS, :].bitcast(I32)
+                )
         load_planes(was_sb[:], wa_scales.rearrange("f s b n -> (f s) b n"))
         nc.sync.dma_start(wa_sb[:].bitcast(I32), wa_words.rearrange("f s p n -> p (f s) n").bitcast(I32))
         nc.sync.dma_start(gate_rows[0:4, :], gate2[0].rearrange("(e p) -> e p", p=P))
@@ -154,8 +151,7 @@ def tile_moe_mlr_silu_kernel(
         def w_tile(e, s, j):
             if e >= 4:
                 return w_late[j // 2][:, PASSES * (e - 4) + s, 4 * P * (j % 2) : 4 * P * (j % 2 + 1)]
-            rows = w_01[:, PASSES * e + s, :] if e < 2 else (w_2, w_3)[e - 2][:, s, :]
-            return rows[:, 4 * P * j : 4 * P * (j + 1)]
+            return w_early[e // 2][:, PASSES * (e % 2) + s, 4 * P * j : 4 * P * (j + 1)]
 
         def experts(j, first, last, bank):
             for s in range(PASSES):
@@ -166,7 +162,7 @@ def tile_moe_mlr_silu_kernel(
                         lhsT=w_tile(e, s, j).bitcast(FP8X4),
                         lhsT_scale=ws_sb[e // 2][ROWS * a : P, j * P : (j + 1) * P],
                         rhs=e_words[s][:, e * C : (e + 1) * C].bitcast(FP8X4),
-                        rhs_scale=planes[ROWS * (1 - s) : P, M + e * C : M + (e + 1) * C],
+                        rhs_scale=e_planes[ROWS * (2 + s) : P, e * C : (e + 1) * C],
                         start=(s == 0 and e == first),
                         stop=(s == PASSES - 1 and e == last - 1),
                     )
@@ -183,7 +179,7 @@ def tile_moe_mlr_silu_kernel(
                 nc.tensor.matmul_mx(
                     out=sums[b][:],
                     lhsT=a_words[s][:, cols].bitcast(FP8X4),
-                    lhsT_scale=(planes if s else a_plane0)[:, cols],
+                    lhsT_scale=a_planes[:, s, cols],
                     rhs=wa_sb[:, f * PASSES + s, :].bitcast(FP4X4),
                     rhs_scale=was_sb[:, f * PASSES + s, :],
                     start=(s == 0),
@@ -222,19 +218,19 @@ def tile_moe_mlr_silu_kernel(
                 nc.tensor.transpose(bank[:, u * P : (u + 1) * P], gated[u][:, j * P : (j + 1) * P], ident[:])
             nc.scalar.copy(z[j][:], bank[:])
 
-        early = [(0, 0, 2), (1, 0, 4), (2, 0, 4), (3, 0, 4), (0, 2, 4)]
+        early = [(0, 0, 2), (1, 0, 2), (2, 0, 4), (3, 0, 4), (0, 2, 4), (1, 2, 4)]
         for n, (j, first, last) in enumerate(early):
             experts(j, first, last, sums[n % BANKS])
         nc.tensor.transpose(turned[BANKS - 1][:, 0:P], gate_rows[:], ident[:])
         nc.scalar.copy(gate_cols[:], turned[BANKS - 1][:, 0:16])
         for u in range(4):
-            adapter_in(u, (2 + u) % BANKS)
+            adapter_in(u, u % BANKS)
         nc.vector.quantize_mx(out=h_codes[:].bitcast(FP8X4), scales=h_scales[:], in_=h_in[:])
-        experts(0, 4, E, sums[0])
-        experts(1, 4, E, sums[1])
+        experts(0, 4, E, sums[1])
+        experts(1, 4, E, sums[2])
         experts(2, 4, E, h_turned[1])
         for u in range(4):
-            adapter_out(u, (2 + u) % BANKS)
+            adapter_out(u, u % BANKS)
         for j in range(NT):
             turn_back(j)
             nc.vector.tensor_copy(z_sb[j][:].indirect(offs2_sb[:]), z[j][:])

@@ -168,6 +168,9 @@ def tile_moe_mlr_silu_kernel(
                     )
             cols = slice(first * C, last * C)
             nc.scalar.copy(y[j][:, cols], bank[:, 0 : (last - first) * C])
+
+        def scatter_y(j, first, last):
+            cols = slice(first * C, last * C)
             nc.vector.tensor_tensor(
                 o_sb[j][:].indirect(offs_sb[:, first * C // 16 : last * C // 16]), y[j][:, cols], gate_sb[:, cols], MULT
             )
@@ -212,33 +215,61 @@ def tile_moe_mlr_silu_kernel(
             )
             nc.scalar.activation(gated[u][:], sums[b][:], COPY, scale=gate_cols[:, u : u + 1])
 
-        def turn_back(j):
-            bank = turned[j % BANKS]
+        def turn_back(j, bank):
             for u in range(M // P):
                 nc.tensor.transpose(bank[:, u * P : (u + 1) * P], gated[u][:, j * P : (j + 1) * P], ident[:])
             nc.scalar.copy(z[j][:], bank[:])
+            nc.vector.tensor_copy(z_sb[j][:].indirect(offs2_sb[:]), z[j][:])
 
         early = [(0, 0, 2), (1, 0, 2), (2, 0, 4), (3, 0, 4), (0, 2, 4), (1, 2, 4)]
         for n, (j, first, last) in enumerate(early):
             experts(j, first, last, sums[n % BANKS])
+            scatter_y(j, first, last)
         nc.tensor.transpose(turned[BANKS - 1][:, 0:P], gate_rows[:], ident[:])
         nc.scalar.copy(gate_cols[:], turned[BANKS - 1][:, 0:16])
         for u in range(4):
             adapter_in(u, u % BANKS)
         nc.vector.quantize_mx(out=h_codes[:].bitcast(FP8X4), scales=h_scales[:], in_=h_in[:])
-        experts(0, 4, E, sums[1])
-        experts(1, 4, E, sums[2])
-        experts(2, 4, E, h_turned[1])
+        for j in range(2):
+            experts(j, 4, E, h_turned[1])
+            scatter_y(j, 4, E)
         for u in range(4):
             adapter_out(u, u % BANKS)
-        for j in range(NT):
-            turn_back(j)
-            nc.vector.tensor_copy(z_sb[j][:].indirect(offs2_sb[:]), z[j][:])
-            if j < NT - 1:
-                nc.gpsimd.tensor_tensor(o_sb[j][:, 0:T], o_sb[j][:, 0:T], z_sb[j][:], ADD)
-                nc.sync.dma_start(out[j * P : (j + 1) * P, :], o_sb[j][:, 0:T])
+        def add_by_turns(j, there, back):
+            staged = gated[2 * (j % 2) : 2 * (j % 2) + 2]
+            for half in range(2):
+                bank = there[half]
+                for c in range(N // P):
+                    cols = slice(half * N + c * P, half * N + (c + 1) * P)
+                    for n, src in enumerate((o_sb[j], z_sb[j])):
+                        nc.tensor.matmul(
+                            bank[:, c * P : (c + 1) * P],
+                            src[:, cols],
+                            ident[:],
+                            start=(n == 0),
+                            stop=(n == 1),
+                            is_transpose=True,
+                        )
+                nc.scalar.copy(staged[half][:], bank[:])
+            for half in range(2):
+                bank = back[half]
+                for c in range(N // P):
+                    nc.tensor.transpose(bank[:, c * P : (c + 1) * P], staged[half][:, c * P : (c + 1) * P], ident[:])
+                nc.scalar.copy(y[j][:, half * N : (half + 1) * N], bank[:])
+            nc.scalar.dma_start(out[j * P : (j + 1) * P, :], y[j][:])
+
+        turn_back(0, turned[0])
+        turn_back(1, turned[1])
+        experts(2, 4, E, turned[1])
+        scatter_y(2, 4, E)
+        turn_back(2, turned[1])
+        turn_back(3, turned[1])
         j = NT - 1
-        experts(j, 4, E, turned[j % BANKS])
+        experts(j, 4, E, turned[1])
+        scatter_y(j, 4, E)
+        add_by_turns(0, [turned[1], turned[1]], [turned[0], turned[2]])
+        for done in range(1, NT - 1):
+            add_by_turns(done, [turned[0], turned[2]], [turned[1], sums[0]])
         edges = [0, 384, 704, 896, T]
         for lo, hi in zip(edges[:-1], edges[1:]):
             nc.vector.tensor_tensor(o_sb[j][:, lo:hi], o_sb[j][:, lo:hi], z_sb[j][:, lo:hi], ADD)

@@ -39,7 +39,7 @@ def tile_moe_mlr_silu_kernel(
 
         offs_sb = keep.tile([P, T // 16], U16, name="offs_sb")
         offs2_sb = keep.tile([P, M // 16], U16, name="offs2_sb")
-        x_sb = keep.tile([P, T + WIDE], I32, name="x_sb", align_bytes=64)
+        x_sb = keep.tile([P, PASSES * T], I32, name="x_sb", align_bytes=64)
         xs_rows = keep.tile([P, T], U8, name="xs_rows", align_bytes=64)
         xs_planes = keep.tile([P, WIDE], U8, name="xs_planes", align_bytes=64)
         a_rows = keep.tile([P, M], U8, name="a_rows", align_bytes=64)
@@ -47,7 +47,7 @@ def tile_moe_mlr_silu_kernel(
         a_planes = keep.tile([P, PASSES, M], U8, name="a_planes", align_bytes=64)
         e_words = [keep.tile([P, T], U32, name="e_words%d" % s, align_bytes=64) for s in range(PASSES)]
         a_words = [keep.tile([P, M], U32, name="a_words%d" % s, align_bytes=64) for s in range(PASSES)]
-        w_early = [keep.tile([P, 2 * PASSES, 4 * N], U8, name="w_early%d" % g, align_bytes=64) for g in range(2)]
+        w_early = [keep.tile([P, PASSES, 4 * N], U8, name="w_early%d" % e, align_bytes=64) for e in range(4)]
         w_late = [keep.tile([P, 4 * PASSES, 2 * N], U8, name="w_late%d" % g, align_bytes=64) for g in range(2)]
         ws_sb = [keep.tile([P, N], U8, name="ws_sb%d" % g, align_bytes=64) for g in range(E // 2)]
         wa_sb = keep.tile([P, F * PASSES, 2 * H], U8, name="wa_sb", align_bytes=64)
@@ -120,17 +120,29 @@ def tile_moe_mlr_silu_kernel(
             x_sb[:, 0 : PASSES * T].rearrange("p (s t) -> p s t", s=PASSES),
             x_words.rearrange("s p t d -> p s (t d)").bitcast(I32),
         )
-        nc.sync.dma_start(w_early[0][:].bitcast(I32), w_rows[:, 0:4, :].bitcast(I32))
+
+        def load_early(e):
+            nc.sync.dma_start(w_early[e][:].bitcast(I32), w_rows[:, PASSES * e : PASSES * (e + 1), :].bitcast(I32))
+
+        def gather_words(dst, s, offsets):
+            nc.vector.tensor_copy(dst, x_sb[:, s * T : (s + 1) * T].bitcast(U32).indirect(offsets))
+
+        load_early(0)
         load_ws(0)
         nc.sync.dma_start(gate_sb[:, 0:N], gate[:, 0:N])
-        nc.sync.dma_start(w_early[1][:].bitcast(I32), w_rows[:, 4:8, :].bitcast(I32))
+        load_early(1)
+        load_early(2)
         load_ws(1)
+        load_early(3)
         nc.vector.tensor_copy(a_rows[:], xs_rows[:].indirect(offs2_sb[:]))
         nc.vector.tensor_copy(e_planes[:], xs_planes[:].indirect(offs_sb[:]))
         for s in range(PASSES):
-            nc.vector.tensor_copy(e_words[s][:], x_sb[:, s * T : s * T + WIDE].bitcast(U32).indirect(offs_sb[:]))
+            gather_words(e_words[s][:, 0:N], s, offs_sb[:, 0:32])
         for s in range(PASSES):
-            nc.vector.tensor_copy(a_words[s][:], x_sb[:, s * T : (s + 1) * T].bitcast(U32).indirect(offs2_sb[:]))
+            gather_words(a_words[s][:], s, offs2_sb[:])
+        for s in range(PASSES):
+            gather_words(e_words[s][:, N:], s, offs_sb[:, 32:64])
+        nc.sync.dma_start(wa_sb[:].bitcast(I32), wa_words.rearrange("f s p n -> p (f s) n").bitcast(I32))
         for s in range(PASSES):
             for q in range(QUADS):
                 row = 16 * s + ROWS * q
@@ -138,20 +150,19 @@ def tile_moe_mlr_silu_kernel(
                     a_planes[32 * q : 32 * q + ROWS, s, :].bitcast(I32), a_rows[row : row + ROWS, :].bitcast(I32)
                 )
         load_planes(was_sb[:], wa_scales.rearrange("f s b n -> (f s) b n"))
-        nc.sync.dma_start(wa_sb[:].bitcast(I32), wa_words.rearrange("f s p n -> p (f s) n").bitcast(I32))
+        nc.sync.dma_start(w_late[0][:].bitcast(I32), w_rows[:, 8:, 0 : 2 * N].bitcast(I32))
         nc.sync.dma_start(gate_rows[0:4, :], gate2[0].rearrange("(e p) -> e p", p=P))
         load_ws(2)
-        load_ws(3)
-        nc.sync.dma_start(w_late[0][:].bitcast(I32), w_rows[:, 8:, 0 : 2 * N].bitcast(I32))
         nc.sync.dma_start(gate_sb[:, N:], gate[:, N:])
-        nc.sync.dma_start(w_late[1][:].bitcast(I32), w_rows[:, 8:, 2 * N :].bitcast(I32))
-        load_planes(wbs_sb[:], wb_scales.rearrange("f s b n -> (f s) b n"))
         nc.sync.dma_start(wb_sb[:].bitcast(I32), wb_words.rearrange("f s p n -> p (f s) n").bitcast(I32))
+        load_ws(3)
+        load_planes(wbs_sb[:], wb_scales.rearrange("f s b n -> (f s) b n"))
+        nc.sync.dma_start(w_late[1][:].bitcast(I32), w_rows[:, 8:, 2 * N :].bitcast(I32))
 
         def w_tile(e, s, j):
             if e >= 4:
                 return w_late[j // 2][:, PASSES * (e - 4) + s, 4 * P * (j % 2) : 4 * P * (j % 2 + 1)]
-            return w_early[e // 2][:, PASSES * (e % 2) + s, 4 * P * j : 4 * P * (j + 1)]
+            return w_early[e][:, s, 4 * P * j : 4 * P * (j + 1)]
 
         def experts(j, first, last, bank):
             for s in range(PASSES):
@@ -215,61 +226,60 @@ def tile_moe_mlr_silu_kernel(
             )
             nc.scalar.activation(gated[u][:], sums[b][:], COPY, scale=gate_cols[:, u : u + 1])
 
-        def turn_back(j, bank):
-            for u in range(M // P):
-                nc.tensor.transpose(bank[:, u * P : (u + 1) * P], gated[u][:, j * P : (j + 1) * P], ident[:])
-            nc.scalar.copy(z[j][:], bank[:])
+        def turn_back(j, banks):
+            blocks = M // P // len(banks)
+            for n, bank in enumerate(banks):
+                for c in range(blocks):
+                    u = n * blocks + c
+                    nc.tensor.transpose(bank[:, c * P : (c + 1) * P], gated[u][:, j * P : (j + 1) * P], ident[:])
+                nc.scalar.copy(z[j][:, n * blocks * P : (n + 1) * blocks * P], bank[:, 0 : blocks * P])
             nc.vector.tensor_copy(z_sb[j][:].indirect(offs2_sb[:]), z[j][:])
 
-        early = [(0, 0, 2), (1, 0, 2), (2, 0, 4), (3, 0, 4), (0, 2, 4), (1, 2, 4)]
+        early = [(0, 0, 1), (1, 0, 1), (2, 0, 2), (3, 0, 2), (0, 1, 4), (1, 1, 4), (2, 2, 4), (3, 2, 4)]
         for n, (j, first, last) in enumerate(early):
             experts(j, first, last, sums[n % BANKS])
             scatter_y(j, first, last)
         nc.tensor.transpose(turned[BANKS - 1][:, 0:P], gate_rows[:], ident[:])
         nc.scalar.copy(gate_cols[:], turned[BANKS - 1][:, 0:16])
         for u in range(4):
-            adapter_in(u, u % BANKS)
+            adapter_in(u, (len(early) + u) % BANKS)
         nc.vector.quantize_mx(out=h_codes[:].bitcast(FP8X4), scales=h_scales[:], in_=h_in[:])
-        for j in range(2):
-            experts(j, 4, E, h_turned[1])
+        for j, bank in enumerate([sums[0], sums[1], h_turned[1]]):
+            experts(j, 4, E, bank)
             scatter_y(j, 4, E)
         for u in range(4):
-            adapter_out(u, u % BANKS)
+            adapter_out(u, (2 + u) % BANKS)
         def add_by_turns(j, there, back):
-            staged = gated[2 * (j % 2) : 2 * (j % 2) + 2]
-            for half in range(2):
-                bank = there[half]
-                for c in range(N // P):
-                    cols = slice(half * N + c * P, half * N + (c + 1) * P)
-                    for n, src in enumerate((o_sb[j], z_sb[j])):
+            for n, src in enumerate((o_sb[j], z_sb[j])):
+                for half in range(2):
+                    for c in range(N // P):
                         nc.tensor.matmul(
-                            bank[:, c * P : (c + 1) * P],
-                            src[:, cols],
+                            there[half][:, c * P : (c + 1) * P],
+                            src[:, half * N + c * P : half * N + (c + 1) * P],
                             ident[:],
-                            start=(n == 0),
-                            stop=(n == 1),
+                            start=(n == 0 and c == 0),
+                            stop=(n == 1 and c == N // P - 1),
                             is_transpose=True,
                         )
-                nc.scalar.copy(staged[half][:], bank[:])
             for half in range(2):
-                bank = back[half]
+                nc.scalar.copy(gated[half][:], there[half][:])
+            for half in range(2):
+                cols = slice(half * N, (half + 1) * N)
                 for c in range(N // P):
-                    nc.tensor.transpose(bank[:, c * P : (c + 1) * P], staged[half][:, c * P : (c + 1) * P], ident[:])
-                nc.scalar.copy(y[j][:, half * N : (half + 1) * N], bank[:])
-            nc.scalar.dma_start(out[j * P : (j + 1) * P, :], y[j][:])
+                    nc.tensor.transpose(back[half][:, c * P : (c + 1) * P], gated[half][:, c * P : (c + 1) * P], ident[:])
+                nc.scalar.copy(y[j][:, cols], back[half][:])
+                nc.scalar.dma_start(out[j * P : (j + 1) * P, cols], y[j][:, cols])
 
-        turn_back(0, turned[0])
-        turn_back(1, turned[1])
-        experts(2, 4, E, turned[1])
-        scatter_y(2, 4, E)
-        turn_back(2, turned[1])
-        turn_back(3, turned[1])
+        for j in range(NT):
+            turn_back(j, [turned[j]] if j < BANKS else turned[0:2])
+            if j < 2:
+                nc.gpsimd.tensor_tensor(o_sb[j][:], o_sb[j][:], z_sb[j][:], ADD)
+                nc.sync.dma_start(out[j * P : (j + 1) * P, :], o_sb[j][:])
         j = NT - 1
-        experts(j, 4, E, turned[1])
+        experts(j, 4, 6, turned[0])
+        experts(j, 6, E, turned[1])
         scatter_y(j, 4, E)
-        add_by_turns(0, [turned[1], turned[1]], [turned[0], turned[2]])
-        for done in range(1, NT - 1):
-            add_by_turns(done, [turned[0], turned[2]], [turned[1], sums[0]])
+        add_by_turns(2, [turned[0], turned[1]], [turned[2], sums[0]])
         edges = [0, 384, 704, 896, T]
         for lo, hi in zip(edges[:-1], edges[1:]):
             nc.vector.tensor_tensor(o_sb[j][:, lo:hi], o_sb[j][:, lo:hi], z_sb[j][:, lo:hi], ADD)

@@ -40,11 +40,10 @@ def tile_moe_mlr_silu_kernel(
         offs_sb = keep.tile([P, T // 16], U16, name="offs_sb")
         offs2_sb = keep.tile([P, M // 16], U16, name="offs2_sb")
         x_sb = keep.tile([P, PASSES * T], I32, name="x_sb", align_bytes=64)
-        xs_rows = keep.tile([P, T], U8, name="xs_rows", align_bytes=64)
-        xs_planes = keep.tile([P, WIDE], U8, name="xs_planes", align_bytes=64)
-        a_rows = keep.tile([P, M], U8, name="a_rows", align_bytes=64)
-        e_planes = keep.tile([P, T], U8, name="e_planes", align_bytes=64)
-        a_planes = keep.tile([P, PASSES, M], U8, name="a_planes", align_bytes=64)
+        xs_rows = keep.tile([P, WIDE], U8, name="xs_rows", align_bytes=64)
+        slot_rows = keep.tile([P, M + T], U8, name="slot_rows", align_bytes=64)
+        planes = keep.tile([P, M + T], U8, name="planes", align_bytes=64)
+        a_plane0 = keep.tile([P, M], U8, name="a_plane0", align_bytes=64)
         e_words = [keep.tile([P, T], U32, name="e_words%d" % s, align_bytes=64) for s in range(PASSES)]
         a_words = [keep.tile([P, M], U32, name="a_words%d" % s, align_bytes=64) for s in range(PASSES)]
         w_early = [keep.tile([P, PASSES, 4 * N], U8, name="w_early%d" % e, align_bytes=64) for e in range(4)]
@@ -75,13 +74,13 @@ def tile_moe_mlr_silu_kernel(
         def zero(tile_ap):
             nc.gpsimd.memset(tile_ap.bitcast(I32), 0)
 
-        zero(xs_planes[:, 0:T])
-        zero(xs_rows[32:64, :])
-        zero(xs_rows[64:P, :])
         zero(ws_sb[0][:])
+        zero(xs_rows[32:64, 0:T])
+        zero(xs_rows[64:P, 0:T])
         nc.gpsimd.memset(zero_col[:], 0.0)
+        zero(planes[:])
         zero(ws_sb[1][:])
-        zero(a_planes[:].rearrange("p a n -> p (a n)"))
+        zero(a_plane0[:])
         zero(was_sb[:].rearrange("p a n -> p (a n)"))
         nc.gpsimd.memset(gate_rows[:], 0.0)
         zero(ws_sb[2][:])
@@ -109,13 +108,12 @@ def tile_moe_mlr_silu_kernel(
                 )
 
         nc.sync.dma_start(offs2_sb[:], offs2)
-        nc.sync.dma_start(xs_rows[0:32, :].bitcast(I32), x_scales.rearrange("s b t -> (s b) t").bitcast(I32))
-        nc.sync.dma_start(offs_sb[:], offs)
-        for q in range(QUADS):
+        for s in range(PASSES):
             nc.sync.dma_start(
-                xs_planes[32 * q + 2 * ROWS : 32 * q + 4 * ROWS, 0:T].bitcast(I32),
-                x_scales[:, ROWS * q : ROWS * (q + 1), :].bitcast(I32),
+                xs_rows[16 * (1 - s) : 16 * (2 - s), 0:T].bitcast(I32),
+                x_scales[s].rearrange("(q r) t -> r q t", r=ROWS).bitcast(I32),
             )
+        nc.sync.dma_start(offs_sb[:], offs)
         nc.sync.dma_start(
             x_sb[:, 0 : PASSES * T].rearrange("p (s t) -> p s t", s=PASSES),
             x_words.rearrange("s p t d -> p s (t d)").bitcast(I32),
@@ -132,10 +130,14 @@ def tile_moe_mlr_silu_kernel(
         nc.sync.dma_start(gate_sb[:, 0:N], gate[:, 0:N])
         load_early(1)
         load_early(2)
+        nc.vector.tensor_copy(slot_rows[:, 0:M], xs_rows[:, 0:T].indirect(offs2_sb[:]))
+        nc.vector.tensor_copy(slot_rows[:, M:], xs_rows[:].indirect(offs_sb[:]))
+        for q in range(QUADS):
+            nc.sync.dma_start(
+                planes[32 * q : 32 * q + 2 * ROWS, :].bitcast(I32), slot_rows[q:32:QUADS, :].bitcast(I32)
+            )
         load_ws(1)
         load_early(3)
-        nc.vector.tensor_copy(a_rows[:], xs_rows[:].indirect(offs2_sb[:]))
-        nc.vector.tensor_copy(e_planes[:], xs_planes[:].indirect(offs_sb[:]))
         for s in range(PASSES):
             gather_words(e_words[s][:, 0:N], s, offs_sb[:, 0:32])
         for s in range(PASSES):
@@ -143,12 +145,10 @@ def tile_moe_mlr_silu_kernel(
         for s in range(PASSES):
             gather_words(e_words[s][:, N:], s, offs_sb[:, 32:64])
         nc.sync.dma_start(wa_sb[:].bitcast(I32), wa_words.rearrange("f s p n -> p (f s) n").bitcast(I32))
-        for s in range(PASSES):
-            for q in range(QUADS):
-                row = 16 * s + ROWS * q
-                nc.sync.dma_start(
-                    a_planes[32 * q : 32 * q + ROWS, s, :].bitcast(I32), a_rows[row : row + ROWS, :].bitcast(I32)
-                )
+        for q in range(QUADS):
+            nc.sync.dma_start(
+                a_plane0[32 * q : 32 * q + ROWS, :].bitcast(I32), slot_rows[16 + q : 32 : QUADS, 0:M].bitcast(I32)
+            )
         load_planes(was_sb[:], wa_scales.rearrange("f s b n -> (f s) b n"))
         nc.sync.dma_start(w_late[0][:].bitcast(I32), w_rows[:, 8:, 0 : 2 * N].bitcast(I32))
         nc.sync.dma_start(gate_rows[0:4, :], gate2[0].rearrange("(e p) -> e p", p=P))
@@ -173,7 +173,7 @@ def tile_moe_mlr_silu_kernel(
                         lhsT=w_tile(e, s, j).bitcast(FP8X4),
                         lhsT_scale=ws_sb[e // 2][ROWS * a : P, j * P : (j + 1) * P],
                         rhs=e_words[s][:, e * C : (e + 1) * C].bitcast(FP8X4),
-                        rhs_scale=e_planes[ROWS * (2 + s) : P, e * C : (e + 1) * C],
+                        rhs_scale=planes[ROWS * (1 - s) : P, M + e * C : M + (e + 1) * C],
                         start=(s == 0 and e == first),
                         stop=(s == PASSES - 1 and e == last - 1),
                     )
@@ -193,7 +193,7 @@ def tile_moe_mlr_silu_kernel(
                 nc.tensor.matmul_mx(
                     out=sums[b][:],
                     lhsT=a_words[s][:, cols].bitcast(FP8X4),
-                    lhsT_scale=a_planes[:, s, cols],
+                    lhsT_scale=(planes if s else a_plane0)[:, cols],
                     rhs=wa_sb[:, f * PASSES + s, :].bitcast(FP4X4),
                     rhs_scale=was_sb[:, f * PASSES + s, :],
                     start=(s == 0),

@@ -109,7 +109,7 @@ def tile_moe_mlr_silu_kernel(
 
         nc.sync.dma_start(offs2_sb[:], offs2)
         for s in range(PASSES):
-            nc.sync.dma_start(
+            nc.scalar.dma_start(
                 xs_rows[16 * (1 - s) : 16 * (2 - s), 0:T].bitcast(I32),
                 x_scales[s].rearrange("(q r) t -> r q t", r=ROWS).bitcast(I32),
             )
@@ -122,8 +122,8 @@ def tile_moe_mlr_silu_kernel(
         def load_early(e):
             nc.sync.dma_start(w_early[e][:].bitcast(I32), w_rows[:, PASSES * e : PASSES * (e + 1), :].bitcast(I32))
 
-        def gather_words(dst, s, offsets):
-            nc.vector.tensor_copy(dst, x_sb[:, s * T : (s + 1) * T].bitcast(U32).indirect(offsets))
+        def gather_words(dst, s, offsets, window=T):
+            nc.vector.tensor_copy(dst, x_sb[:, s * T : s * T + window].bitcast(U32).indirect(offsets))
 
         load_early(0)
         load_ws(0)
@@ -138,12 +138,11 @@ def tile_moe_mlr_silu_kernel(
             )
         load_ws(1)
         load_early(3)
-        for s in range(PASSES):
-            gather_words(e_words[s][:, 0:N], s, offs_sb[:, 0:32])
+        gather_words(e_words[0][:], 0, offs_sb[:], WIDE)
+        gather_words(e_words[1][:, 0:N], 1, offs_sb[:, 0:32])
         for s in range(PASSES):
             gather_words(a_words[s][:], s, offs2_sb[:])
-        for s in range(PASSES):
-            gather_words(e_words[s][:, N:], s, offs_sb[:, 32:64])
+        gather_words(e_words[1][:, N:], 1, offs_sb[:, 32:64])
         nc.sync.dma_start(wa_sb[:].bitcast(I32), wa_words.rearrange("f s p n -> p (f s) n").bitcast(I32))
         for q in range(QUADS):
             nc.sync.dma_start(
@@ -235,7 +234,7 @@ def tile_moe_mlr_silu_kernel(
                 nc.scalar.copy(z[j][:, n * blocks * P : (n + 1) * blocks * P], bank[:, 0 : blocks * P])
             nc.vector.tensor_copy(z_sb[j][:].indirect(offs2_sb[:]), z[j][:])
 
-        early = [(0, 0, 1), (1, 0, 1), (2, 0, 2), (3, 0, 2), (0, 1, 4), (1, 1, 4), (2, 2, 4), (3, 2, 4)]
+        early = [(0, 0, 2), (1, 0, 2), (2, 0, 4), (3, 0, 4), (0, 2, 4), (1, 2, 4)]
         for n, (j, first, last) in enumerate(early):
             experts(j, first, last, sums[n % BANKS])
             scatter_y(j, first, last)
@@ -244,11 +243,11 @@ def tile_moe_mlr_silu_kernel(
         for u in range(4):
             adapter_in(u, (len(early) + u) % BANKS)
         nc.vector.quantize_mx(out=h_codes[:].bitcast(FP8X4), scales=h_scales[:], in_=h_in[:])
-        for j, bank in enumerate([sums[0], sums[1], h_turned[1]]):
+        for j, bank in enumerate([sums[1], sums[2], h_turned[1]]):
             experts(j, 4, E, bank)
             scatter_y(j, 4, E)
         for u in range(4):
-            adapter_out(u, (2 + u) % BANKS)
+            adapter_out(u, u % BANKS)
         def add_by_turns(j, there, back):
             for n, src in enumerate((o_sb[j], z_sb[j])):
                 for half in range(2):
@@ -279,8 +278,8 @@ def tile_moe_mlr_silu_kernel(
         experts(j, 4, 6, turned[0])
         experts(j, 6, E, turned[1])
         scatter_y(j, 4, E)
-        add_by_turns(2, [turned[0], turned[1]], [turned[2], sums[0]])
-        edges = [0, 384, 704, 896, T]
+        add_by_turns(2, [turned[0], turned[1]], [turned[2], sums[1]])
+        edges = [0, 256, 640, T]
         for lo, hi in zip(edges[:-1], edges[1:]):
             nc.vector.tensor_tensor(o_sb[j][:, lo:hi], o_sb[j][:, lo:hi], z_sb[j][:, lo:hi], ADD)
             nc.sync.dma_start(out[j * P : (j + 1) * P, lo:hi], o_sb[j][:, lo:hi])

@@ -77,9 +77,9 @@ def tile_moe_mlr_silu_kernel(
         zero(ws_sb[0][:])
         zero(xs_rows[32:64, 0:T])
         zero(xs_rows[64:P, 0:T])
+        zero(ws_sb[1][:])
         nc.gpsimd.memset(zero_col[:], 0.0)
         zero(planes[:])
-        zero(ws_sb[1][:])
         zero(a_plane0[:])
         zero(was_sb[:].rearrange("p a n -> p (a n)"))
         nc.gpsimd.memset(gate_rows[:], 0.0)
@@ -109,7 +109,7 @@ def tile_moe_mlr_silu_kernel(
 
         nc.sync.dma_start(offs2_sb[:], offs2)
         for s in range(PASSES):
-            nc.scalar.dma_start(
+            nc.sync.dma_start(
                 xs_rows[16 * (1 - s) : 16 * (2 - s), 0:T].bitcast(I32),
                 x_scales[s].rearrange("(q r) t -> r q t", r=ROWS).bitcast(I32),
             )
@@ -127,16 +127,16 @@ def tile_moe_mlr_silu_kernel(
 
         load_early(0)
         load_ws(0)
-        nc.sync.dma_start(gate_sb[:, 0:N], gate[:, 0:N])
         load_early(1)
-        load_early(2)
+        load_ws(1)
         nc.vector.tensor_copy(slot_rows[:, 0:M], xs_rows[:, 0:T].indirect(offs2_sb[:]))
         nc.vector.tensor_copy(slot_rows[:, M:], xs_rows[:].indirect(offs_sb[:]))
         for q in range(QUADS):
             nc.sync.dma_start(
                 planes[32 * q : 32 * q + 2 * ROWS, :].bitcast(I32), slot_rows[q:32:QUADS, :].bitcast(I32)
             )
-        load_ws(1)
+        nc.sync.dma_start(gate_sb[:, 0:N], gate[:, 0:N])
+        load_early(2)
         load_early(3)
         gather_words(e_words[0][:], 0, offs_sb[:], WIDE)
         gather_words(e_words[1][:, 0:N], 1, offs_sb[:, 0:32])

@@ -27,6 +27,7 @@ M = F * D
 NT = N // P
 BANKS = 3
 WIDE = 1376
+ROW0 = 96
 
 
 def tile_moe_mlr_silu_kernel(
@@ -39,7 +40,7 @@ def tile_moe_mlr_silu_kernel(
 
         offs_sb = keep.tile([P, T // 16], U16, name="offs_sb")
         offs2_sb = keep.tile([P, M // 16], U16, name="offs2_sb")
-        x_sb = keep.tile([P, PASSES * T], I32, name="x_sb", align_bytes=64)
+        x_sb = keep.tile([P, T + WIDE], I32, name="x_sb", align_bytes=64)
         xs_rows = keep.tile([P, WIDE], U8, name="xs_rows", align_bytes=64)
         slot_rows = keep.tile([P, M + T], U8, name="slot_rows", align_bytes=64)
         planes = keep.tile([P, M + T], U8, name="planes", align_bytes=64)
@@ -75,8 +76,7 @@ def tile_moe_mlr_silu_kernel(
             nc.gpsimd.memset(tile_ap.bitcast(I32), 0)
 
         zero(ws_sb[0][:])
-        zero(xs_rows[32:64, 0:T])
-        zero(xs_rows[64:P, 0:T])
+        nc.vector.memset(xs_rows[0:ROW0, 0 : T + 4].bitcast(I32), 0)
         zero(ws_sb[1][:])
         nc.gpsimd.memset(zero_col[:], 0.0)
         zero(planes[:])
@@ -110,7 +110,7 @@ def tile_moe_mlr_silu_kernel(
         nc.sync.dma_start(offs2_sb[:], offs2)
         for s in range(PASSES):
             nc.sync.dma_start(
-                xs_rows[16 * (1 - s) : 16 * (2 - s), 0:T].bitcast(I32),
+                xs_rows[ROW0 + 16 * (1 - s) : ROW0 + 16 * (2 - s), 0:T].bitcast(I32),
                 x_scales[s].rearrange("(q r) t -> r q t", r=ROWS).bitcast(I32),
             )
         nc.sync.dma_start(offs_sb[:], offs)
@@ -133,20 +133,19 @@ def tile_moe_mlr_silu_kernel(
         nc.vector.tensor_copy(slot_rows[:, M:], xs_rows[:].indirect(offs_sb[:]))
         for q in range(QUADS):
             nc.sync.dma_start(
-                planes[32 * q : 32 * q + 2 * ROWS, :].bitcast(I32), slot_rows[q:32:QUADS, :].bitcast(I32)
+                planes[32 * q : 32 * q + 2 * ROWS, :].bitcast(I32), slot_rows[ROW0 + q : P : QUADS, :].bitcast(I32)
             )
         nc.sync.dma_start(gate_sb[:, 0:N], gate[:, 0:N])
         load_early(2)
         load_early(3)
-        gather_words(e_words[0][:], 0, offs_sb[:], WIDE)
-        gather_words(e_words[1][:, 0:N], 1, offs_sb[:, 0:32])
+        for s in range(PASSES):
+            gather_words(e_words[s][:], s, offs_sb[:], WIDE)
         for s in range(PASSES):
             gather_words(a_words[s][:], s, offs2_sb[:])
-        gather_words(e_words[1][:, N:], 1, offs_sb[:, 32:64])
         nc.sync.dma_start(wa_sb[:].bitcast(I32), wa_words.rearrange("f s p n -> p (f s) n").bitcast(I32))
         for q in range(QUADS):
             nc.sync.dma_start(
-                a_plane0[32 * q : 32 * q + ROWS, :].bitcast(I32), slot_rows[16 + q : 32 : QUADS, 0:M].bitcast(I32)
+                a_plane0[32 * q : 32 * q + ROWS, :].bitcast(I32), slot_rows[ROW0 + 16 + q : P : QUADS, 0:M].bitcast(I32)
             )
         load_planes(was_sb[:], wa_scales.rearrange("f s b n -> (f s) b n"))
         nc.sync.dma_start(w_late[0][:].bitcast(I32), w_rows[:, 8:, 0 : 2 * N].bitcast(I32))

@@ -28,6 +28,7 @@ NT = N // P
 BANKS = 3
 WIDE = 1376
 ROW0 = 96
+GROUP = E // 2
 
 
 def tile_moe_mlr_silu_kernel(
@@ -47,9 +48,9 @@ def tile_moe_mlr_silu_kernel(
         a_plane0 = keep.tile([P, M], U8, name="a_plane0", align_bytes=64)
         e_words = [keep.tile([P, T], U32, name="e_words%d" % s, align_bytes=64) for s in range(PASSES)]
         a_words = [keep.tile([P, M], U32, name="a_words%d" % s, align_bytes=64) for s in range(PASSES)]
-        w_early = [keep.tile([P, PASSES, 4 * N], U8, name="w_early%d" % e, align_bytes=64) for e in range(4)]
-        w_late = [keep.tile([P, 4 * PASSES, 2 * N], U8, name="w_late%d" % g, align_bytes=64) for g in range(2)]
-        ws_sb = [keep.tile([P, N], U8, name="ws_sb%d" % g, align_bytes=64) for g in range(E // 2)]
+        w_left = [keep.tile([P, GROUP * PASSES, 2 * N], U8, name="w_left%d" % g, align_bytes=64) for g in range(2)]
+        w_right = keep.tile([P, E * PASSES, 2 * N], U8, name="w_right", align_bytes=64)
+        ws_sb = [keep.tile([P, GROUP * PASSES, N], U8, name="ws_sb%d" % g, align_bytes=64) for g in range(2)]
         wa_sb = keep.tile([P, F * PASSES, 2 * H], U8, name="wa_sb", align_bytes=64)
         was_sb = keep.tile([P, F * PASSES, H], U8, name="was_sb", align_bytes=64)
         wb_sb = keep.tile([P, F, 2 * N], U8, name="wb_sb", align_bytes=64)
@@ -59,7 +60,7 @@ def tile_moe_mlr_silu_kernel(
         gate_sb = keep.tile([P, T], F32, name="gate_sb")
         zero_col = keep.tile([P, 1], F32, name="zero_col")
         ident = keep.tile([P, P], F32, name="ident")
-        o_sb = [keep.tile([P, T], F32, name="o_sb%d" % j) for j in range(NT)]
+        o_sb = [keep.tile([P, WIDE if j else T], F32, name="o_sb%d" % j) for j in range(NT)]
         z_sb = [keep.tile([P, T], F32, name="z_sb%d" % j) for j in range(NT)]
         y = [keep.tile([P, T], F32, name="y%d" % j) for j in range(NT)]
         z = [keep.tile([P, M], F32, name="z%d" % j) for j in range(NT)]
@@ -75,37 +76,27 @@ def tile_moe_mlr_silu_kernel(
         def zero(tile_ap):
             nc.gpsimd.memset(tile_ap.bitcast(I32), 0)
 
-        zero(ws_sb[0][:])
+        zero(ws_sb[0][:].rearrange("p a n -> p (a n)"))
         nc.vector.memset(xs_rows[0:ROW0, 0 : T + 4].bitcast(I32), 0)
-        zero(ws_sb[1][:])
         nc.gpsimd.memset(zero_col[:], 0.0)
         zero(planes[:])
+        zero(ws_sb[1][:].rearrange("p a n -> p (a n)"))
         zero(a_plane0[:])
         zero(was_sb[:].rearrange("p a n -> p (a n)"))
         nc.gpsimd.memset(gate_rows[:], 0.0)
-        zero(ws_sb[2][:])
-        zero(ws_sb[3][:])
         make_identity(nc, ident[:])
         zero(wbs_sb[:].rearrange("p a n -> p (a n)"))
         for j in range(NT):
             nc.scalar.activation(z_sb[j][:], zero_col[:].to_broadcast([P, T]), SILU)
 
         def load_planes(dst, src):
-            for q in range(QUADS):
-                nc.sync.dma_start(
-                    dst[32 * q : 32 * q + ROWS, :, :].bitcast(I32),
-                    src[:, ROWS * q : ROWS * (q + 1), :].rearrange("a r n -> r a n").bitcast(I32),
-                )
+            rows = src.rearrange("a (q r) n -> r q a n", r=ROWS)
+            for r in range(ROWS):
+                nc.sync.dma_start(dst[r:P:32, :, :].bitcast(I32), rows[r].bitcast(I32))
 
         w_rows = w_words.rearrange("e s p n d -> p (e s) (n d)")
         ws_rows = w_scales.rearrange("e s b n -> (e s) b n")
-
-        def load_ws(g):
-            for q in range(QUADS):
-                nc.sync.dma_start(
-                    ws_sb[g][32 * q : 32 * q + 4 * ROWS, :].bitcast(I32),
-                    ws_rows[4 * g : 4 * (g + 1), ROWS * q : ROWS * (q + 1), :].bitcast(I32),
-                )
+        group = [slice(g * GROUP * PASSES, (g + 1) * GROUP * PASSES) for g in range(2)]
 
         nc.sync.dma_start(offs2_sb[:], offs2)
         for s in range(PASSES):
@@ -119,16 +110,11 @@ def tile_moe_mlr_silu_kernel(
             x_words.rearrange("s p t d -> p s (t d)").bitcast(I32),
         )
 
-        def load_early(e):
-            nc.sync.dma_start(w_early[e][:].bitcast(I32), w_rows[:, PASSES * e : PASSES * (e + 1), :].bitcast(I32))
-
         def gather_words(dst, s, offsets, window=T):
             nc.vector.tensor_copy(dst, x_sb[:, s * T : s * T + window].bitcast(U32).indirect(offsets))
 
-        load_early(0)
-        load_ws(0)
-        load_early(1)
-        load_ws(1)
+        load_planes(ws_sb[0][:], ws_rows[group[0]])
+        nc.sync.dma_start(w_left[0][:].bitcast(I32), w_rows[:, group[0], 0 : 2 * N].bitcast(I32))
         nc.vector.tensor_copy(slot_rows[:, 0:M], xs_rows[:, 0:T].indirect(offs2_sb[:]))
         nc.vector.tensor_copy(slot_rows[:, M:], xs_rows[:].indirect(offs_sb[:]))
         for q in range(QUADS):
@@ -136,40 +122,37 @@ def tile_moe_mlr_silu_kernel(
                 planes[32 * q : 32 * q + 2 * ROWS, :].bitcast(I32), slot_rows[ROW0 + q : P : QUADS, :].bitcast(I32)
             )
         nc.sync.dma_start(gate_sb[:, 0:N], gate[:, 0:N])
-        load_early(2)
-        load_early(3)
+        nc.sync.dma_start(w_left[1][:].bitcast(I32), w_rows[:, group[1], 0 : 2 * N].bitcast(I32))
         for s in range(PASSES):
             gather_words(e_words[s][:], s, offs_sb[:], WIDE)
         for s in range(PASSES):
             gather_words(a_words[s][:], s, offs2_sb[:])
+        load_planes(ws_sb[1][:], ws_rows[group[1]])
+        nc.sync.dma_start(gate_sb[:, N:], gate[:, N:])
         nc.sync.dma_start(wa_sb[:].bitcast(I32), wa_words.rearrange("f s p n -> p (f s) n").bitcast(I32))
         for q in range(QUADS):
             nc.sync.dma_start(
                 a_plane0[32 * q : 32 * q + ROWS, :].bitcast(I32), slot_rows[ROW0 + 16 + q : P : QUADS, 0:M].bitcast(I32)
             )
         load_planes(was_sb[:], wa_scales.rearrange("f s b n -> (f s) b n"))
-        nc.sync.dma_start(w_late[0][:].bitcast(I32), w_rows[:, 8:, 0 : 2 * N].bitcast(I32))
         nc.sync.dma_start(gate_rows[0:4, :], gate2[0].rearrange("(e p) -> e p", p=P))
-        load_ws(2)
-        nc.sync.dma_start(gate_sb[:, N:], gate[:, N:])
+        nc.sync.dma_start(w_right[:].bitcast(I32), w_rows[:, :, 2 * N :].bitcast(I32))
         nc.sync.dma_start(wb_sb[:].bitcast(I32), wb_words.rearrange("f s p n -> p (f s) n").bitcast(I32))
-        load_ws(3)
         load_planes(wbs_sb[:], wb_scales.rearrange("f s b n -> (f s) b n"))
-        nc.sync.dma_start(w_late[1][:].bitcast(I32), w_rows[:, 8:, 2 * N :].bitcast(I32))
 
         def w_tile(e, s, j):
-            if e >= 4:
-                return w_late[j // 2][:, PASSES * (e - 4) + s, 4 * P * (j % 2) : 4 * P * (j % 2 + 1)]
-            return w_early[e][:, s, 4 * P * j : 4 * P * (j + 1)]
+            cols = slice(4 * P * (j % 2), 4 * P * (j % 2 + 1))
+            if j >= 2:
+                return w_right[:, PASSES * e + s, cols]
+            return w_left[e // GROUP][:, PASSES * (e % GROUP) + s, cols]
 
         def experts(j, first, last, bank):
             for s in range(PASSES):
                 for e in range(first, last):
-                    a = PASSES * (e % 2) + s
                     nc.tensor.matmul_mx(
                         out=bank[:, (e - first) * C : (e - first + 1) * C],
                         lhsT=w_tile(e, s, j).bitcast(FP8X4),
-                        lhsT_scale=ws_sb[e // 2][ROWS * a : P, j * P : (j + 1) * P],
+                        lhsT_scale=ws_sb[e // GROUP][:, PASSES * (e % GROUP) + s, j * P : (j + 1) * P],
                         rhs=e_words[s][:, e * C : (e + 1) * C].bitcast(FP8X4),
                         rhs_scale=planes[ROWS * (1 - s) : P, M + e * C : M + (e + 1) * C],
                         start=(s == 0 and e == first),
@@ -224,61 +207,42 @@ def tile_moe_mlr_silu_kernel(
             )
             nc.scalar.activation(gated[u][:], sums[b][:], COPY, scale=gate_cols[:, u : u + 1])
 
-        def turn_back(j, banks):
-            blocks = M // P // len(banks)
-            for n, bank in enumerate(banks):
-                for c in range(blocks):
-                    u = n * blocks + c
-                    nc.tensor.transpose(bank[:, c * P : (c + 1) * P], gated[u][:, j * P : (j + 1) * P], ident[:])
-                nc.scalar.copy(z[j][:, n * blocks * P : (n + 1) * blocks * P], bank[:, 0 : blocks * P])
+        def turn_back(j, bank):
+            for u in range(M // P):
+                nc.tensor.transpose(bank[:, u * P : (u + 1) * P], gated[u][:, j * P : (j + 1) * P], ident[:])
+            nc.scalar.copy(z[j][:], bank[:])
             nc.vector.tensor_copy(z_sb[j][:].indirect(offs2_sb[:]), z[j][:])
 
-        early = [(0, 0, 2), (1, 0, 2), (2, 0, 4), (3, 0, 4), (0, 2, 4), (1, 2, 4)]
-        for n, (j, first, last) in enumerate(early):
-            experts(j, first, last, sums[n % BANKS])
-            scatter_y(j, first, last)
+        experts(0, 0, 2, sums[0])
+        experts(0, 2, 4, sums[1])
+        scatter_y(0, 0, GROUP)
+        experts(1, 0, GROUP, sums[2])
+        experts(1, GROUP, E, sums[0])
+        scatter_y(1, 0, E)
         nc.tensor.transpose(turned[BANKS - 1][:, 0:P], gate_rows[:], ident[:])
         nc.scalar.copy(gate_cols[:], turned[BANKS - 1][:, 0:16])
         for u in range(4):
-            adapter_in(u, (len(early) + u) % BANKS)
+            adapter_in(u, (1 + u) % BANKS)
         nc.vector.quantize_mx(out=h_codes[:].bitcast(FP8X4), scales=h_scales[:], in_=h_in[:])
-        for j, bank in enumerate([sums[1], sums[2], h_turned[1]]):
-            experts(j, 4, E, bank)
-            scatter_y(j, 4, E)
+        experts(0, GROUP, E, h_turned[1])
+        scatter_y(0, GROUP, E)
+        experts(2, 0, GROUP, sums[1])
+        experts(2, GROUP, E, h_turned[1])
+        scatter_y(2, 0, E)
         for u in range(4):
-            adapter_out(u, u % BANKS)
-        def add_by_turns(j, there, back):
-            for n, src in enumerate((o_sb[j], z_sb[j])):
-                for half in range(2):
-                    for c in range(N // P):
-                        nc.tensor.matmul(
-                            there[half][:, c * P : (c + 1) * P],
-                            src[:, half * N + c * P : half * N + (c + 1) * P],
-                            ident[:],
-                            start=(n == 0 and c == 0),
-                            stop=(n == 1 and c == N // P - 1),
-                            is_transpose=True,
-                        )
-            for half in range(2):
-                nc.scalar.copy(gated[half][:], there[half][:])
-            for half in range(2):
-                cols = slice(half * N, (half + 1) * N)
-                for c in range(N // P):
-                    nc.tensor.transpose(back[half][:, c * P : (c + 1) * P], gated[half][:, c * P : (c + 1) * P], ident[:])
-                nc.scalar.copy(y[j][:, cols], back[half][:])
-                nc.scalar.dma_start(out[j * P : (j + 1) * P, cols], y[j][:, cols])
-
+            adapter_out(u, (u + 2) % BANKS)
         for j in range(NT):
-            turn_back(j, [turned[j]] if j < BANKS else turned[0:2])
-            if j < 2:
-                nc.gpsimd.tensor_tensor(o_sb[j][:], o_sb[j][:], z_sb[j][:], ADD)
-                nc.sync.dma_start(out[j * P : (j + 1) * P, :], o_sb[j][:])
+            turn_back(j, turned[j % BANKS])
+            if j == 0:
+                experts(NT - 1, 0, GROUP, sums[0])
+                experts(NT - 1, GROUP, E, sums[1])
+                nc.gpsimd.tensor_tensor(y[NT - 2][:], y[NT - 1][:], gate_sb[:], MULT)
+            if j < NT - 1:
+                nc.gpsimd.tensor_tensor(z_sb[j][:], o_sb[j][:, 0:T], z_sb[j][:], ADD)
+                nc.sync.dma_start(out[j * P : (j + 1) * P, :], z_sb[j][:])
         j = NT - 1
-        experts(j, 4, 6, turned[0])
-        experts(j, 6, E, turned[1])
-        scatter_y(j, 4, E)
-        add_by_turns(2, [turned[0], turned[1]], [turned[2], sums[1]])
+        nc.vector.tensor_copy(o_sb[j][:].indirect(offs_sb[:]), y[NT - 2][:])
         edges = [0, 256, 640, T]
         for lo, hi in zip(edges[:-1], edges[1:]):
-            nc.vector.tensor_tensor(o_sb[j][:, lo:hi], o_sb[j][:, lo:hi], z_sb[j][:, lo:hi], ADD)
-            nc.sync.dma_start(out[j * P : (j + 1) * P, lo:hi], o_sb[j][:, lo:hi])
+            nc.vector.tensor_tensor(z_sb[j][:, lo:hi], o_sb[j][:, lo:hi], z_sb[j][:, lo:hi], ADD)
+            nc.sync.dma_start(out[j * P : (j + 1) * P, lo:hi], z_sb[j][:, lo:hi])

@@ -29,6 +29,7 @@ BANKS = 3
 WIDE = 1376
 ROW0 = 96
 GROUP = E // 2
+LATE_WINDOW = 1536
 
 
 def tile_moe_mlr_silu_kernel(
@@ -48,9 +49,9 @@ def tile_moe_mlr_silu_kernel(
         a_plane0 = keep.tile([P, M], U8, name="a_plane0", align_bytes=64)
         e_words = [keep.tile([P, T], U32, name="e_words%d" % s, align_bytes=64) for s in range(PASSES)]
         a_words = [keep.tile([P, M], U32, name="a_words%d" % s, align_bytes=64) for s in range(PASSES)]
-        w_left = [keep.tile([P, GROUP * PASSES, 2 * N], U8, name="w_left%d" % g, align_bytes=64) for g in range(2)]
-        w_right = keep.tile([P, E * PASSES, 2 * N], U8, name="w_right", align_bytes=64)
-        ws_sb = [keep.tile([P, GROUP * PASSES, N], U8, name="ws_sb%d" % g, align_bytes=64) for g in range(2)]
+        w_early = [keep.tile([P, PASSES, 4 * N], U8, name="w_early%d" % e, align_bytes=64) for e in range(GROUP)]
+        w_late = [keep.tile([P, GROUP * PASSES, 2 * N], U8, name="w_late%d" % g, align_bytes=64) for g in range(2)]
+        ws_sb = [keep.tile([P, N], U8, name="ws_sb%d" % g, align_bytes=64) for g in range(E // 2)]
         wa_sb = keep.tile([P, F * PASSES, 2 * H], U8, name="wa_sb", align_bytes=64)
         was_sb = keep.tile([P, F * PASSES, H], U8, name="was_sb", align_bytes=64)
         wb_sb = keep.tile([P, F, 2 * N], U8, name="wb_sb", align_bytes=64)
@@ -60,7 +61,7 @@ def tile_moe_mlr_silu_kernel(
         gate_sb = keep.tile([P, T], F32, name="gate_sb")
         zero_col = keep.tile([P, 1], F32, name="zero_col")
         ident = keep.tile([P, P], F32, name="ident")
-        o_sb = [keep.tile([P, WIDE if j else T], F32, name="o_sb%d" % j) for j in range(NT)]
+        o_sb = [keep.tile([P, LATE_WINDOW if j < 2 else T], F32, name="o_sb%d" % j) for j in range(NT)]
         z_sb = [keep.tile([P, T], F32, name="z_sb%d" % j) for j in range(NT)]
         y = [keep.tile([P, T], F32, name="y%d" % j) for j in range(NT)]
         z = [keep.tile([P, M], F32, name="z%d" % j) for j in range(NT)]
@@ -76,11 +77,13 @@ def tile_moe_mlr_silu_kernel(
         def zero(tile_ap):
             nc.gpsimd.memset(tile_ap.bitcast(I32), 0)
 
-        zero(ws_sb[0][:].rearrange("p a n -> p (a n)"))
+        zero(ws_sb[0][:])
         nc.vector.memset(xs_rows[0:ROW0, 0 : T + 4].bitcast(I32), 0)
+        zero(ws_sb[1][:])
         nc.gpsimd.memset(zero_col[:], 0.0)
         zero(planes[:])
-        zero(ws_sb[1][:].rearrange("p a n -> p (a n)"))
+        zero(ws_sb[2][:])
+        zero(ws_sb[3][:])
         zero(a_plane0[:])
         zero(was_sb[:].rearrange("p a n -> p (a n)"))
         nc.gpsimd.memset(gate_rows[:], 0.0)
@@ -90,13 +93,29 @@ def tile_moe_mlr_silu_kernel(
             nc.scalar.activation(z_sb[j][:], zero_col[:].to_broadcast([P, T]), SILU)
 
         def load_planes(dst, src):
-            rows = src.rearrange("a (q r) n -> r q a n", r=ROWS)
-            for r in range(ROWS):
-                nc.sync.dma_start(dst[r:P:32, :, :].bitcast(I32), rows[r].bitcast(I32))
+            for q in range(QUADS):
+                nc.sync.dma_start(
+                    dst[32 * q : 32 * q + ROWS, :, :].bitcast(I32),
+                    src[:, ROWS * q : ROWS * (q + 1), :].rearrange("a r n -> r a n").bitcast(I32),
+                )
 
         w_rows = w_words.rearrange("e s p n d -> p (e s) (n d)")
         ws_rows = w_scales.rearrange("e s b n -> (e s) b n")
-        group = [slice(g * GROUP * PASSES, (g + 1) * GROUP * PASSES) for g in range(2)]
+
+        def load_ws(g):
+            for q in range(QUADS):
+                nc.sync.dma_start(
+                    ws_sb[g][32 * q : 32 * q + 4 * ROWS, :].bitcast(I32),
+                    ws_rows[4 * g : 4 * (g + 1), ROWS * q : ROWS * (q + 1), :].bitcast(I32),
+                )
+
+        def load_early(e):
+            nc.sync.dma_start(w_early[e][:].bitcast(I32), w_rows[:, PASSES * e : PASSES * (e + 1), :].bitcast(I32))
+
+        def load_late(g):
+            nc.sync.dma_start(
+                w_late[g][:].bitcast(I32), w_rows[:, GROUP * PASSES :, 2 * N * g : 2 * N * (g + 1)].bitcast(I32)
+            )
 
         nc.sync.dma_start(offs2_sb[:], offs2)
         for s in range(PASSES):
@@ -113,8 +132,10 @@ def tile_moe_mlr_silu_kernel(
         def gather_words(dst, s, offsets, window=T):
             nc.vector.tensor_copy(dst, x_sb[:, s * T : s * T + window].bitcast(U32).indirect(offsets))
 
-        load_planes(ws_sb[0][:], ws_rows[group[0]])
-        nc.sync.dma_start(w_left[0][:].bitcast(I32), w_rows[:, group[0], 0 : 2 * N].bitcast(I32))
+        load_early(0)
+        load_ws(0)
+        load_early(1)
+        load_ws(1)
         nc.vector.tensor_copy(slot_rows[:, 0:M], xs_rows[:, 0:T].indirect(offs2_sb[:]))
         nc.vector.tensor_copy(slot_rows[:, M:], xs_rows[:].indirect(offs_sb[:]))
         for q in range(QUADS):
@@ -122,12 +143,15 @@ def tile_moe_mlr_silu_kernel(
                 planes[32 * q : 32 * q + 2 * ROWS, :].bitcast(I32), slot_rows[ROW0 + q : P : QUADS, :].bitcast(I32)
             )
         nc.sync.dma_start(gate_sb[:, 0:N], gate[:, 0:N])
-        nc.sync.dma_start(w_left[1][:].bitcast(I32), w_rows[:, group[1], 0 : 2 * N].bitcast(I32))
+        load_early(2)
+        load_early(3)
         for s in range(PASSES):
             gather_words(e_words[s][:], s, offs_sb[:], WIDE)
         for s in range(PASSES):
             gather_words(a_words[s][:], s, offs2_sb[:])
-        load_planes(ws_sb[1][:], ws_rows[group[1]])
+        load_late(0)
+        load_ws(2)
+        load_ws(3)
         nc.sync.dma_start(gate_sb[:, N:], gate[:, N:])
         nc.sync.dma_start(wa_sb[:].bitcast(I32), wa_words.rearrange("f s p n -> p (f s) n").bitcast(I32))
         for q in range(QUADS):
@@ -136,15 +160,14 @@ def tile_moe_mlr_silu_kernel(
             )
         load_planes(was_sb[:], wa_scales.rearrange("f s b n -> (f s) b n"))
         nc.sync.dma_start(gate_rows[0:4, :], gate2[0].rearrange("(e p) -> e p", p=P))
-        nc.sync.dma_start(w_right[:].bitcast(I32), w_rows[:, :, 2 * N :].bitcast(I32))
+        load_late(1)
         nc.sync.dma_start(wb_sb[:].bitcast(I32), wb_words.rearrange("f s p n -> p (f s) n").bitcast(I32))
         load_planes(wbs_sb[:], wb_scales.rearrange("f s b n -> (f s) b n"))
 
         def w_tile(e, s, j):
-            cols = slice(4 * P * (j % 2), 4 * P * (j % 2 + 1))
-            if j >= 2:
-                return w_right[:, PASSES * e + s, cols]
-            return w_left[e // GROUP][:, PASSES * (e % GROUP) + s, cols]
+            if e >= GROUP:
+                return w_late[j // 2][:, PASSES * (e - GROUP) + s, 4 * P * (j % 2) : 4 * P * (j % 2 + 1)]
+            return w_early[e][:, s, 4 * P * j : 4 * P * (j + 1)]
 
         def experts(j, first, last, bank):
             for s in range(PASSES):
@@ -152,7 +175,7 @@ def tile_moe_mlr_silu_kernel(
                     nc.tensor.matmul_mx(
                         out=bank[:, (e - first) * C : (e - first + 1) * C],
                         lhsT=w_tile(e, s, j).bitcast(FP8X4),
-                        lhsT_scale=ws_sb[e // GROUP][:, PASSES * (e % GROUP) + s, j * P : (j + 1) * P],
+                        lhsT_scale=ws_sb[e // 2][ROWS * (PASSES * (e % 2) + s) : P, j * P : (j + 1) * P],
                         rhs=e_words[s][:, e * C : (e + 1) * C].bitcast(FP8X4),
                         rhs_scale=planes[ROWS * (1 - s) : P, M + e * C : M + (e + 1) * C],
                         start=(s == 0 and e == first),
@@ -213,35 +236,30 @@ def tile_moe_mlr_silu_kernel(
             nc.scalar.copy(z[j][:], bank[:])
             nc.vector.tensor_copy(z_sb[j][:].indirect(offs2_sb[:]), z[j][:])
 
-        experts(0, 0, 2, sums[0])
-        experts(0, 2, 4, sums[1])
-        scatter_y(0, 0, GROUP)
-        experts(1, 0, GROUP, sums[2])
-        experts(1, GROUP, E, sums[0])
-        scatter_y(1, 0, E)
+        early = [(0, 0, 2), (1, 0, 2), (2, 0, GROUP), (3, 0, GROUP)]
+        for n, (j, first, last) in enumerate(early):
+            experts(j, first, last, sums[n % BANKS])
+            scatter_y(j, first, last)
+        for j in range(2):
+            experts(j, 2, GROUP, turned[j])
+            experts(j, GROUP, E, sums[1 + j])
+            scatter_y(j, 2, E)
         nc.tensor.transpose(turned[BANKS - 1][:, 0:P], gate_rows[:], ident[:])
         nc.scalar.copy(gate_cols[:], turned[BANKS - 1][:, 0:16])
         for u in range(4):
-            adapter_in(u, (1 + u) % BANKS)
+            adapter_in(u, u % BANKS)
         nc.vector.quantize_mx(out=h_codes[:].bitcast(FP8X4), scales=h_scales[:], in_=h_in[:])
-        experts(0, GROUP, E, h_turned[1])
-        scatter_y(0, GROUP, E)
-        experts(2, 0, GROUP, sums[1])
-        experts(2, GROUP, E, h_turned[1])
-        scatter_y(2, 0, E)
+        for j in range(2, NT):
+            experts(j, GROUP, E, h_turned[1])
+            scatter_y(j, GROUP, E)
         for u in range(4):
-            adapter_out(u, (u + 2) % BANKS)
+            adapter_out(u, (u + 1) % BANKS)
         for j in range(NT):
             turn_back(j, turned[j % BANKS])
-            if j == 0:
-                experts(NT - 1, 0, GROUP, sums[0])
-                experts(NT - 1, GROUP, E, sums[1])
-                nc.gpsimd.tensor_tensor(y[NT - 2][:], y[NT - 1][:], gate_sb[:], MULT)
             if j < NT - 1:
                 nc.gpsimd.tensor_tensor(z_sb[j][:], o_sb[j][:, 0:T], z_sb[j][:], ADD)
                 nc.sync.dma_start(out[j * P : (j + 1) * P, :], z_sb[j][:])
         j = NT - 1
-        nc.vector.tensor_copy(o_sb[j][:].indirect(offs_sb[:]), y[NT - 2][:])
         edges = [0, 256, 640, T]
         for lo, hi in zip(edges[:-1], edges[1:]):
             nc.vector.tensor_tensor(z_sb[j][:, lo:hi], o_sb[j][:, lo:hi], z_sb[j][:, lo:hi], ADD)

@@ -42,11 +42,10 @@ def tile_moe_mlr_silu_kernel(
 
         offs_sb = keep.tile([P, T // 16], U16, name="offs_sb")
         offs2_sb = keep.tile([P, M // 16], U16, name="offs2_sb")
-        x_sb = keep.tile([P, T + WIDE], I32, name="x_sb", align_bytes=64)
+        x_sb = keep.tile([P, PASSES * WIDE], I32, name="x_sb", align_bytes=64)
         xs_rows = keep.tile([P, WIDE], U8, name="xs_rows", align_bytes=64)
         slot_rows = keep.tile([P, M + T], U8, name="slot_rows", align_bytes=64)
-        planes = keep.tile([P, M + T], U8, name="planes", align_bytes=64)
-        a_plane0 = keep.tile([P, M], U8, name="a_plane0", align_bytes=64)
+        planes = [keep.tile([P, M + T], U8, name="planes%d" % s, align_bytes=64) for s in range(PASSES)]
         e_words = [keep.tile([P, T], U32, name="e_words%d" % s, align_bytes=64) for s in range(PASSES)]
         a_words = [keep.tile([P, M], U32, name="a_words%d" % s, align_bytes=64) for s in range(PASSES)]
         w_early = [keep.tile([P, PASSES, 4 * N], U8, name="w_early%d" % e, align_bytes=64) for e in range(GROUP)]
@@ -79,12 +78,11 @@ def tile_moe_mlr_silu_kernel(
 
         zero(ws_sb[0][:])
         nc.vector.memset(xs_rows[0:ROW0, 0 : T + 4].bitcast(I32), 0)
-        zero(ws_sb[1][:])
         nc.gpsimd.memset(zero_col[:], 0.0)
-        zero(planes[:])
-        zero(ws_sb[2][:])
-        zero(ws_sb[3][:])
-        zero(a_plane0[:])
+        for s in range(PASSES):
+            zero(planes[s][:])
+        for g in range(1, E // 2):
+            zero(ws_sb[g][:])
         zero(was_sb[:].rearrange("p a n -> p (a n)"))
         nc.gpsimd.memset(gate_rows[:], 0.0)
         make_identity(nc, ident[:])
@@ -118,46 +116,38 @@ def tile_moe_mlr_silu_kernel(
             )
 
         nc.sync.dma_start(offs2_sb[:], offs2)
-        for s in range(PASSES):
-            nc.sync.dma_start(
-                xs_rows[ROW0 + 16 * (1 - s) : ROW0 + 16 * (2 - s), 0:T].bitcast(I32),
-                x_scales[s].rearrange("(q r) t -> r q t", r=ROWS).bitcast(I32),
-            )
+        nc.sync.dma_start(xs_rows[ROW0:P, 0:T].bitcast(I32), x_scales.rearrange("s b t -> (s b) t").bitcast(I32))
         nc.sync.dma_start(offs_sb[:], offs)
-        nc.sync.dma_start(
-            x_sb[:, 0 : PASSES * T].rearrange("p (s t) -> p s t", s=PASSES),
-            x_words.rearrange("s p t d -> p s (t d)").bitcast(I32),
-        )
+        for s in range(PASSES):
+            nc.sync.dma_start(x_sb[:, s * WIDE : s * WIDE + T], x_words[s].rearrange("p t d -> p (t d)").bitcast(I32))
 
-        def gather_words(dst, s, offsets, window=T):
-            nc.vector.tensor_copy(dst, x_sb[:, s * T : s * T + window].bitcast(U32).indirect(offsets))
+        def gather_words(dst, s, offsets, window):
+            nc.vector.tensor_copy(dst, x_sb[:, s * WIDE : s * WIDE + window].bitcast(U32).indirect(offsets))
 
         load_early(0)
         load_ws(0)
         load_early(1)
-        load_ws(1)
+        nc.sync.dma_start(gate_sb[:, 0:N], gate[:, 0:N])
         nc.vector.tensor_copy(slot_rows[:, 0:M], xs_rows[:, 0:T].indirect(offs2_sb[:]))
         nc.vector.tensor_copy(slot_rows[:, M:], xs_rows[:].indirect(offs_sb[:]))
-        for q in range(QUADS):
-            nc.sync.dma_start(
-                planes[32 * q : 32 * q + 2 * ROWS, :].bitcast(I32), slot_rows[ROW0 + q : P : QUADS, :].bitcast(I32)
-            )
-        nc.sync.dma_start(gate_sb[:, 0:N], gate[:, 0:N])
+        for s in range(PASSES):
+            for q in range(QUADS):
+                row = ROW0 + 16 * s + ROWS * q
+                nc.sync.dma_start(
+                    planes[s][32 * q : 32 * q + ROWS, :].bitcast(I32), slot_rows[row : row + ROWS, :].bitcast(I32)
+                )
         load_early(2)
         load_early(3)
+        load_ws(1)
         for s in range(PASSES):
             gather_words(e_words[s][:], s, offs_sb[:], WIDE)
         for s in range(PASSES):
-            gather_words(a_words[s][:], s, offs2_sb[:])
+            gather_words(a_words[s][:], s, offs2_sb[:], T if s else WIDE + 32)
         load_late(0)
         load_ws(2)
         load_ws(3)
         nc.sync.dma_start(gate_sb[:, N:], gate[:, N:])
         nc.sync.dma_start(wa_sb[:].bitcast(I32), wa_words.rearrange("f s p n -> p (f s) n").bitcast(I32))
-        for q in range(QUADS):
-            nc.sync.dma_start(
-                a_plane0[32 * q : 32 * q + ROWS, :].bitcast(I32), slot_rows[ROW0 + 16 + q : P : QUADS, 0:M].bitcast(I32)
-            )
         load_planes(was_sb[:], wa_scales.rearrange("f s b n -> (f s) b n"))
         nc.sync.dma_start(gate_rows[0:4, :], gate2[0].rearrange("(e p) -> e p", p=P))
         load_late(1)
@@ -177,7 +167,7 @@ def tile_moe_mlr_silu_kernel(
                         lhsT=w_tile(e, s, j).bitcast(FP8X4),
                         lhsT_scale=ws_sb[e // 2][ROWS * (PASSES * (e % 2) + s) : P, j * P : (j + 1) * P],
                         rhs=e_words[s][:, e * C : (e + 1) * C].bitcast(FP8X4),
-                        rhs_scale=planes[ROWS * (1 - s) : P, M + e * C : M + (e + 1) * C],
+                        rhs_scale=planes[s][:, M + e * C : M + (e + 1) * C],
                         start=(s == 0 and e == first),
                         stop=(s == PASSES - 1 and e == last - 1),
                     )
@@ -197,7 +187,7 @@ def tile_moe_mlr_silu_kernel(
                 nc.tensor.matmul_mx(
                     out=sums[b][:],
                     lhsT=a_words[s][:, cols].bitcast(FP8X4),
-                    lhsT_scale=(planes if s else a_plane0)[:, cols],
+                    lhsT_scale=planes[s][:, cols],
                     rhs=wa_sb[:, f * PASSES + s, :].bitcast(FP4X4),
                     rhs_scale=was_sb[:, f * PASSES + s, :],
                     start=(s == 0),

@@ -250,7 +250,7 @@ def tile_moe_mlr_silu_kernel(
                 nc.gpsimd.tensor_tensor(z_sb[j][:], o_sb[j][:, 0:T], z_sb[j][:], ADD)
                 nc.sync.dma_start(out[j * P : (j + 1) * P, :], z_sb[j][:])
         j = NT - 1
-        edges = [0, 256, 640, T]
+        edges = [0, N, T]
         for lo, hi in zip(edges[:-1], edges[1:]):
             nc.vector.tensor_tensor(z_sb[j][:, lo:hi], o_sb[j][:, lo:hi], z_sb[j][:, lo:hi], ADD)
             nc.sync.dma_start(out[j * P : (j + 1) * P, lo:hi], z_sb[j][:, lo:hi])

@@ -250,7 +250,7 @@ def tile_moe_mlr_silu_kernel(
                 nc.gpsimd.tensor_tensor(z_sb[j][:], o_sb[j][:, 0:T], z_sb[j][:], ADD)
                 nc.sync.dma_start(out[j * P : (j + 1) * P, :], z_sb[j][:])
         j = NT - 1
-        edges = [0, N, T]
+        edges = [0, 256, 512, 768, T]
         for lo, hi in zip(edges[:-1], edges[1:]):
             nc.vector.tensor_tensor(z_sb[j][:, lo:hi], o_sb[j][:, lo:hi], z_sb[j][:, lo:hi], ADD)
             nc.sync.dma_start(out[j * P : (j + 1) * P, lo:hi], z_sb[j][:, lo:hi])

@@ -25,11 +25,9 @@ QUADS = 4
 ROWS = 4
 M = F * D
 NT = N // P
-BANKS = 3
-WIDE = 1376
-ROW0 = 96
-GROUP = E // 2
-LATE_WINDOW = 1536
+EARLY = 2 * C
+LATE = T - EARLY
+SHARE = 448
 
 
 def tile_moe_mlr_silu_kernel(
@@ -38,156 +36,157 @@ def tile_moe_mlr_silu_kernel(
     nc = tc.nc
     with ExitStack() as ctx:
         keep = ctx.enter_context(tc.tile_pool(name="keep", bufs=1))
+        reuse = ctx.enter_context(tc.tile_pool(name="reuse", bufs=1))
         psum = ctx.enter_context(tc.psum_pool(name="psum", bufs=1))
 
         offs_sb = keep.tile([P, T // 16], U16, name="offs_sb")
         offs2_sb = keep.tile([P, M // 16], U16, name="offs2_sb")
-        x_sb = keep.tile([P, PASSES * WIDE], I32, name="x_sb", align_bytes=64)
-        xs_rows = keep.tile([P, WIDE], U8, name="xs_rows", align_bytes=64)
-        slot_rows = keep.tile([P, M + T], U8, name="slot_rows", align_bytes=64)
-        planes = [keep.tile([P, M + T], U8, name="planes%d" % s, align_bytes=64) for s in range(PASSES)]
-        e_words = [keep.tile([P, T], U32, name="e_words%d" % s, align_bytes=64) for s in range(PASSES)]
-        a_words = [keep.tile([P, M], U32, name="a_words%d" % s, align_bytes=64) for s in range(PASSES)]
-        w_early = [keep.tile([P, PASSES, 4 * N], U8, name="w_early%d" % e, align_bytes=64) for e in range(GROUP)]
-        w_late = [keep.tile([P, GROUP * PASSES, 2 * N], U8, name="w_late%d" % g, align_bytes=64) for g in range(2)]
-        ws_sb = [keep.tile([P, N], U8, name="ws_sb%d" % g, align_bytes=64) for g in range(E // 2)]
+        x_sb = keep.tile([P, PASSES * T], I32, name="x_sb", align_bytes=64)
+        xs_sb = keep.tile([P, T], U8, name="xs_sb", align_bytes=64)
+        early_words = [keep.tile([P, EARLY], U32, name="early_words%d" % s, align_bytes=64) for s in range(PASSES)]
+        early_planes = keep.tile([P, EARLY], U8, name="early_planes", align_bytes=64)
+        a_words0 = keep.tile([P, M], U32, name="a_words0", align_bytes=64)
+        a_planes = keep.tile([P, M], U8, name="a_planes", align_bytes=64)
+        a_plane1 = keep.tile([P, M], U8, name="a_plane1", align_bytes=64)
+
+        w0_at = 4 * M - 64
+        w0_sb = reuse.tile([P, PASSES, 4 * N], U8, name="w0_sb", align_bytes=64, offset=w0_at)
+        a_words1 = reuse.tile([P, M], U32, name="a_words1", align_bytes=64, offset=0)
+        late_planes = reuse.tile([P, LATE], U8, name="late_planes", align_bytes=64, offset=4 * M)
+        late_words = [
+            reuse.tile([P, LATE], U32, name="late_words%d" % s, align_bytes=64, offset=4 * M + LATE + 4 * LATE * s)
+            for s in range(PASSES)
+        ]
+        a_words = [a_words0, a_words1]
+
+        w1_sb = keep.tile([P, PASSES, 4 * N], U8, name="w1_sb", align_bytes=64)
+        w_pairs = [keep.tile([P, 2 * PASSES, 4 * N], U8, name="w_pair%d" % g, align_bytes=64) for g in range(1, E // 2)]
+        ws0_sb = keep.tile([P, N], U8, name="ws0_sb", align_bytes=64)
+        ws_sb = keep.tile([P, E - 1, N], U8, name="ws_sb", align_bytes=64)
         wa_sb = keep.tile([P, F * PASSES, 2 * H], U8, name="wa_sb", align_bytes=64)
         was_sb = keep.tile([P, F * PASSES, H], U8, name="was_sb", align_bytes=64)
         wb_sb = keep.tile([P, F, 2 * N], U8, name="wb_sb", align_bytes=64)
         wbs_sb = keep.tile([P, F, N], U8, name="wbs_sb", align_bytes=64)
-        gate_rows = keep.tile([P, P], F32, name="gate_rows")
-        gate_cols = keep.tile([P, 16], F32, name="gate_cols")
-        gate_sb = keep.tile([P, T], F32, name="gate_sb")
+        gate0_sb = keep.tile([P, C], F32, name="gate0_sb")
+        gate_sb = keep.tile([P, T - C], F32, name="gate_sb")
+        gate2_sb = keep.tile([P, M], F32, name="gate2_sb")
         zero_col = keep.tile([P, 1], F32, name="zero_col")
         ident = keep.tile([P, P], F32, name="ident")
-        o_sb = [keep.tile([P, LATE_WINDOW if j < 2 else T], F32, name="o_sb%d" % j) for j in range(NT)]
+        o_sb = [keep.tile([P, T], F32, name="o_sb%d" % j) for j in range(NT)]
         z_sb = [keep.tile([P, T], F32, name="z_sb%d" % j) for j in range(NT)]
-        y = [keep.tile([P, T], F32, name="y%d" % j) for j in range(NT)]
+        y = keep.tile([P, NT, T], F32, name="y")
         z = [keep.tile([P, M], F32, name="z%d" % j) for j in range(NT)]
-        gated = [keep.tile([P, N], F32, name="gated%d" % u) for u in range(M // P)]
         h_rows = [keep.tile([P, H], BF16, name="h_rows%d" % b) for b in range(2)]
         h_in = keep.tile([P, 4 * M], BF16, name="h_in", align_bytes=64)
         h_codes = keep.tile([P, M], U32, name="h_codes", align_bytes=64)
         h_scales = keep.tile([P, M], U8, name="h_scales", align_bytes=64)
-        sums = [psum.tile([P, N], F32, name="sums%d" % b) for b in range(BANKS)]
-        turned = [psum.tile([P, N], F32, name="turned%d" % b) for b in range(BANKS)]
-        h_turned = [psum.tile([P, N], F32, name="h_turned%d" % b) for b in range(2)]
+        banks = [psum.tile([P, N], F32, name="bank%d" % b) for b in range(8)]
 
         def zero(tile_ap):
             nc.gpsimd.memset(tile_ap.bitcast(I32), 0)
 
-        zero(ws_sb[0][:])
-        nc.vector.memset(xs_rows[0:ROW0, 0 : T + 4].bitcast(I32), 0)
+        nc.vector.memset(xs_sb[:].bitcast(I32), 0)
+        zero(ws0_sb[:])
         nc.gpsimd.memset(zero_col[:], 0.0)
-        for s in range(PASSES):
-            zero(planes[s][:])
-        for g in range(1, E // 2):
-            zero(ws_sb[g][:])
         zero(was_sb[:].rearrange("p a n -> p (a n)"))
-        nc.gpsimd.memset(gate_rows[:], 0.0)
+        zero(a_plane1[:])
+        zero(ws_sb[:].rearrange("p a n -> p (a n)"))
         make_identity(nc, ident[:])
         zero(wbs_sb[:].rearrange("p a n -> p (a n)"))
-        for j in range(NT):
+        for j in range(NT - 1):
             nc.scalar.activation(z_sb[j][:], zero_col[:].to_broadcast([P, T]), SILU)
+        nc.gpsimd.memset(z_sb[NT - 1][:], 0.0)
 
-        def load_planes(dst, src):
+        def load(dst, src):
+            nc.sync.dma_start(dst.bitcast(I32), src.bitcast(I32))
+
+        def load_planes(dst, src, start):
             for q in range(QUADS):
-                nc.sync.dma_start(
-                    dst[32 * q : 32 * q + ROWS, :, :].bitcast(I32),
-                    src[:, ROWS * q : ROWS * (q + 1), :].rearrange("a r n -> r a n").bitcast(I32),
-                )
+                row = 32 * q + start
+                load(dst[row : row + ROWS, :, :], src[:, ROWS * q : ROWS * (q + 1), :].rearrange("a r n -> r a n"))
+
+        def load_both_passes(dst, src):
+            for q in range(QUADS):
+                load(dst[32 * q : 32 * q + PASSES * ROWS, :], src[:, ROWS * q : ROWS * (q + 1), :])
 
         w_rows = w_words.rearrange("e s p n d -> p (e s) (n d)")
-        ws_rows = w_scales.rearrange("e s b n -> (e s) b n")
 
-        def load_ws(g):
-            for q in range(QUADS):
-                nc.sync.dma_start(
-                    ws_sb[g][32 * q : 32 * q + 4 * ROWS, :].bitcast(I32),
-                    ws_rows[4 * g : 4 * (g + 1), ROWS * q : ROWS * (q + 1), :].bitcast(I32),
-                )
-
-        def load_early(e):
-            nc.sync.dma_start(w_early[e][:].bitcast(I32), w_rows[:, PASSES * e : PASSES * (e + 1), :].bitcast(I32))
-
-        def load_late(g):
-            nc.sync.dma_start(
-                w_late[g][:].bitcast(I32), w_rows[:, GROUP * PASSES :, 2 * N * g : 2 * N * (g + 1)].bitcast(I32)
-            )
-
-        nc.sync.dma_start(offs2_sb[:], offs2)
-        nc.sync.dma_start(xs_rows[ROW0:P, 0:T].bitcast(I32), x_scales.rearrange("s b t -> (s b) t").bitcast(I32))
         nc.sync.dma_start(offs_sb[:], offs)
-        for s in range(PASSES):
-            nc.sync.dma_start(x_sb[:, s * WIDE : s * WIDE + T], x_words[s].rearrange("p t d -> p (t d)").bitcast(I32))
+        nc.sync.dma_start(offs2_sb[:], offs2)
+        load_both_passes(xs_sb, x_scales)
+        load(x_sb[:].rearrange("p (s t) -> p s t", s=PASSES), x_words.rearrange("s p t d -> p s (t d)"))
+        load(w0_sb[:], w_rows[:, 0:PASSES, :])
+        load_both_passes(ws0_sb, w_scales[0])
+        nc.sync.dma_start(gate0_sb[:], gate[:, 0:C])
 
-        def gather_words(dst, s, offsets, window):
-            nc.vector.tensor_copy(dst, x_sb[:, s * WIDE : s * WIDE + window].bitcast(U32).indirect(offsets))
+        def slots(lo, hi):
+            return offs_sb[:, lo // 16 : hi // 16]
 
-        load_early(0)
-        load_ws(0)
-        load_early(1)
-        nc.sync.dma_start(gate_sb[:, 0:N], gate[:, 0:N])
-        nc.vector.tensor_copy(slot_rows[:, 0:M], xs_rows[:, 0:T].indirect(offs2_sb[:]))
-        nc.vector.tensor_copy(slot_rows[:, M:], xs_rows[:].indirect(offs_sb[:]))
-        for s in range(PASSES):
-            for q in range(QUADS):
-                row = ROW0 + 16 * s + ROWS * q
-                nc.sync.dma_start(
-                    planes[s][32 * q : 32 * q + ROWS, :].bitcast(I32), slot_rows[row : row + ROWS, :].bitcast(I32)
-                )
-        load_early(2)
-        load_early(3)
-        load_ws(1)
-        for s in range(PASSES):
-            gather_words(e_words[s][:], s, offs_sb[:], WIDE)
-        for s in range(PASSES):
-            gather_words(a_words[s][:], s, offs2_sb[:], T if s else WIDE + 32)
-        load_late(0)
-        load_ws(2)
-        load_ws(3)
-        nc.sync.dma_start(gate_sb[:, N:], gate[:, N:])
-        nc.sync.dma_start(wa_sb[:].bitcast(I32), wa_words.rearrange("f s p n -> p (f s) n").bitcast(I32))
-        load_planes(was_sb[:], wa_scales.rearrange("f s b n -> (f s) b n"))
-        nc.sync.dma_start(gate_rows[0:4, :], gate2[0].rearrange("(e p) -> e p", p=P))
-        load_late(1)
-        nc.sync.dma_start(wb_sb[:].bitcast(I32), wb_words.rearrange("f s p n -> p (f s) n").bitcast(I32))
-        load_planes(wbs_sb[:], wb_scales.rearrange("f s b n -> (f s) b n"))
+        def gather_words(dst, s, offsets):
+            nc.vector.tensor_copy(dst, x_sb[:, s * T : (s + 1) * T].bitcast(U32).indirect(offsets))
 
-        def w_tile(e, s, j):
-            if e >= GROUP:
-                return w_late[j // 2][:, PASSES * (e - GROUP) + s, 4 * P * (j % 2) : 4 * P * (j % 2 + 1)]
-            return w_early[e][:, s, 4 * P * j : 4 * P * (j + 1)]
+        def gather_bytes(dst, offsets):
+            nc.vector.tensor_copy(dst, xs_sb[:].indirect(offsets))
 
-        def experts(j, first, last, bank):
-            for s in range(PASSES):
-                for e in range(first, last):
+        gather_bytes(early_planes[:], slots(0, EARLY))
+        gather_words(early_words[0][:], 0, slots(0, EARLY))
+        gather_bytes(a_planes[:], offs2_sb[:])
+        gather_words(early_words[1][:], 1, slots(0, EARLY))
+        gather_words(a_words[0][:], 0, offs2_sb[:])
+
+        load(wa_sb[:], wa_words.rearrange("f s p n -> p (f s) n"))
+        load_planes(was_sb[:], wa_scales.rearrange("f s b n -> (f s) b n"), 0)
+        load(w1_sb[:], w_rows[:, PASSES : 2 * PASSES, :])
+        for q in range(QUADS):
+            load(a_plane1[32 * q : 32 * q + ROWS, :], a_planes[32 * q + ROWS : 32 * q + 2 * ROWS, :])
+        load(w_pairs[0][:], w_rows[:, 2 * PASSES : 4 * PASSES, :])
+        load_planes(ws_sb[:], w_scales[1:, 0], 0)
+        nc.sync.dma_start(gate_sb[:], gate[:, C:])
+        load_planes(ws_sb[:], w_scales[1:, 1], ROWS)
+        load(w_pairs[1][:], w_rows[:, 4 * PASSES : 6 * PASSES, :])
+        load(wb_sb[:], wb_words.rearrange("f s p n -> p (f s) n"))
+        nc.sync.dma_start(gate2_sb[:], gate2)
+        load_planes(wbs_sb[:], wb_scales.rearrange("f s b n -> (f s) b n"), 0)
+        load(w_pairs[2][:], w_rows[:, 6 * PASSES : 8 * PASSES, :])
+
+        def expert(e, bank, tiles=range(NT)):
+            if e < 2:
+                w_sb, words, planes, first = (w0_sb, w1_sb)[e][:], early_words, early_planes, e * C
+            else:
+                w_sb = w_pairs[e // 2 - 1][:, PASSES * (e % 2) : PASSES * (e % 2 + 1), :]
+                words, planes, first = late_words, late_planes, e * C - EARLY
+            for n, j in enumerate(tiles):
+                cols = slice(j * P, (j + 1) * P)
+                for s in range(PASSES):
                     nc.tensor.matmul_mx(
-                        out=bank[:, (e - first) * C : (e - first + 1) * C],
-                        lhsT=w_tile(e, s, j).bitcast(FP8X4),
-                        lhsT_scale=ws_sb[e // 2][ROWS * (PASSES * (e % 2) + s) : P, j * P : (j + 1) * P],
-                        rhs=e_words[s][:, e * C : (e + 1) * C].bitcast(FP8X4),
-                        rhs_scale=planes[s][:, M + e * C : M + (e + 1) * C],
-                        start=(s == 0 and e == first),
-                        stop=(s == PASSES - 1 and e == last - 1),
+                        out=bank[:, n * C : (n + 1) * C],
+                        lhsT=w_sb[:, s, 4 * P * j : 4 * P * (j + 1)].bitcast(FP8X4),
+                        lhsT_scale=ws0_sb[ROWS * s : P, cols] if e == 0 else ws_sb[ROWS * s : P, e - 1, cols],
+                        rhs=words[s][:, first : first + C].bitcast(FP8X4),
+                        rhs_scale=planes[ROWS * s : P, first : first + C],
+                        start=(s == 0),
+                        stop=(s == PASSES - 1),
                     )
-            cols = slice(first * C, last * C)
-            nc.scalar.copy(y[j][:, cols], bank[:, 0 : (last - first) * C])
-
-        def scatter_y(j, first, last):
-            cols = slice(first * C, last * C)
+            g = gate0_sb[:] if e == 0 else gate_sb[:, (e - 1) * C : e * C]
             nc.vector.tensor_tensor(
-                o_sb[j][:].indirect(offs_sb[:, first * C // 16 : last * C // 16]), y[j][:, cols], gate_sb[:, cols], MULT
+                y[:, tiles.start : tiles.stop, e * C : (e + 1) * C],
+                bank[:, 0 : len(tiles) * C].rearrange("p (j c) -> p j c", c=C),
+                g.unsqueeze(1).to_broadcast([P, len(tiles), C]),
+                MULT,
             )
 
-        def adapter_in(u, b):
+        def scatter_on_scalar(lo, hi):
+            for j in range(NT):
+                nc.scalar.activation(o_sb[j][:].indirect(slots(lo, hi)), y[:, j, lo:hi], COPY)
+
+        def adapter_in(u, sums, turned):
             f = u * P // D
             cols = slice(u * P, (u + 1) * P)
             for s in range(PASSES):
                 nc.tensor.matmul_mx(
-                    out=sums[b][:],
+                    out=sums[:],
                     lhsT=a_words[s][:, cols].bitcast(FP8X4),
-                    lhsT_scale=planes[s][:, cols],
+                    lhsT_scale=(a_planes, a_plane1)[s][:, cols],
                     rhs=wa_sb[:, f * PASSES + s, :].bitcast(FP4X4),
                     rhs_scale=was_sb[:, f * PASSES + s, :],
                     start=(s == 0),
@@ -195,62 +194,63 @@ def tile_moe_mlr_silu_kernel(
                 )
             nc.scalar.activation(
                 h_rows[u % 2][:].rearrange("m (v p e) -> m v p e", v=2, e=2),
-                sums[b][:].rearrange("m (p v e) -> m v p e", v=2, e=2),
+                sums[:].rearrange("m (p v e) -> m v p e", v=2, e=2),
                 SILU,
             )
             pairs = h_rows[u % 2][:].bitcast(F32)
             for v in range(2):
-                nc.tensor.transpose(h_turned[u % 2][:, v * P : (v + 1) * P], pairs[:, v * P : (v + 1) * P], ident[:])
+                nc.tensor.transpose(turned[:, v * P : (v + 1) * P], pairs[:, v * P : (v + 1) * P], ident[:])
             nc.scalar.copy(
                 h_in[:, 4 * u * P : 4 * (u + 1) * P].bitcast(F32).rearrange("p (m v) -> p m v", v=2),
-                h_turned[u % 2][:, 0 : 2 * P].rearrange("p (v m) -> p m v", v=2),
+                turned[:, 0 : 2 * P].rearrange("p (v m) -> p m v", v=2),
             )
 
-        def adapter_out(u, b):
-            f = u * P // D
-            cols = slice(u * P, (u + 1) * P)
-            nc.tensor.matmul_mx(
-                out=sums[b][:],
-                lhsT=h_codes[:, cols].bitcast(FP8X4),
-                lhsT_scale=h_scales[:, cols],
-                rhs=wb_sb[:, f, :].bitcast(FP4X4),
-                rhs_scale=wbs_sb[:, f, :],
-                start=True,
-                stop=True,
-            )
-            nc.scalar.activation(gated[u][:], sums[b][:], COPY, scale=gate_cols[:, u : u + 1])
+        def adapter_out(j, bank):
+            for f in range(F):
+                cols = slice(f * D, (f + 1) * D)
+                nc.tensor.matmul_mx(
+                    out=bank[:, cols],
+                    lhsT=wb_sb[:, f, 2 * P * j : 2 * P * (j + 1)].bitcast(FP4X4),
+                    lhsT_scale=wbs_sb[:, f, j * P : (j + 1) * P],
+                    rhs=h_codes[:, cols].bitcast(FP8X4),
+                    rhs_scale=h_scales[:, cols],
+                    start=True,
+                    stop=True,
+                )
+            nc.vector.tensor_tensor(z[j][:], bank[:], gate2_sb[:], MULT)
 
-        def turn_back(j, bank):
-            for u in range(M // P):
-                nc.tensor.transpose(bank[:, u * P : (u + 1) * P], gated[u][:, j * P : (j + 1) * P], ident[:])
-            nc.scalar.copy(z[j][:], bank[:])
-            nc.vector.tensor_copy(z_sb[j][:].indirect(offs2_sb[:]), z[j][:])
-
-        early = [(0, 0, 2), (1, 0, 2), (2, 0, GROUP), (3, 0, GROUP)]
-        for n, (j, first, last) in enumerate(early):
-            experts(j, first, last, sums[n % BANKS])
-            scatter_y(j, first, last)
-        for j in range(2):
-            experts(j, 2, GROUP, turned[j])
-            experts(j, GROUP, E, sums[1 + j])
-            scatter_y(j, 2, E)
-        nc.tensor.transpose(turned[BANKS - 1][:, 0:P], gate_rows[:], ident[:])
-        nc.scalar.copy(gate_cols[:], turned[BANKS - 1][:, 0:16])
-        for u in range(4):
-            adapter_in(u, u % BANKS)
+        expert(0, banks[0], range(0, 2))
+        expert(0, banks[5], range(2, NT))
+        gather_words(a_words[1][:], 1, offs2_sb[:])
+        gather_bytes(late_planes[:], slots(EARLY, T))
+        for half in range(2):
+            lo, hi = half * LATE // 2, (half + 1) * LATE // 2
+            for s in range(PASSES):
+                gather_words(late_words[s][:, lo:hi], s, slots(EARLY + lo, EARLY + hi))
+        scatter_on_scalar(0, C)
+        for u in range(M // P):
+            adapter_in(u, banks[1 + u % 2], banks[3 + u % 2])
+        expert(1, banks[1])
+        scatter_on_scalar(C, 2 * C)
+        expert(2, banks[2])
         nc.vector.quantize_mx(out=h_codes[:].bitcast(FP8X4), scales=h_scales[:], in_=h_in[:])
-        for j in range(2, NT):
-            experts(j, GROUP, E, h_turned[1])
-            scatter_y(j, GROUP, E)
-        for u in range(4):
-            adapter_out(u, (u + 1) % BANKS)
+        for e in range(3, 6):
+            expert(e, banks[1 + (e - 1) % 4])
+        scatter_on_scalar(EARLY, SHARE)
         for j in range(NT):
-            turn_back(j, turned[j % BANKS])
+            adapter_out(j, banks[(0, 5, 6, 7)[j]])
+        for e in range(6, E):
+            expert(e, banks[1 + (e - 1) % 4])
+        for j in range(NT):
+            for f in range(F):
+                cols = slice(f * D, (f + 1) * D)
+                nc.scalar.activation(z_sb[j][:].indirect(offs2_sb[:, f * D // 16 : (f + 1) * D // 16]), z[j][:, cols], COPY)
+            nc.vector.tensor_copy(o_sb[j][:].indirect(slots(SHARE, T)), y[:, j, SHARE:T])
             if j < NT - 1:
-                nc.gpsimd.tensor_tensor(z_sb[j][:], o_sb[j][:, 0:T], z_sb[j][:], ADD)
+                nc.gpsimd.tensor_tensor(z_sb[j][:], o_sb[j][:], z_sb[j][:], ADD)
                 nc.sync.dma_start(out[j * P : (j + 1) * P, :], z_sb[j][:])
         j = NT - 1
-        edges = [0, 256, 512, 768, T]
-        for lo, hi in zip(edges[:-1], edges[1:]):
-            nc.vector.tensor_tensor(z_sb[j][:, lo:hi], o_sb[j][:, lo:hi], z_sb[j][:, lo:hi], ADD)
-            nc.sync.dma_start(out[j * P : (j + 1) * P, lo:hi], z_sb[j][:, lo:hi])
+        for lo in range(0, T, 256):
+            cols = slice(lo, lo + 256)
+            nc.vector.tensor_tensor(o_sb[j - 1][:, cols], o_sb[j][:, cols], z_sb[j][:, cols], ADD)
+            nc.sync.dma_start(out[j * P : (j + 1) * P, cols], o_sb[j - 1][:, cols])

@@ -27,7 +27,7 @@ M = F * D
 NT = N // P
 EARLY = 2 * C
 LATE = T - EARLY
-SHARE = 448
+SHARE = 480
 
 
 def tile_moe_mlr_silu_kernel(
@@ -61,14 +61,14 @@ def tile_moe_mlr_silu_kernel(
 
         w1_sb = keep.tile([P, PASSES, 4 * N], U8, name="w1_sb", align_bytes=64)
         w_pairs = [keep.tile([P, 2 * PASSES, 4 * N], U8, name="w_pair%d" % g, align_bytes=64) for g in range(1, E // 2)]
-        ws0_sb = keep.tile([P, N], U8, name="ws0_sb", align_bytes=64)
-        ws_sb = keep.tile([P, E - 1, N], U8, name="ws_sb", align_bytes=64)
+        ws_early = [keep.tile([P, N], U8, name="ws_early%d" % e, align_bytes=64) for e in range(2)]
+        ws_sb = keep.tile([P, E - 2, N], U8, name="ws_sb", align_bytes=64)
         wa_sb = keep.tile([P, F * PASSES, 2 * H], U8, name="wa_sb", align_bytes=64)
         was_sb = keep.tile([P, F * PASSES, H], U8, name="was_sb", align_bytes=64)
         wb_sb = keep.tile([P, F, 2 * N], U8, name="wb_sb", align_bytes=64)
         wbs_sb = keep.tile([P, F, N], U8, name="wbs_sb", align_bytes=64)
-        gate0_sb = keep.tile([P, C], F32, name="gate0_sb")
-        gate_sb = keep.tile([P, T - C], F32, name="gate_sb")
+        gate0_sb = keep.tile([P, EARLY], F32, name="gate0_sb")
+        gate_sb = keep.tile([P, LATE], F32, name="gate_sb")
         gate2_sb = keep.tile([P, M], F32, name="gate2_sb")
         zero_col = keep.tile([P, 1], F32, name="zero_col")
         ident = keep.tile([P, P], F32, name="ident")
@@ -76,7 +76,7 @@ def tile_moe_mlr_silu_kernel(
         z_sb = [keep.tile([P, T], F32, name="z_sb%d" % j) for j in range(NT)]
         y = keep.tile([P, NT, T], F32, name="y")
         z = [keep.tile([P, M], F32, name="z%d" % j) for j in range(NT)]
-        h_rows = [keep.tile([P, H], BF16, name="h_rows%d" % b) for b in range(2)]
+        h_rows = [keep.tile([P, H], BF16, name="h_rows%d" % u) for u in range(M // P)]
         h_in = keep.tile([P, 4 * M], BF16, name="h_in", align_bytes=64)
         h_codes = keep.tile([P, M], U32, name="h_codes", align_bytes=64)
         h_scales = keep.tile([P, M], U8, name="h_scales", align_bytes=64)
@@ -85,11 +85,12 @@ def tile_moe_mlr_silu_kernel(
         def zero(tile_ap):
             nc.gpsimd.memset(tile_ap.bitcast(I32), 0)
 
-        nc.vector.memset(xs_sb[:].bitcast(I32), 0)
-        zero(ws0_sb[:])
+        zero(xs_sb[:])
+        zero(ws_early[0][:])
         nc.gpsimd.memset(zero_col[:], 0.0)
         zero(was_sb[:].rearrange("p a n -> p (a n)"))
         zero(a_plane1[:])
+        zero(ws_early[1][:])
         zero(ws_sb[:].rearrange("p a n -> p (a n)"))
         make_identity(nc, ident[:])
         zero(wbs_sb[:].rearrange("p a n -> p (a n)"))
@@ -116,8 +117,8 @@ def tile_moe_mlr_silu_kernel(
         load_both_passes(xs_sb, x_scales)
         load(x_sb[:].rearrange("p (s t) -> p s t", s=PASSES), x_words.rearrange("s p t d -> p s (t d)"))
         load(w0_sb[:], w_rows[:, 0:PASSES, :])
-        load_both_passes(ws0_sb, w_scales[0])
-        nc.sync.dma_start(gate0_sb[:], gate[:, 0:C])
+        load_both_passes(ws_early[0], w_scales[0])
+        nc.sync.dma_start(gate0_sb[:], gate[:, 0:EARLY])
 
         def slots(lo, hi):
             return offs_sb[:, lo // 16 : hi // 16]
@@ -139,14 +140,15 @@ def tile_moe_mlr_silu_kernel(
         load(w1_sb[:], w_rows[:, PASSES : 2 * PASSES, :])
         for q in range(QUADS):
             load(a_plane1[32 * q : 32 * q + ROWS, :], a_planes[32 * q + ROWS : 32 * q + 2 * ROWS, :])
-        load(w_pairs[0][:], w_rows[:, 2 * PASSES : 4 * PASSES, :])
-        load_planes(ws_sb[:], w_scales[1:, 0], 0)
-        nc.sync.dma_start(gate_sb[:], gate[:, C:])
-        load_planes(ws_sb[:], w_scales[1:, 1], ROWS)
-        load(w_pairs[1][:], w_rows[:, 4 * PASSES : 6 * PASSES, :])
         load(wb_sb[:], wb_words.rearrange("f s p n -> p (f s) n"))
+        load_both_passes(ws_early[1], w_scales[1])
         nc.sync.dma_start(gate2_sb[:], gate2)
         load_planes(wbs_sb[:], wb_scales.rearrange("f s b n -> (f s) b n"), 0)
+        load(w_pairs[0][:], w_rows[:, 2 * PASSES : 4 * PASSES, :])
+        load_planes(ws_sb[:], w_scales[2:, 0], 0)
+        nc.sync.dma_start(gate_sb[:], gate[:, EARLY:])
+        load_planes(ws_sb[:], w_scales[2:, 1], ROWS)
+        load(w_pairs[1][:], w_rows[:, 4 * PASSES : 6 * PASSES, :])
         load(w_pairs[2][:], w_rows[:, 6 * PASSES : 8 * PASSES, :])
 
         def expert(e, bank, tiles=range(NT)):
@@ -161,13 +163,13 @@ def tile_moe_mlr_silu_kernel(
                     nc.tensor.matmul_mx(
                         out=bank[:, n * C : (n + 1) * C],
                         lhsT=w_sb[:, s, 4 * P * j : 4 * P * (j + 1)].bitcast(FP8X4),
-                        lhsT_scale=ws0_sb[ROWS * s : P, cols] if e == 0 else ws_sb[ROWS * s : P, e - 1, cols],
+                        lhsT_scale=ws_early[e][ROWS * s : P, cols] if e < 2 else ws_sb[ROWS * s : P, e - 2, cols],
                         rhs=words[s][:, first : first + C].bitcast(FP8X4),
                         rhs_scale=planes[ROWS * s : P, first : first + C],
                         start=(s == 0),
                         stop=(s == PASSES - 1),
                     )
-            g = gate0_sb[:] if e == 0 else gate_sb[:, (e - 1) * C : e * C]
+            g = gate0_sb[:, e * C : (e + 1) * C] if e < 2 else gate_sb[:, (e - 2) * C : (e - 1) * C]
             nc.vector.tensor_tensor(
                 y[:, tiles.start : tiles.stop, e * C : (e + 1) * C],
                 bank[:, 0 : len(tiles) * C].rearrange("p (j c) -> p j c", c=C),
@@ -175,11 +177,19 @@ def tile_moe_mlr_silu_kernel(
                 MULT,
             )
 
-        def scatter_on_scalar(lo, hi):
-            for j in range(NT):
+        def scatter_on_scalar(lo, hi, tiles):
+            for j in tiles:
                 nc.scalar.activation(o_sb[j][:].indirect(slots(lo, hi)), y[:, j, lo:hi], COPY)
 
-        def adapter_in(u, sums, turned):
+        def scatter_on_vector(j, lo, hi):
+            nc.vector.tensor_copy(o_sb[j][:].indirect(slots(lo, hi)), y[:, j, lo:hi])
+
+        def scatter_z(j):
+            for f in range(F):
+                cols = slice(f * D, (f + 1) * D)
+                nc.scalar.activation(z_sb[j][:].indirect(offs2_sb[:, f * D // 16 : (f + 1) * D // 16]), z[j][:, cols], COPY)
+
+        def adapter_in(u, sums):
             f = u * P // D
             cols = slice(u * P, (u + 1) * P)
             for s in range(PASSES):
@@ -193,16 +203,20 @@ def tile_moe_mlr_silu_kernel(
                     stop=(s == PASSES - 1),
                 )
             nc.scalar.activation(
-                h_rows[u % 2][:].rearrange("m (v p e) -> m v p e", v=2, e=2),
+                h_rows[u][:].rearrange("m (v p e) -> m v p e", v=2, e=2),
                 sums[:].rearrange("m (p v e) -> m v p e", v=2, e=2),
                 SILU,
             )
-            pairs = h_rows[u % 2][:].bitcast(F32)
-            for v in range(2):
-                nc.tensor.transpose(turned[:, v * P : (v + 1) * P], pairs[:, v * P : (v + 1) * P], ident[:])
+
+        def turn_h(f, turned):
+            for b in range(D // P):
+                pairs = h_rows[f * D // P + b][:].bitcast(F32)
+                for v in range(2):
+                    at = v * D + b * P
+                    nc.tensor.transpose(turned[:, at : at + P], pairs[:, v * P : (v + 1) * P], ident[:])
             nc.scalar.copy(
-                h_in[:, 4 * u * P : 4 * (u + 1) * P].bitcast(F32).rearrange("p (m v) -> p m v", v=2),
-                turned[:, 0 : 2 * P].rearrange("p (v m) -> p m v", v=2),
+                h_in[:, 4 * f * D : 4 * (f + 1) * D].bitcast(F32).rearrange("p (m v) -> p m v", v=2),
+                turned[:].rearrange("p (v m) -> p m v", v=2),
             )
 
         def adapter_out(j, bank):
@@ -227,25 +241,31 @@ def tile_moe_mlr_silu_kernel(
             lo, hi = half * LATE // 2, (half + 1) * LATE // 2
             for s in range(PASSES):
                 gather_words(late_words[s][:, lo:hi], s, slots(EARLY + lo, EARLY + hi))
-        scatter_on_scalar(0, C)
+        scatter_on_scalar(0, C, range(NT))
         for u in range(M // P):
-            adapter_in(u, banks[1 + u % 2], banks[3 + u % 2])
+            adapter_in(u, banks[(6, 7, 1, 2)[u]])
+            if u % 2:
+                turn_h(u // 2, banks[3 + u // 2])
         expert(1, banks[1])
-        scatter_on_scalar(C, 2 * C)
-        expert(2, banks[2])
+        scatter_on_scalar(C, 2 * C, range(NT))
         nc.vector.quantize_mx(out=h_codes[:].bitcast(FP8X4), scales=h_scales[:], in_=h_in[:])
-        for e in range(3, 6):
+        adapter_out(0, banks[6])
+        scatter_z(0)
+        for e in range(2, 6):
             expert(e, banks[1 + (e - 1) % 4])
-        scatter_on_scalar(EARLY, SHARE)
+        scatter_on_scalar(EARLY, SHARE, range(1, NT))
+        scatter_on_vector(0, SHARE, 6 * C)
+        expert(6, banks[2])
+        expert(7, banks[3])
+        adapter_out(1, banks[2])
+        scatter_on_vector(0, 6 * C, T)
+        scatter_on_scalar(EARLY, SHARE, range(0, 1))
         for j in range(NT):
-            adapter_out(j, banks[(0, 5, 6, 7)[j]])
-        for e in range(6, E):
-            expert(e, banks[1 + (e - 1) % 4])
-        for j in range(NT):
-            for f in range(F):
-                cols = slice(f * D, (f + 1) * D)
-                nc.scalar.activation(z_sb[j][:].indirect(offs2_sb[:, f * D // 16 : (f + 1) * D // 16]), z[j][:, cols], COPY)
-            nc.vector.tensor_copy(o_sb[j][:].indirect(slots(SHARE, T)), y[:, j, SHARE:T])
+            if j > 0:
+                scatter_z(j)
+                if j < NT - 1:
+                    adapter_out(j + 1, banks[2 + j % 2])
+                scatter_on_vector(j, SHARE, T)
             if j < NT - 1:
                 nc.gpsimd.tensor_tensor(z_sb[j][:], o_sb[j][:], z_sb[j][:], ADD)
                 nc.sync.dma_start(out[j * P : (j + 1) * P, :], z_sb[j][:])

@@ -26,7 +26,9 @@ ROWS = 4
 M = F * D
 NT = N // P
 EARLY = 2 * C
-LATE = T - EARLY
+HALF = (T - EARLY) // 2
+WIDE = 1376
+WS_GROUPS = (range(1, 5), range(0, 16, 15), range(5, 9), range(9, 13), range(13, 15))
 SHARE = 480
 
 
@@ -42,34 +44,32 @@ def tile_moe_mlr_silu_kernel(
         offs_sb = keep.tile([P, T // 16], U16, name="offs_sb")
         offs2_sb = keep.tile([P, M // 16], U16, name="offs2_sb")
         x_sb = keep.tile([P, PASSES * T], I32, name="x_sb", align_bytes=64)
-        xs_sb = keep.tile([P, T], U8, name="xs_sb", align_bytes=64)
-        early_words = [keep.tile([P, EARLY], U32, name="early_words%d" % s, align_bytes=64) for s in range(PASSES)]
-        early_planes = keep.tile([P, EARLY], U8, name="early_planes", align_bytes=64)
-        a_words0 = keep.tile([P, M], U32, name="a_words0", align_bytes=64)
+        xs_sb = keep.tile([P, WIDE], U8, name="xs_sb", align_bytes=64)
+        e_planes = keep.tile([P, T], U8, name="e_planes", align_bytes=64)
+        words1 = keep.tile([P, PASSES * C], U32, name="words1", align_bytes=64)
         a_planes = keep.tile([P, M], U8, name="a_planes", align_bytes=64)
         a_plane1 = keep.tile([P, M], U8, name="a_plane1", align_bytes=64)
 
-        w0_at = 4 * M - 64
+        a_bytes = 4 * PASSES * M
+        w1_sb = reuse.tile([P, PASSES, 4 * N], U8, name="w1_sb", align_bytes=64, offset=a_bytes - 64)
+        a_words = reuse.tile([P, PASSES * M], U32, name="a_words", align_bytes=64, offset=0)
+        words0 = reuse.tile([P, PASSES * C], U32, name="words0", align_bytes=64, offset=a_bytes)
+        late_at = a_bytes + 4 * PASSES * C
+        w0_at = late_at + 4 * PASSES * HALF
         w0_sb = reuse.tile([P, PASSES, 4 * N], U8, name="w0_sb", align_bytes=64, offset=w0_at)
-        a_words1 = reuse.tile([P, M], U32, name="a_words1", align_bytes=64, offset=0)
-        late_planes = reuse.tile([P, LATE], U8, name="late_planes", align_bytes=64, offset=4 * M)
         late_words = [
-            reuse.tile([P, LATE], U32, name="late_words%d" % s, align_bytes=64, offset=4 * M + LATE + 4 * LATE * s)
-            for s in range(PASSES)
+            reuse.tile([P, PASSES * HALF], U32, name="late_words%d" % n, align_bytes=64, offset=(late_at, w0_at)[n])
+            for n in range(2)
         ]
-        a_words = [a_words0, a_words1]
-
-        w1_sb = keep.tile([P, PASSES, 4 * N], U8, name="w1_sb", align_bytes=64)
         w_pairs = [keep.tile([P, 2 * PASSES, 4 * N], U8, name="w_pair%d" % g, align_bytes=64) for g in range(1, E // 2)]
-        ws_early = [keep.tile([P, N], U8, name="ws_early%d" % e, align_bytes=64) for e in range(2)]
-        ws_sb = keep.tile([P, E - 2, N], U8, name="ws_sb", align_bytes=64)
+        ws_sb = [keep.tile([P, N], U8, name="ws_sb%d" % g, align_bytes=64) for g in range(len(WS_GROUPS))]
         wa_sb = keep.tile([P, F * PASSES, 2 * H], U8, name="wa_sb", align_bytes=64)
         was_sb = keep.tile([P, F * PASSES, H], U8, name="was_sb", align_bytes=64)
         wb_sb = keep.tile([P, F, 2 * N], U8, name="wb_sb", align_bytes=64)
         wbs_sb = keep.tile([P, F, N], U8, name="wbs_sb", align_bytes=64)
-        gate0_sb = keep.tile([P, EARLY], F32, name="gate0_sb")
-        gate_sb = keep.tile([P, LATE], F32, name="gate_sb")
-        gate2_sb = keep.tile([P, M], F32, name="gate2_sb")
+        gate_rows = keep.tile([P, P], F32, name="gate_rows")
+        gate_cols = keep.tile([P, 16], F32, name="gate_cols")
+        gates = [keep.tile([P, N], F32, name="gates%d" % b) for b in range(3)]
         zero_col = keep.tile([P, 1], F32, name="zero_col")
         ident = keep.tile([P, P], F32, name="ident")
         o_sb = [keep.tile([P, T], F32, name="o_sb%d" % j) for j in range(NT)]
@@ -85,91 +85,112 @@ def tile_moe_mlr_silu_kernel(
         def zero(tile_ap):
             nc.gpsimd.memset(tile_ap.bitcast(I32), 0)
 
-        zero(xs_sb[:])
-        zero(ws_early[0][:])
+        zero(xs_sb[:, 0:T])
+        nc.gpsimd.memset(gate_rows[:], 0.0)
         nc.gpsimd.memset(zero_col[:], 0.0)
+        zero(ws_sb[0][:])
+        make_identity(nc, ident[:])
         zero(was_sb[:].rearrange("p a n -> p (a n)"))
         zero(a_plane1[:])
-        zero(ws_early[1][:])
-        zero(ws_sb[:].rearrange("p a n -> p (a n)"))
-        make_identity(nc, ident[:])
+        for g in range(1, len(WS_GROUPS)):
+            zero(ws_sb[g][:])
         zero(wbs_sb[:].rearrange("p a n -> p (a n)"))
-        for j in range(NT - 1):
-            nc.scalar.activation(z_sb[j][:], zero_col[:].to_broadcast([P, T]), SILU)
-        nc.gpsimd.memset(z_sb[NT - 1][:], 0.0)
+        nc.scalar.activation(z_sb[0][:], zero_col[:].to_broadcast([P, T]), SILU)
+        for j in range(1, NT):
+            nc.gpsimd.memset(z_sb[j][:], 0.0)
 
         def load(dst, src):
             nc.sync.dma_start(dst.bitcast(I32), src.bitcast(I32))
 
-        def load_planes(dst, src, start):
-            for q in range(QUADS):
-                row = 32 * q + start
-                load(dst[row : row + ROWS, :, :], src[:, ROWS * q : ROWS * (q + 1), :].rearrange("a r n -> r a n"))
-
-        def load_both_passes(dst, src):
-            for q in range(QUADS):
-                load(dst[32 * q : 32 * q + PASSES * ROWS, :], src[:, ROWS * q : ROWS * (q + 1), :])
+        def load_planes(dst, src):
+            for r in range(ROWS):
+                load(dst[r:P:32, :, :], src[:, r :: ROWS, :].rearrange("a q n -> q a n"))
 
         w_rows = w_words.rearrange("e s p n d -> p (e s) (n d)")
+        ws_rows = w_scales.rearrange("e s b n -> (e s) b n")
+
+        def load_ws(g):
+            group = WS_GROUPS[g]
+            for q in range(QUADS):
+                load(
+                    ws_sb[g][32 * q : 32 * q + ROWS * len(group), :],
+                    ws_rows[group.start : group.stop : group.step, ROWS * q : ROWS * (q + 1), :],
+                )
 
         nc.sync.dma_start(offs_sb[:], offs)
-        nc.sync.dma_start(offs2_sb[:], offs2)
-        load_both_passes(xs_sb, x_scales)
+        for q in range(QUADS):
+            load(xs_sb[32 * q : 32 * q + PASSES * ROWS, 0:T], x_scales[:, ROWS * q : ROWS * (q + 1), :])
+        nc.sync.dma_start(gate_rows[0:E, :], gate[0].rearrange("(e p) -> e p", p=P))
+        nc.sync.dma_start(gate_rows[E : E + M // P, :], gate2[0].rearrange("(e p) -> e p", p=P))
         load(x_sb[:].rearrange("p (s t) -> p s t", s=PASSES), x_words.rearrange("s p t d -> p s (t d)"))
-        load(w0_sb[:], w_rows[:, 0:PASSES, :])
-        load_both_passes(ws_early[0], w_scales[0])
-        nc.sync.dma_start(gate0_sb[:], gate[:, 0:EARLY])
+        nc.sync.dma_start(offs2_sb[:], offs2)
+        load_ws(0)
+        load(w1_sb[:], w_rows[:, PASSES : 2 * PASSES, :])
+
+        nc.tensor.transpose(banks[7][:, 0:P], gate_rows[:], ident[:])
+        nc.scalar.copy(gate_cols[:], banks[7][:, 0:16])
+        for b in range(3):
+            bank = banks[(1, 2, 6)[b]]
+            for u in range(4):
+                col = gate_cols[:, 4 * b + u : 4 * b + u + 1]
+                nc.tensor.transpose(bank[:, u * P : (u + 1) * P], col.to_broadcast([P, P]), ident[:])
+            nc.scalar.copy(gates[b][:], bank[:])
 
         def slots(lo, hi):
             return offs_sb[:, lo // 16 : hi // 16]
 
+        def a_slots(f):
+            return offs2_sb[:, f * D // 16 : (f + 1) * D // 16]
+
         def gather_words(dst, s, offsets):
             nc.vector.tensor_copy(dst, x_sb[:, s * T : (s + 1) * T].bitcast(U32).indirect(offsets))
 
-        def gather_bytes(dst, offsets):
-            nc.vector.tensor_copy(dst, xs_sb[:].indirect(offsets))
+        def gather_bytes(dst, window, offsets):
+            nc.vector.tensor_copy(dst, window.indirect(offsets))
 
-        gather_bytes(early_planes[:], slots(0, EARLY))
-        gather_words(early_words[0][:], 0, slots(0, EARLY))
-        gather_bytes(a_planes[:], offs2_sb[:])
-        gather_words(early_words[1][:], 1, slots(0, EARLY))
-        gather_words(a_words[0][:], 0, offs2_sb[:])
+        gather_bytes(e_planes[:], xs_sb[:], offs_sb[:])
+        for s in range(PASSES):
+            gather_words(words1[:, s * C : (s + 1) * C], s, slots(C, 2 * C))
+        gather_bytes(a_planes[:], xs_sb[:, 0:T], offs2_sb[:])
 
         load(wa_sb[:], wa_words.rearrange("f s p n -> p (f s) n"))
-        load_planes(was_sb[:], wa_scales.rearrange("f s b n -> (f s) b n"), 0)
-        load(w1_sb[:], w_rows[:, PASSES : 2 * PASSES, :])
-        for q in range(QUADS):
-            load(a_plane1[32 * q : 32 * q + ROWS, :], a_planes[32 * q + ROWS : 32 * q + 2 * ROWS, :])
+        load_planes(was_sb[:], wa_scales.rearrange("f s b n -> (f s) b n"))
+        load(w0_sb[:], w_rows[:, 0:PASSES, :])
+        for r in range(ROWS):
+            load(a_plane1[r:P:32, :], a_planes[ROWS + r : P : 32, :])
         load(wb_sb[:], wb_words.rearrange("f s p n -> p (f s) n"))
-        load_both_passes(ws_early[1], w_scales[1])
-        nc.sync.dma_start(gate2_sb[:], gate2)
-        load_planes(wbs_sb[:], wb_scales.rearrange("f s b n -> (f s) b n"), 0)
-        load(w_pairs[0][:], w_rows[:, 2 * PASSES : 4 * PASSES, :])
-        load_planes(ws_sb[:], w_scales[2:, 0], 0)
-        nc.sync.dma_start(gate_sb[:], gate[:, EARLY:])
-        load_planes(ws_sb[:], w_scales[2:, 1], ROWS)
-        load(w_pairs[1][:], w_rows[:, 4 * PASSES : 6 * PASSES, :])
-        load(w_pairs[2][:], w_rows[:, 6 * PASSES : 8 * PASSES, :])
+        load_ws(1)
+        load(w_pairs[0][:, 0:PASSES, :], w_rows[:, 2 * PASSES : 3 * PASSES, :])
+        load_ws(2)
+        load(w_pairs[0][:, PASSES:, :], w_rows[:, 3 * PASSES : 4 * PASSES, :])
+        load_planes(wbs_sb[:], wb_scales.rearrange("f s b n -> (f s) b n"))
+        for g in range(1, 3):
+            load(w_pairs[g][:], w_rows[:, 2 * PASSES * (g + 1) : 2 * PASSES * (g + 2), :])
+            load_ws(2 + g)
+
+        def w_plane(e, s):
+            g = [2 * e + s in group for group in WS_GROUPS].index(True)
+            return ws_sb[g][ROWS * list(WS_GROUPS[g]).index(2 * e + s) : P, :]
 
         def expert(e, bank, tiles=range(NT)):
             if e < 2:
-                w_sb, words, planes, first = (w0_sb, w1_sb)[e][:], early_words, early_planes, e * C
+                w_sb, words, first, width = (w0_sb, w1_sb)[e][:], (words0, words1)[e], 0, C
             else:
                 w_sb = w_pairs[e // 2 - 1][:, PASSES * (e % 2) : PASSES * (e % 2 + 1), :]
-                words, planes, first = late_words, late_planes, e * C - EARLY
+                words, first, width = late_words[(e - 2) // 3], (e - 2) % 3 * C, HALF
             for n, j in enumerate(tiles):
                 cols = slice(j * P, (j + 1) * P)
                 for s in range(PASSES):
                     nc.tensor.matmul_mx(
                         out=bank[:, n * C : (n + 1) * C],
                         lhsT=w_sb[:, s, 4 * P * j : 4 * P * (j + 1)].bitcast(FP8X4),
-                        lhsT_scale=ws_early[e][ROWS * s : P, cols] if e < 2 else ws_sb[ROWS * s : P, e - 2, cols],
-                        rhs=words[s][:, first : first + C].bitcast(FP8X4),
-                        rhs_scale=planes[ROWS * s : P, first : first + C],
+                        lhsT_scale=w_plane(e, s)[:, cols],
+                        rhs=words[:, s * width + first : s * width + first + C].bitcast(FP8X4),
+                        rhs_scale=e_planes[ROWS * s : P, e * C : (e + 1) * C],
                         start=(s == 0),
                         stop=(s == PASSES - 1),
                     )
-            g = gate0_sb[:, e * C : (e + 1) * C] if e < 2 else gate_sb[:, (e - 2) * C : (e - 1) * C]
+            g = gates[e // 4][:, e % 4 * C : (e % 4 + 1) * C]
             nc.vector.tensor_tensor(
                 y[:, tiles.start : tiles.stop, e * C : (e + 1) * C],
                 bank[:, 0 : len(tiles) * C].rearrange("p (j c) -> p j c", c=C),
@@ -187,7 +208,7 @@ def tile_moe_mlr_silu_kernel(
         def scatter_z(j):
             for f in range(F):
                 cols = slice(f * D, (f + 1) * D)
-                nc.scalar.activation(z_sb[j][:].indirect(offs2_sb[:, f * D // 16 : (f + 1) * D // 16]), z[j][:, cols], COPY)
+                nc.scalar.activation(z_sb[j][:].indirect(a_slots(f)), z[j][:, cols], COPY)
 
         def adapter_in(u, sums):
             f = u * P // D
@@ -195,7 +216,7 @@ def tile_moe_mlr_silu_kernel(
             for s in range(PASSES):
                 nc.tensor.matmul_mx(
                     out=sums[:],
-                    lhsT=a_words[s][:, cols].bitcast(FP8X4),
+                    lhsT=a_words[:, s * M + u * P : s * M + (u + 1) * P].bitcast(FP8X4),
                     lhsT_scale=(a_planes, a_plane1)[s][:, cols],
                     rhs=wa_sb[:, f * PASSES + s, :].bitcast(FP4X4),
                     rhs_scale=was_sb[:, f * PASSES + s, :],
@@ -231,32 +252,38 @@ def tile_moe_mlr_silu_kernel(
                     start=True,
                     stop=True,
                 )
-            nc.vector.tensor_tensor(z[j][:], bank[:], gate2_sb[:], MULT)
+            nc.vector.tensor_tensor(z[j][:], bank[:], gates[2][:], MULT)
 
-        expert(0, banks[0], range(0, 2))
-        expert(0, banks[5], range(2, NT))
-        gather_words(a_words[1][:], 1, offs2_sb[:])
-        gather_bytes(late_planes[:], slots(EARLY, T))
-        for half in range(2):
-            lo, hi = half * LATE // 2, (half + 1) * LATE // 2
+        def gather_late(n):
+            lo = EARLY + n * HALF
             for s in range(PASSES):
-                gather_words(late_words[s][:, lo:hi], s, slots(EARLY + lo, EARLY + hi))
-        scatter_on_scalar(0, C, range(NT))
+                gather_words(late_words[n][:, s * HALF : (s + 1) * HALF], s, slots(lo, lo + HALF))
+
+        expert(1, banks[0], range(0, 2))
+        expert(1, banks[5], range(2, NT))
+        for f in range(F):
+            for s in range(PASSES):
+                gather_words(a_words[:, s * M + f * D : s * M + (f + 1) * D], s, a_slots(f))
+        for s in range(PASSES):
+            gather_words(words0[:, s * C : (s + 1) * C], s, slots(0, C))
+        gather_late(0)
+        scatter_on_scalar(C, 2 * C, range(NT))
         for u in range(M // P):
             adapter_in(u, banks[(6, 7, 1, 2)[u]])
-            if u % 2:
-                turn_h(u // 2, banks[3 + u // 2])
-        expert(1, banks[1])
-        scatter_on_scalar(C, 2 * C, range(NT))
+        expert(0, banks[0])
+        gather_late(1)
+        for f in range(F):
+            turn_h(f, banks[3 + f])
+        scatter_on_scalar(0, C, range(NT))
         nc.vector.quantize_mx(out=h_codes[:].bitcast(FP8X4), scales=h_scales[:], in_=h_in[:])
         adapter_out(0, banks[6])
         scatter_z(0)
         for e in range(2, 6):
-            expert(e, banks[1 + (e - 1) % 4])
+            expert(e, banks[(2, 1, 5, 7)[e - 2]])
         scatter_on_scalar(EARLY, SHARE, range(1, NT))
         scatter_on_vector(0, SHARE, 6 * C)
         expert(6, banks[2])
-        expert(7, banks[3])
+        expert(7, banks[1])
         adapter_out(1, banks[2])
         scatter_on_vector(0, 6 * C, T)
         scatter_on_scalar(EARLY, SHARE, range(0, 1))
@@ -264,7 +291,7 @@ def tile_moe_mlr_silu_kernel(
             if j > 0:
                 scatter_z(j)
                 if j < NT - 1:
-                    adapter_out(j + 1, banks[2 + j % 2])
+                    adapter_out(j + 1, banks[2 - j % 2])
                 scatter_on_vector(j, SHARE, T)
             if j < NT - 1:
                 nc.gpsimd.tensor_tensor(z_sb[j][:], o_sb[j][:], z_sb[j][:], ADD)

@@ -29,7 +29,7 @@ EARLY = 2 * C
 HALF = (T - EARLY) // 2
 WIDE = 1376
 WS_GROUPS = (range(1, 5), range(0, 16, 15), range(5, 9), range(9, 13), range(13, 15))
-SHARE = 480
+SHARE = 448
 
 
 def tile_moe_mlr_silu_kernel(
@@ -53,14 +53,17 @@ def tile_moe_mlr_silu_kernel(
         a_bytes = 4 * PASSES * M
         w1_sb = reuse.tile([P, PASSES, 4 * N], U8, name="w1_sb", align_bytes=64, offset=a_bytes - 64)
         a_words = reuse.tile([P, PASSES * M], U32, name="a_words", align_bytes=64, offset=0)
-        words0 = reuse.tile([P, PASSES * C], U32, name="words0", align_bytes=64, offset=a_bytes)
-        late_at = a_bytes + 4 * PASSES * C
-        w0_at = late_at + 4 * PASSES * HALF
-        w0_sb = reuse.tile([P, PASSES, 4 * N], U8, name="w0_sb", align_bytes=64, offset=w0_at)
-        late_words = [
-            reuse.tile([P, PASSES * HALF], U32, name="late_words%d" % n, align_bytes=64, offset=(late_at, w0_at)[n])
-            for n in range(2)
+        words0 = keep.tile([P, PASSES * C], U32, name="words0", align_bytes=64)
+        late_at = a_bytes
+        late_words = reuse.tile([P, 2 * PASSES * HALF], U32, name="late_words", align_bytes=64, offset=late_at)
+        y0_at = late_at + 4 * 2 * PASSES * HALF
+        y0 = reuse.tile([P, NT, C], F32, name="y0", align_bytes=64, offset=y0_at)
+        h_rows = [
+            keep.tile([P, D // P, H], BF16, name="h_rows0"),
+            reuse.tile([P, D // P, H], BF16, name="h_rows1", align_bytes=64, offset=y0_at),
         ]
+
+        w0_sb = keep.tile([P, PASSES, 4 * N], U8, name="w0_sb", align_bytes=64)
         w_pairs = [keep.tile([P, 2 * PASSES, 4 * N], U8, name="w_pair%d" % g, align_bytes=64) for g in range(1, E // 2)]
         ws_sb = [keep.tile([P, N], U8, name="ws_sb%d" % g, align_bytes=64) for g in range(len(WS_GROUPS))]
         wa_sb = keep.tile([P, F * PASSES, 2 * H], U8, name="wa_sb", align_bytes=64)
@@ -74,9 +77,8 @@ def tile_moe_mlr_silu_kernel(
         ident = keep.tile([P, P], F32, name="ident")
         o_sb = [keep.tile([P, T], F32, name="o_sb%d" % j) for j in range(NT)]
         z_sb = [keep.tile([P, T], F32, name="z_sb%d" % j) for j in range(NT)]
-        y = keep.tile([P, NT, T], F32, name="y")
+        y = keep.tile([P, NT, T - C], F32, name="y")
         z = [keep.tile([P, M], F32, name="z%d" % j) for j in range(NT)]
-        h_rows = [keep.tile([P, H], BF16, name="h_rows%d" % u) for u in range(M // P)]
         h_in = keep.tile([P, 4 * M], BF16, name="h_in", align_bytes=64)
         h_codes = keep.tile([P, M], U32, name="h_codes", align_bytes=64)
         h_scales = keep.tile([P, M], U8, name="h_scales", align_bytes=64)
@@ -90,9 +92,10 @@ def tile_moe_mlr_silu_kernel(
         nc.gpsimd.memset(zero_col[:], 0.0)
         zero(ws_sb[0][:])
         make_identity(nc, ident[:])
+        zero(ws_sb[1][:])
         zero(was_sb[:].rearrange("p a n -> p (a n)"))
         zero(a_plane1[:])
-        for g in range(1, len(WS_GROUPS)):
+        for g in range(2, len(WS_GROUPS)):
             zero(ws_sb[g][:])
         zero(wbs_sb[:].rearrange("p a n -> p (a n)"))
         nc.scalar.activation(z_sb[0][:], zero_col[:].to_broadcast([P, T]), SILU)
@@ -152,16 +155,18 @@ def tile_moe_mlr_silu_kernel(
         for s in range(PASSES):
             gather_words(words1[:, s * C : (s + 1) * C], s, slots(C, 2 * C))
         gather_bytes(a_planes[:], xs_sb[:, 0:T], offs2_sb[:])
+        for s in range(PASSES):
+            gather_words(words0[:, s * C : (s + 1) * C], s, slots(0, C))
 
-        load(wa_sb[:], wa_words.rearrange("f s p n -> p (f s) n"))
-        load_planes(was_sb[:], wa_scales.rearrange("f s b n -> (f s) b n"))
+        load_ws(1)
         load(w0_sb[:], w_rows[:, 0:PASSES, :])
+        load_planes(was_sb[:], wa_scales.rearrange("f s b n -> (f s) b n"))
+        load(wa_sb[:], wa_words.rearrange("f s p n -> p (f s) n"))
         for r in range(ROWS):
             load(a_plane1[r:P:32, :], a_planes[ROWS + r : P : 32, :])
-        load(wb_sb[:], wb_words.rearrange("f s p n -> p (f s) n"))
-        load_ws(1)
         load(w_pairs[0][:, 0:PASSES, :], w_rows[:, 2 * PASSES : 3 * PASSES, :])
         load_ws(2)
+        load(wb_sb[:], wb_words.rearrange("f s p n -> p (f s) n"))
         load(w_pairs[0][:, PASSES:, :], w_rows[:, 3 * PASSES : 4 * PASSES, :])
         load_planes(wbs_sb[:], wb_scales.rearrange("f s b n -> (f s) b n"))
         for g in range(1, 3):
@@ -172,12 +177,18 @@ def tile_moe_mlr_silu_kernel(
             g = [2 * e + s in group for group in WS_GROUPS].index(True)
             return ws_sb[g][ROWS * list(WS_GROUPS[g]).index(2 * e + s) : P, :]
 
+        def late_part(n, s):
+            part = PASSES * n + s
+            return late_words[:, part * HALF : (part + 1) * HALF]
+
         def expert(e, bank, tiles=range(NT)):
             if e < 2:
-                w_sb, words, first, width = (w0_sb, w1_sb)[e][:], (words0, words1)[e], 0, C
+                w_sb = (w0_sb, w1_sb)[e][:]
+                words = [(words0, words1)[e][:, s * C : (s + 1) * C] for s in range(PASSES)]
             else:
                 w_sb = w_pairs[e // 2 - 1][:, PASSES * (e % 2) : PASSES * (e % 2 + 1), :]
-                words, first, width = late_words[(e - 2) // 3], (e - 2) % 3 * C, HALF
+                first = (e - 2) % 3 * C
+                words = [late_part((e - 2) // 3, s)[:, first : first + C] for s in range(PASSES)]
             for n, j in enumerate(tiles):
                 cols = slice(j * P, (j + 1) * P)
                 for s in range(PASSES):
@@ -185,14 +196,14 @@ def tile_moe_mlr_silu_kernel(
                         out=bank[:, n * C : (n + 1) * C],
                         lhsT=w_sb[:, s, 4 * P * j : 4 * P * (j + 1)].bitcast(FP8X4),
                         lhsT_scale=w_plane(e, s)[:, cols],
-                        rhs=words[:, s * width + first : s * width + first + C].bitcast(FP8X4),
+                        rhs=words[s].bitcast(FP8X4),
                         rhs_scale=e_planes[ROWS * s : P, e * C : (e + 1) * C],
                         start=(s == 0),
                         stop=(s == PASSES - 1),
                     )
             g = gates[e // 4][:, e % 4 * C : (e % 4 + 1) * C]
             nc.vector.tensor_tensor(
-                y[:, tiles.start : tiles.stop, e * C : (e + 1) * C],
+                y0[:] if e == 0 else y[:, tiles.start : tiles.stop, (e - 1) * C : e * C],
                 bank[:, 0 : len(tiles) * C].rearrange("p (j c) -> p j c", c=C),
                 g.unsqueeze(1).to_broadcast([P, len(tiles), C]),
                 MULT,
@@ -200,10 +211,10 @@ def tile_moe_mlr_silu_kernel(
 
         def scatter_on_scalar(lo, hi, tiles):
             for j in tiles:
-                nc.scalar.activation(o_sb[j][:].indirect(slots(lo, hi)), y[:, j, lo:hi], COPY)
+                nc.scalar.activation(o_sb[j][:].indirect(slots(lo, hi)), y[:, j, lo - C : hi - C] if lo else y0[:, j, :], COPY)
 
         def scatter_on_vector(j, lo, hi):
-            nc.vector.tensor_copy(o_sb[j][:].indirect(slots(lo, hi)), y[:, j, lo:hi])
+            nc.vector.tensor_copy(o_sb[j][:].indirect(slots(lo, hi)), y[:, j, lo - C : hi - C])
 
         def scatter_z(j):
             for f in range(F):
@@ -224,14 +235,14 @@ def tile_moe_mlr_silu_kernel(
                     stop=(s == PASSES - 1),
                 )
             nc.scalar.activation(
-                h_rows[u][:].rearrange("m (v p e) -> m v p e", v=2, e=2),
+                h_rows[f][:, u % 2, :].rearrange("m (v p e) -> m v p e", v=2, e=2),
                 sums[:].rearrange("m (p v e) -> m v p e", v=2, e=2),
                 SILU,
             )
 
         def turn_h(f, turned):
             for b in range(D // P):
-                pairs = h_rows[f * D // P + b][:].bitcast(F32)
+                pairs = h_rows[f][:, b, :].bitcast(F32)
                 for v in range(2):
                     at = v * D + b * P
                     nc.tensor.transpose(turned[:, at : at + P], pairs[:, v * P : (v + 1) * P], ident[:])
@@ -254,26 +265,24 @@ def tile_moe_mlr_silu_kernel(
                 )
             nc.vector.tensor_tensor(z[j][:], bank[:], gates[2][:], MULT)
 
-        def gather_late(n):
+        def gather_late(n, s):
             lo = EARLY + n * HALF
-            for s in range(PASSES):
-                gather_words(late_words[n][:, s * HALF : (s + 1) * HALF], s, slots(lo, lo + HALF))
+            gather_words(late_part(n, s), s, slots(lo, lo + HALF))
 
         expert(1, banks[0], range(0, 2))
         expert(1, banks[5], range(2, NT))
         for f in range(F):
             for s in range(PASSES):
                 gather_words(a_words[:, s * M + f * D : s * M + (f + 1) * D], s, a_slots(f))
-        for s in range(PASSES):
-            gather_words(words0[:, s * C : (s + 1) * C], s, slots(0, C))
-        gather_late(0)
+        for n in range(2):
+            for s in range(PASSES):
+                gather_late(n, s)
         scatter_on_scalar(C, 2 * C, range(NT))
         for u in range(M // P):
             adapter_in(u, banks[(6, 7, 1, 2)[u]])
-        expert(0, banks[0])
-        gather_late(1)
         for f in range(F):
             turn_h(f, banks[3 + f])
+        expert(0, banks[0])
         scatter_on_scalar(0, C, range(NT))
         nc.vector.quantize_mx(out=h_codes[:].bitcast(FP8X4), scales=h_scales[:], in_=h_in[:])
         adapter_out(0, banks[6])

@@ -26,10 +26,10 @@ ROWS = 4
 M = F * D
 NT = N // P
 EARLY = 2 * C
-HALF = (T - EARLY) // 2
 WIDE = 1376
+HALF = (T - EARLY) // 2
 WS_GROUPS = (range(1, 5), range(0, 16, 15), range(5, 9), range(9, 13), range(13, 15))
-SHARE = 448
+SHARE = (EARLY, 512, 512, 576)
 
 
 def tile_moe_mlr_silu_kernel(
@@ -50,21 +50,30 @@ def tile_moe_mlr_silu_kernel(
         a_planes = keep.tile([P, M], U8, name="a_planes", align_bytes=64)
         a_plane1 = keep.tile([P, M], U8, name="a_plane1", align_bytes=64)
 
-        a_bytes = 4 * PASSES * M
-        w1_sb = reuse.tile([P, PASSES, 4 * N], U8, name="w1_sb", align_bytes=64, offset=a_bytes - 64)
-        a_words = reuse.tile([P, PASSES * M], U32, name="a_words", align_bytes=64, offset=0)
-        words0 = keep.tile([P, PASSES * C], U32, name="words0", align_bytes=64)
-        late_at = a_bytes
-        late_words = reuse.tile([P, 2 * PASSES * HALF], U32, name="late_words", align_bytes=64, offset=late_at)
-        y0_at = late_at + 4 * 2 * PASSES * HALF
-        y0 = reuse.tile([P, NT, C], F32, name="y0", align_bytes=64, offset=y0_at)
-        h_rows = [
-            keep.tile([P, D // P, H], BF16, name="h_rows0"),
-            reuse.tile([P, D // P, H], BF16, name="h_rows1", align_bytes=64, offset=y0_at),
+        a_bytes = 4 * PASSES * D
+        w1_halves = [
+            reuse.tile([P, PASSES, 2 * N], U8, name="w1_half%d" % n, align_bytes=64, offset=(0, 2 * a_bytes - 64)[n])
+            for n in range(2)
         ]
-
-        w0_sb = keep.tile([P, PASSES, 4 * N], U8, name="w0_sb", align_bytes=64)
-        w_pairs = [keep.tile([P, 2 * PASSES, 4 * N], U8, name="w_pair%d" % g, align_bytes=64) for g in range(1, E // 2)]
+        a_words = [
+            reuse.tile([P, PASSES * D], U32, name="a_words%d" % f, align_bytes=64, offset=f * a_bytes) for f in range(F)
+        ]
+        words0 = reuse.tile([P, PASSES * C], U32, name="words0", align_bytes=64, offset=2 * a_bytes)
+        late_at = 2 * a_bytes + 4 * PASSES * C
+        w0_at = late_at + 4 * PASSES * HALF
+        w0_sb = reuse.tile([P, PASSES, 4 * N], U8, name="w0_sb", align_bytes=64, offset=w0_at)
+        late_words = [
+            reuse.tile([P, PASSES * HALF], U32, name="late_words%d" % n, align_bytes=64, offset=(late_at, w0_at)[n])
+            for n in range(2)
+        ]
+        w45_at = w0_at + PASSES * 4 * N
+        w_pairs = [
+            keep.tile([P, 2 * PASSES, 4 * N], U8, name="w23", align_bytes=64),
+            reuse.tile([P, 2 * PASSES, 4 * N], U8, name="w45", align_bytes=64, offset=w45_at),
+            keep.tile([P, 2 * PASSES, 4 * N], U8, name="w67", align_bytes=64),
+        ]
+        h_codes = reuse.tile([P, M], U32, name="h_codes", align_bytes=64, offset=w45_at)
+        h_rows = [keep.tile([P, D // P, H], BF16, name="h_rows%d" % f) for f in range(F)]
         ws_sb = [keep.tile([P, N], U8, name="ws_sb%d" % g, align_bytes=64) for g in range(len(WS_GROUPS))]
         wa_sb = keep.tile([P, F * PASSES, 2 * H], U8, name="wa_sb", align_bytes=64)
         was_sb = keep.tile([P, F * PASSES, H], U8, name="was_sb", align_bytes=64)
@@ -77,10 +86,9 @@ def tile_moe_mlr_silu_kernel(
         ident = keep.tile([P, P], F32, name="ident")
         o_sb = [keep.tile([P, T], F32, name="o_sb%d" % j) for j in range(NT)]
         z_sb = [keep.tile([P, T], F32, name="z_sb%d" % j) for j in range(NT)]
-        y = keep.tile([P, NT, T - C], F32, name="y")
-        z = [keep.tile([P, M], F32, name="z%d" % j) for j in range(NT)]
+        y = keep.tile([P, NT, T], F32, name="y")
+        z = keep.tile([P, NT, M], F32, name="z")
         h_in = keep.tile([P, 4 * M], BF16, name="h_in", align_bytes=64)
-        h_codes = keep.tile([P, M], U32, name="h_codes", align_bytes=64)
         h_scales = keep.tile([P, M], U8, name="h_scales", align_bytes=64)
         banks = [psum.tile([P, N], F32, name="bank%d" % b) for b in range(8)]
 
@@ -92,10 +100,9 @@ def tile_moe_mlr_silu_kernel(
         nc.gpsimd.memset(zero_col[:], 0.0)
         zero(ws_sb[0][:])
         make_identity(nc, ident[:])
-        zero(ws_sb[1][:])
         zero(was_sb[:].rearrange("p a n -> p (a n)"))
         zero(a_plane1[:])
-        for g in range(2, len(WS_GROUPS)):
+        for g in range(1, len(WS_GROUPS)):
             zero(ws_sb[g][:])
         zero(wbs_sb[:].rearrange("p a n -> p (a n)"))
         nc.scalar.activation(z_sb[0][:], zero_col[:].to_broadcast([P, T]), SILU)
@@ -120,6 +127,9 @@ def tile_moe_mlr_silu_kernel(
                     ws_rows[group.start : group.stop : group.step, ROWS * q : ROWS * (q + 1), :],
                 )
 
+        def load_w1(n):
+            load(w1_halves[n][:], w_rows[:, PASSES : 2 * PASSES, 2 * N * n : 2 * N * (n + 1)])
+
         nc.sync.dma_start(offs_sb[:], offs)
         for q in range(QUADS):
             load(xs_sb[32 * q : 32 * q + PASSES * ROWS, 0:T], x_scales[:, ROWS * q : ROWS * (q + 1), :])
@@ -128,7 +138,8 @@ def tile_moe_mlr_silu_kernel(
         load(x_sb[:].rearrange("p (s t) -> p s t", s=PASSES), x_words.rearrange("s p t d -> p s (t d)"))
         nc.sync.dma_start(offs2_sb[:], offs2)
         load_ws(0)
-        load(w1_sb[:], w_rows[:, PASSES : 2 * PASSES, :])
+        load_w1(0)
+        load_w1(1)
 
         nc.tensor.transpose(banks[7][:, 0:P], gate_rows[:], ident[:])
         nc.scalar.copy(gate_cols[:], banks[7][:, 0:16])
@@ -151,19 +162,24 @@ def tile_moe_mlr_silu_kernel(
         def gather_bytes(dst, window, offsets):
             nc.vector.tensor_copy(dst, window.indirect(offsets))
 
-        gather_bytes(e_planes[:], xs_sb[:], offs_sb[:])
-        for s in range(PASSES):
-            gather_words(words1[:, s * C : (s + 1) * C], s, slots(C, 2 * C))
-        gather_bytes(a_planes[:], xs_sb[:, 0:T], offs2_sb[:])
-        for s in range(PASSES):
-            gather_words(words0[:, s * C : (s + 1) * C], s, slots(0, C))
+        def gather_expert(dst, e):
+            for s in range(PASSES):
+                gather_words(dst[:, s * C : (s + 1) * C], s, slots(e * C, (e + 1) * C))
 
-        load_ws(1)
-        load(w0_sb[:], w_rows[:, 0:PASSES, :])
+        def gather_adapter(f):
+            for s in range(PASSES):
+                gather_words(a_words[f][:, s * D : (s + 1) * D], s, a_slots(f))
+
+        gather_bytes(e_planes[:], xs_sb[:], offs_sb[:])
+        gather_expert(words1, 1)
+        gather_bytes(a_planes[:], xs_sb[:, 0:T], offs2_sb[:])
+
         load_planes(was_sb[:], wa_scales.rearrange("f s b n -> (f s) b n"))
         load(wa_sb[:], wa_words.rearrange("f s p n -> p (f s) n"))
+        load(w0_sb[:], w_rows[:, 0:PASSES, :])
         for r in range(ROWS):
             load(a_plane1[r:P:32, :], a_planes[ROWS + r : P : 32, :])
+        load_ws(1)
         load(w_pairs[0][:, 0:PASSES, :], w_rows[:, 2 * PASSES : 3 * PASSES, :])
         load_ws(2)
         load(wb_sb[:], wb_words.rearrange("f s p n -> p (f s) n"))
@@ -178,12 +194,11 @@ def tile_moe_mlr_silu_kernel(
             return ws_sb[g][ROWS * list(WS_GROUPS[g]).index(2 * e + s) : P, :]
 
         def late_part(n, s):
-            part = PASSES * n + s
-            return late_words[:, part * HALF : (part + 1) * HALF]
+            return late_words[n][:, s * HALF : (s + 1) * HALF]
 
         def expert(e, bank, tiles=range(NT)):
             if e < 2:
-                w_sb = (w0_sb, w1_sb)[e][:]
+                w_sb = w0_sb[:]
                 words = [(words0, words1)[e][:, s * C : (s + 1) * C] for s in range(PASSES)]
             else:
                 w_sb = w_pairs[e // 2 - 1][:, PASSES * (e % 2) : PASSES * (e % 2 + 1), :]
@@ -192,9 +207,13 @@ def tile_moe_mlr_silu_kernel(
             for n, j in enumerate(tiles):
                 cols = slice(j * P, (j + 1) * P)
                 for s in range(PASSES):
+                    if e == 1:
+                        w_tile = w1_halves[j // 2][:, s, 4 * P * (j % 2) : 4 * P * (j % 2 + 1)]
+                    else:
+                        w_tile = w_sb[:, s, 4 * P * j : 4 * P * (j + 1)]
                     nc.tensor.matmul_mx(
                         out=bank[:, n * C : (n + 1) * C],
-                        lhsT=w_sb[:, s, 4 * P * j : 4 * P * (j + 1)].bitcast(FP8X4),
+                        lhsT=w_tile.bitcast(FP8X4),
                         lhsT_scale=w_plane(e, s)[:, cols],
                         rhs=words[s].bitcast(FP8X4),
                         rhs_scale=e_planes[ROWS * s : P, e * C : (e + 1) * C],
@@ -203,7 +222,7 @@ def tile_moe_mlr_silu_kernel(
                     )
             g = gates[e // 4][:, e % 4 * C : (e % 4 + 1) * C]
             nc.vector.tensor_tensor(
-                y0[:] if e == 0 else y[:, tiles.start : tiles.stop, (e - 1) * C : e * C],
+                y[:, tiles.start : tiles.stop, e * C : (e + 1) * C],
                 bank[:, 0 : len(tiles) * C].rearrange("p (j c) -> p j c", c=C),
                 g.unsqueeze(1).to_broadcast([P, len(tiles), C]),
                 MULT,
@@ -211,15 +230,14 @@ def tile_moe_mlr_silu_kernel(
 
         def scatter_on_scalar(lo, hi, tiles):
             for j in tiles:
-                nc.scalar.activation(o_sb[j][:].indirect(slots(lo, hi)), y[:, j, lo - C : hi - C] if lo else y0[:, j, :], COPY)
+                nc.scalar.activation(o_sb[j][:].indirect(slots(lo, hi)), y[:, j, lo:hi], COPY)
 
         def scatter_on_vector(j, lo, hi):
-            nc.vector.tensor_copy(o_sb[j][:].indirect(slots(lo, hi)), y[:, j, lo - C : hi - C])
+            nc.vector.tensor_copy(o_sb[j][:].indirect(slots(lo, hi)), y[:, j, lo:hi])
 
-        def scatter_z(j):
-            for f in range(F):
-                cols = slice(f * D, (f + 1) * D)
-                nc.scalar.activation(z_sb[j][:].indirect(a_slots(f)), z[j][:, cols], COPY)
+        def scatter_z(parts):
+            for j, f in parts:
+                nc.scalar.activation(z_sb[j][:].indirect(a_slots(f)), z[:, j, f * D : (f + 1) * D], COPY)
 
         def adapter_in(u, sums):
             f = u * P // D
@@ -227,7 +245,7 @@ def tile_moe_mlr_silu_kernel(
             for s in range(PASSES):
                 nc.tensor.matmul_mx(
                     out=sums[:],
-                    lhsT=a_words[:, s * M + u * P : s * M + (u + 1) * P].bitcast(FP8X4),
+                    lhsT=a_words[f][:, s * D + u * P % D : s * D + u * P % D + P].bitcast(FP8X4),
                     lhsT_scale=(a_planes, a_plane1)[s][:, cols],
                     rhs=wa_sb[:, f * PASSES + s, :].bitcast(FP4X4),
                     rhs_scale=was_sb[:, f * PASSES + s, :],
@@ -251,57 +269,75 @@ def tile_moe_mlr_silu_kernel(
                 turned[:].rearrange("p (v m) -> p m v", v=2),
             )
 
+        def multiply_h(j, f, sums):
+            cols = slice(f * D, (f + 1) * D)
+            nc.tensor.matmul_mx(
+                out=sums,
+                lhsT=wb_sb[:, f, 2 * P * j : 2 * P * (j + 1)].bitcast(FP4X4),
+                lhsT_scale=wbs_sb[:, f, j * P : (j + 1) * P],
+                rhs=h_codes[:, cols].bitcast(FP8X4),
+                rhs_scale=h_scales[:, cols],
+                start=True,
+                stop=True,
+            )
+
         def adapter_out(j, bank):
             for f in range(F):
-                cols = slice(f * D, (f + 1) * D)
-                nc.tensor.matmul_mx(
-                    out=bank[:, cols],
-                    lhsT=wb_sb[:, f, 2 * P * j : 2 * P * (j + 1)].bitcast(FP4X4),
-                    lhsT_scale=wbs_sb[:, f, j * P : (j + 1) * P],
-                    rhs=h_codes[:, cols].bitcast(FP8X4),
-                    rhs_scale=h_scales[:, cols],
-                    start=True,
-                    stop=True,
-                )
-            nc.vector.tensor_tensor(z[j][:], bank[:], gates[2][:], MULT)
+                multiply_h(j, f, bank[:, f * D : (f + 1) * D])
+            nc.vector.tensor_tensor(z[:, j, :], bank[:], gates[2][:], MULT)
+
+        def adapter_out_pair(f, bank):
+            for j in range(2):
+                multiply_h(j, f, bank[:, j * D : (j + 1) * D])
+            nc.vector.tensor_tensor(
+                z[:, 0:2, f * D : (f + 1) * D],
+                bank[:].rearrange("p (j m) -> p j m", j=2),
+                gates[2][:, f * D : (f + 1) * D].unsqueeze(1).to_broadcast([P, 2, D]),
+                MULT,
+            )
 
         def gather_late(n, s):
             lo = EARLY + n * HALF
             gather_words(late_part(n, s), s, slots(lo, lo + HALF))
 
         expert(1, banks[0], range(0, 2))
+        gather_adapter(0)
         expert(1, banks[5], range(2, NT))
-        for f in range(F):
-            for s in range(PASSES):
-                gather_words(a_words[:, s * M + f * D : s * M + (f + 1) * D], s, a_slots(f))
-        for n in range(2):
-            for s in range(PASSES):
-                gather_late(n, s)
+        gather_adapter(1)
+        gather_expert(words0, 0)
+        for s in range(PASSES):
+            gather_late(0, s)
         scatter_on_scalar(C, 2 * C, range(NT))
         for u in range(M // P):
             adapter_in(u, banks[(6, 7, 1, 2)[u]])
+        for n in range(2):
+            expert(0, banks[3 + n], range(2 * n, 2 * n + 2))
+        for s in range(PASSES):
+            gather_late(1, s)
+        scatter_on_scalar(0, C, range(NT))
         for f in range(F):
             turn_h(f, banks[3 + f])
-        expert(0, banks[0])
-        scatter_on_scalar(0, C, range(NT))
+        for e in range(2, 4):
+            expert(e, banks[(0, 5)[e - 2]])
+        for j in range(1, NT - 1):
+            scatter_on_scalar(EARLY, SHARE[j], range(j, j + 1))
+        scatter_on_vector(0, EARLY, 4 * C)
+        for e in range(4, 6):
+            expert(e, banks[(6, 7)[e - 4]])
+        scatter_on_scalar(EARLY, SHARE[NT - 1], range(NT - 1, NT))
         nc.vector.quantize_mx(out=h_codes[:].bitcast(FP8X4), scales=h_scales[:], in_=h_in[:])
-        adapter_out(0, banks[6])
-        scatter_z(0)
-        for e in range(2, 6):
-            expert(e, banks[(2, 1, 5, 7)[e - 2]])
-        scatter_on_scalar(EARLY, SHARE, range(1, NT))
-        scatter_on_vector(0, SHARE, 6 * C)
-        expert(6, banks[2])
-        expert(7, banks[1])
-        adapter_out(1, banks[2])
-        scatter_on_vector(0, 6 * C, T)
-        scatter_on_scalar(EARLY, SHARE, range(0, 1))
+        scatter_on_vector(0, 4 * C, 6 * C)
+        for f in range(F):
+            adapter_out_pair(f, banks[1 + f])
+        for j in range(2, NT):
+            adapter_out(j, banks[(0, 5)[j - 2]])
+        for e in range(6, E):
+            expert(e, banks[e])
+        scatter_z([(j, f) for f in range(F) for j in range(2)])
         for j in range(NT):
-            if j > 0:
-                scatter_z(j)
-                if j < NT - 1:
-                    adapter_out(j + 1, banks[2 - j % 2])
-                scatter_on_vector(j, SHARE, T)
+            scatter_on_vector(j, SHARE[j] if j else 6 * C, T)
+            if j >= 2:
+                scatter_z([(j, f) for f in range(F)])
             if j < NT - 1:
                 nc.gpsimd.tensor_tensor(z_sb[j][:], o_sb[j][:], z_sb[j][:], ADD)
                 nc.sync.dma_start(out[j * P : (j + 1) * P, :], z_sb[j][:])

@@ -176,18 +176,18 @@ def tile_moe_mlr_silu_kernel(
 
         load_planes(was_sb[:], wa_scales.rearrange("f s b n -> (f s) b n"))
         load(wa_sb[:], wa_words.rearrange("f s p n -> p (f s) n"))
-        load(w0_sb[:], w_rows[:, 0:PASSES, :])
         for r in range(ROWS):
             load(a_plane1[r:P:32, :], a_planes[ROWS + r : P : 32, :])
+        load(w0_sb[:], w_rows[:, 0:PASSES, :])
         load_ws(1)
-        load(w_pairs[0][:, 0:PASSES, :], w_rows[:, 2 * PASSES : 3 * PASSES, :])
-        load_ws(2)
-        load(wb_sb[:], wb_words.rearrange("f s p n -> p (f s) n"))
-        load(w_pairs[0][:, PASSES:, :], w_rows[:, 3 * PASSES : 4 * PASSES, :])
+        for e in range(2, 4):
+            load(w_pairs[0][:, PASSES * (e - 2) : PASSES * (e - 1), :], w_rows[:, PASSES * e : PASSES * (e + 1), :])
+            load_ws(e)
+        load(w_pairs[1][:], w_rows[:, 4 * PASSES : 6 * PASSES, :])
         load_planes(wbs_sb[:], wb_scales.rearrange("f s b n -> (f s) b n"))
-        for g in range(1, 3):
-            load(w_pairs[g][:], w_rows[:, 2 * PASSES * (g + 1) : 2 * PASSES * (g + 2), :])
-            load_ws(2 + g)
+        load(wb_sb[:], wb_words.rearrange("f s p n -> p (f s) n"))
+        load(w_pairs[2][:], w_rows[:, 6 * PASSES : 8 * PASSES, :])
+        load_ws(4)
 
         def w_plane(e, s):
             g = [2 * e + s in group for group in WS_GROUPS].index(True)

@@ -80,7 +80,7 @@ def tile_moe_mlr_silu_kernel(
         wb_sb = keep.tile([P, F, 2 * N], U8, name="wb_sb", align_bytes=64)
         wbs_sb = keep.tile([P, F, N], U8, name="wbs_sb", align_bytes=64)
         gate_rows = keep.tile([P, P], F32, name="gate_rows")
-        gate_cols = keep.tile([P, 16], F32, name="gate_cols")
+        gate_wide = keep.tile([P, E, P], F32, name="gate_wide")
         gates = [keep.tile([P, N], F32, name="gates%d" % b) for b in range(3)]
         zero_col = keep.tile([P, 1], F32, name="zero_col")
         ident = keep.tile([P, P], F32, name="ident")
@@ -134,7 +134,6 @@ def tile_moe_mlr_silu_kernel(
         for q in range(QUADS):
             load(xs_sb[32 * q : 32 * q + PASSES * ROWS, 0:T], x_scales[:, ROWS * q : ROWS * (q + 1), :])
         nc.sync.dma_start(gate_rows[0:E, :], gate[0].rearrange("(e p) -> e p", p=P))
-        nc.sync.dma_start(gate_rows[E : E + M // P, :], gate2[0].rearrange("(e p) -> e p", p=P))
         load(x_sb[:].rearrange("p (s t) -> p s t", s=PASSES), x_words.rearrange("s p t d -> p s (t d)"))
         nc.sync.dma_start(offs2_sb[:], offs2)
         load_ws(0)
@@ -142,12 +141,13 @@ def tile_moe_mlr_silu_kernel(
         load_w1(1)
 
         nc.tensor.transpose(banks[7][:, 0:P], gate_rows[:], ident[:])
-        nc.scalar.copy(gate_cols[:], banks[7][:, 0:16])
-        for b in range(3):
-            bank = banks[(1, 2, 6)[b]]
+        for b in range(2):
+            group = slice(4 * b, 4 * (b + 1))
+            nc.scalar.copy(gate_wide[:, group, :], banks[7][:, group].unsqueeze(2).to_broadcast([P, 4, P]))
+        for b in range(2):
+            bank = banks[1 + b]
             for u in range(4):
-                col = gate_cols[:, 4 * b + u : 4 * b + u + 1]
-                nc.tensor.transpose(bank[:, u * P : (u + 1) * P], col.to_broadcast([P, P]), ident[:])
+                nc.tensor.transpose(bank[:, u * P : (u + 1) * P], gate_wide[:, 4 * b + u, :], ident[:])
             nc.scalar.copy(gates[b][:], bank[:])
 
         def slots(lo, hi):
@@ -186,6 +186,7 @@ def tile_moe_mlr_silu_kernel(
         load(w_pairs[1][:], w_rows[:, 4 * PASSES : 6 * PASSES, :])
         load_planes(wbs_sb[:], wb_scales.rearrange("f s b n -> (f s) b n"))
         load(wb_sb[:], wb_words.rearrange("f s p n -> p (f s) n"))
+        nc.sync.dma_start(gates[2][:], gate2)
         load(w_pairs[2][:], w_rows[:, 6 * PASSES : 8 * PASSES, :])
         load_ws(4)
 

@@ -25,11 +25,13 @@ QUADS = 4
 ROWS = 4
 M = F * D
 NT = N // P
-EARLY = 2 * C
-WIDE = 1376
-HALF = (T - EARLY) // 2
+PAIR = 2 * C
+EARLY = 6 * C
+KIB = 1024
 WS_GROUPS = (range(1, 5), range(0, 16, 15), range(5, 9), range(9, 13), range(13, 15))
-SHARE = (EARLY, 512, 512, 576)
+Z_PARTS = ((0, 0), (1, 0), (2, 0), (0, 1), (1, 1), (2, 1), (3, 0), (3, 1))
+Z_ORDER = (0, 1, 3, 2, 4, 5, 6, 7)
+LAST = 256
 
 
 def tile_moe_mlr_silu_kernel(
@@ -41,69 +43,69 @@ def tile_moe_mlr_silu_kernel(
         reuse = ctx.enter_context(tc.tile_pool(name="reuse", bufs=1))
         psum = ctx.enter_context(tc.psum_pool(name="psum", bufs=1))
 
+        def kept(shape, dtype, name):
+            return keep.tile(shape, dtype, name=name, align_bytes=64)
+
+        def placed(shape, dtype, name, at):
+            return reuse.tile(shape, dtype, name=name, align_bytes=64, offset=at)
+
         offs_sb = keep.tile([P, T // 16], U16, name="offs_sb")
         offs2_sb = keep.tile([P, M // 16], U16, name="offs2_sb")
-        x_sb = keep.tile([P, PASSES * T], I32, name="x_sb", align_bytes=64)
-        xs_sb = keep.tile([P, WIDE], U8, name="xs_sb", align_bytes=64)
-        e_planes = keep.tile([P, T], U8, name="e_planes", align_bytes=64)
-        words1 = keep.tile([P, PASSES * C], U32, name="words1", align_bytes=64)
-        a_planes = keep.tile([P, M], U8, name="a_planes", align_bytes=64)
-        a_plane1 = keep.tile([P, M], U8, name="a_plane1", align_bytes=64)
+        x_sb = [kept([P, T], I32, "x_sb%d" % s) for s in range(PASSES)]
+        xs_sb = kept([P, T], U8, "xs_sb")
+        early_planes = kept([P, EARLY], U8, "early_planes")
+        a_planes = kept([P, M], U8, "a_planes")
+        a_plane1 = kept([P, M], U8, "a_plane1")
 
-        a_bytes = 4 * PASSES * D
-        w1_halves = [
-            reuse.tile([P, PASSES, 2 * N], U8, name="w1_half%d" % n, align_bytes=64, offset=(0, 2 * a_bytes - 64)[n])
-            for n in range(2)
+        w1_halves = [placed([P, PASSES, 2 * N], U8, "w1_half%d" % n, 2 * KIB * n) for n in range(2)]
+        w_sb = {e: placed([P, PASSES, 4 * N], U8, "w_sb%d" % e, 4 * KIB * max(e, 1)) for e in (0, 2, 3)}
+        w45 = placed([P, 2 * PASSES, 4 * N], U8, "w45", 16 * KIB)
+        for e in range(4, 6):
+            w_sb[e] = w45[:, PASSES * (e - 4) : PASSES * (e - 3), :]
+        for e in range(6, E):
+            w_sb[e] = kept([P, PASSES, 4 * N], U8, "w_sb%d" % e)
+        pair_words = [
+            kept([P, PASSES * PAIR], U32, "pair_words0"),
+            placed([P, PASSES * PAIR], U32, "pair_words1", 0),
+            placed([P, PASSES * PAIR], U32, "pair_words2", 8 * KIB),
+            placed([P, PASSES * PAIR], U32, "pair_words3", 12 * KIB),
         ]
-        a_words = [
-            reuse.tile([P, PASSES * D], U32, name="a_words%d" % f, align_bytes=64, offset=f * a_bytes) for f in range(F)
-        ]
-        words0 = reuse.tile([P, PASSES * C], U32, name="words0", align_bytes=64, offset=2 * a_bytes)
-        late_at = 2 * a_bytes + 4 * PASSES * C
-        w0_at = late_at + 4 * PASSES * HALF
-        w0_sb = reuse.tile([P, PASSES, 4 * N], U8, name="w0_sb", align_bytes=64, offset=w0_at)
-        late_words = [
-            reuse.tile([P, PASSES * HALF], U32, name="late_words%d" % n, align_bytes=64, offset=(late_at, w0_at)[n])
-            for n in range(2)
-        ]
-        w45_at = w0_at + PASSES * 4 * N
-        w_pairs = [
-            keep.tile([P, 2 * PASSES, 4 * N], U8, name="w23", align_bytes=64),
-            reuse.tile([P, 2 * PASSES, 4 * N], U8, name="w45", align_bytes=64, offset=w45_at),
-            keep.tile([P, 2 * PASSES, 4 * N], U8, name="w67", align_bytes=64),
-        ]
-        h_codes = reuse.tile([P, M], U32, name="h_codes", align_bytes=64, offset=w45_at)
-        h_rows = [keep.tile([P, D // P, H], BF16, name="h_rows%d" % f) for f in range(F)]
-        ws_sb = [keep.tile([P, N], U8, name="ws_sb%d" % g, align_bytes=64) for g in range(len(WS_GROUPS))]
-        wa_sb = keep.tile([P, F * PASSES, 2 * H], U8, name="wa_sb", align_bytes=64)
-        was_sb = keep.tile([P, F * PASSES, H], U8, name="was_sb", align_bytes=64)
-        wb_sb = keep.tile([P, F, 2 * N], U8, name="wb_sb", align_bytes=64)
-        wbs_sb = keep.tile([P, F, N], U8, name="wbs_sb", align_bytes=64)
-        gate_rows = keep.tile([P, P], F32, name="gate_rows")
-        gate_wide = keep.tile([P, E, P], F32, name="gate_wide")
-        gates = [keep.tile([P, N], F32, name="gates%d" % b) for b in range(3)]
-        zero_col = keep.tile([P, 1], F32, name="zero_col")
-        ident = keep.tile([P, P], F32, name="ident")
-        o_sb = [keep.tile([P, T], F32, name="o_sb%d" % j) for j in range(NT)]
-        z_sb = [keep.tile([P, T], F32, name="z_sb%d" % j) for j in range(NT)]
-        y = keep.tile([P, NT, T], F32, name="y")
-        z = keep.tile([P, NT, M], F32, name="z")
-        h_in = keep.tile([P, 4 * M], BF16, name="h_in", align_bytes=64)
-        h_scales = keep.tile([P, M], U8, name="h_scales", align_bytes=64)
+        a_words = [placed([P, PASSES * D], U32, "a_words%d" % f, 2 * KIB * (f + 1)) for f in range(F)]
+        late_planes = placed([P, T - EARLY], U8, "late_planes", 10 * KIB)
+
+        ws_sb = [kept([P, N], U8, "ws_sb%d" % g) for g in range(len(WS_GROUPS))]
+        wa_sb = kept([P, F * PASSES, 2 * H], U8, "wa_sb")
+        was_sb = kept([P, F * PASSES, H], U8, "was_sb")
+        wb_sb = kept([P, F, 2 * N], U8, "wb_sb")
+        wbs_sb = kept([P, F, N], U8, "wbs_sb")
+        h_rows = [kept([P, D // P, H], BF16, "h_rows%d" % f) for f in range(F)]
+        h_in = [kept([P, 4 * D], BF16, "h_in%d" % f) for f in range(F)]
+        h_codes = [placed([P, D], U32, "h_codes%d" % f, (16 + f) * KIB) for f in range(F)]
+        h_scales = [kept([P, D], U8, "h_scales%d" % f) for f in range(F)]
+        gate_rows = kept([P, P], F32, "gate_rows")
+        gate_wide = kept([P, E, P], F32, "gate_wide")
+        gates = [kept([P, N], F32, "gates%d" % b) for b in range(2)]
+        gate2_sb = kept([P, M], F32, "gate2_sb")
+        zero_col = kept([P, 1], F32, "zero_col")
+        ident = kept([P, P], F32, "ident")
+        o_sb = [kept([P, T], F32, "o_sb%d" % j) for j in range(NT)]
+        z_sb = [kept([P, T], F32, "z_sb%d" % j) for j in range(NT)]
+        y = kept([P, NT, T], F32, "y")
+        z = kept([P, len(Z_PARTS), D], F32, "z")
         banks = [psum.tile([P, N], F32, name="bank%d" % b) for b in range(8)]
 
         def zero(tile_ap):
             nc.gpsimd.memset(tile_ap.bitcast(I32), 0)
 
-        zero(xs_sb[:, 0:T])
+        zero(xs_sb[:])
         nc.gpsimd.memset(gate_rows[:], 0.0)
         nc.gpsimd.memset(zero_col[:], 0.0)
         zero(ws_sb[0][:])
         make_identity(nc, ident[:])
-        zero(was_sb[:].rearrange("p a n -> p (a n)"))
-        zero(a_plane1[:])
         for g in range(1, len(WS_GROUPS)):
             zero(ws_sb[g][:])
+        zero(was_sb[:].rearrange("p a n -> p (a n)"))
+        zero(a_plane1[:])
         zero(wbs_sb[:].rearrange("p a n -> p (a n)"))
         nc.scalar.activation(z_sb[0][:], zero_col[:].to_broadcast([P, T]), SILU)
         for j in range(1, NT):
@@ -127,25 +129,35 @@ def tile_moe_mlr_silu_kernel(
                     ws_rows[group.start : group.stop : group.step, ROWS * q : ROWS * (q + 1), :],
                 )
 
+        def load_w(e):
+            load(w_sb[e][:], w_rows[:, PASSES * e : PASSES * (e + 1), :])
+
         def load_w1(n):
             load(w1_halves[n][:], w_rows[:, PASSES : 2 * PASSES, 2 * N * n : 2 * N * (n + 1)])
 
         nc.sync.dma_start(offs_sb[:], offs)
         for q in range(QUADS):
-            load(xs_sb[32 * q : 32 * q + PASSES * ROWS, 0:T], x_scales[:, ROWS * q : ROWS * (q + 1), :])
+            load(xs_sb[32 * q : 32 * q + PASSES * ROWS, :], x_scales[:, ROWS * q : ROWS * (q + 1), :])
         nc.sync.dma_start(gate_rows[0:E, :], gate[0].rearrange("(e p) -> e p", p=P))
-        load(x_sb[:].rearrange("p (s t) -> p s t", s=PASSES), x_words.rearrange("s p t d -> p s (t d)"))
+        for s in range(PASSES):
+            load(x_sb[s][:], x_words[s].rearrange("p t d -> p (t d)"))
         nc.sync.dma_start(offs2_sb[:], offs2)
-        load_ws(0)
         load_w1(0)
+        load_ws(0)
         load_w1(1)
+        load_w(0)
+        load_ws(1)
+        load_w(2)
+        load_ws(2)
+        load_planes(was_sb[:], wa_scales.rearrange("f s b n -> (f s) b n"))
+        load(wa_sb[:], wa_words.rearrange("f s p n -> p (f s) n"))
 
         nc.tensor.transpose(banks[7][:, 0:P], gate_rows[:], ident[:])
         for b in range(2):
             group = slice(4 * b, 4 * (b + 1))
             nc.scalar.copy(gate_wide[:, group, :], banks[7][:, group].unsqueeze(2).to_broadcast([P, 4, P]))
         for b in range(2):
-            bank = banks[1 + b]
+            bank = banks[5 + b]
             for u in range(4):
                 nc.tensor.transpose(bank[:, u * P : (u + 1) * P], gate_wide[:, 4 * b + u, :], ident[:])
             nc.scalar.copy(gates[b][:], bank[:])
@@ -156,68 +168,36 @@ def tile_moe_mlr_silu_kernel(
         def a_slots(f):
             return offs2_sb[:, f * D // 16 : (f + 1) * D // 16]
 
-        def gather_words(dst, s, offsets):
-            nc.vector.tensor_copy(dst, x_sb[:, s * T : (s + 1) * T].bitcast(U32).indirect(offsets))
-
-        def gather_bytes(dst, window, offsets):
-            nc.vector.tensor_copy(dst, window.indirect(offsets))
-
-        def gather_expert(dst, e):
+        def gather_words(dst, offsets):
+            width = dst.shape[1] // PASSES
             for s in range(PASSES):
-                gather_words(dst[:, s * C : (s + 1) * C], s, slots(e * C, (e + 1) * C))
+                nc.vector.tensor_copy(dst[:, s * width : (s + 1) * width], x_sb[s][:].bitcast(U32).indirect(offsets))
 
-        def gather_adapter(f):
-            for s in range(PASSES):
-                gather_words(a_words[f][:, s * D : (s + 1) * D], s, a_slots(f))
+        def gather_bytes(dst, offsets):
+            nc.vector.tensor_copy(dst[:], xs_sb[:].indirect(offsets))
 
-        gather_bytes(e_planes[:], xs_sb[:], offs_sb[:])
-        gather_expert(words1, 1)
-        gather_bytes(a_planes[:], xs_sb[:, 0:T], offs2_sb[:])
-
-        load_planes(was_sb[:], wa_scales.rearrange("f s b n -> (f s) b n"))
-        load(wa_sb[:], wa_words.rearrange("f s p n -> p (f s) n"))
-        for r in range(ROWS):
-            load(a_plane1[r:P:32, :], a_planes[ROWS + r : P : 32, :])
-        load(w0_sb[:], w_rows[:, 0:PASSES, :])
-        load_ws(1)
-        for e in range(2, 4):
-            load(w_pairs[0][:, PASSES * (e - 2) : PASSES * (e - 1), :], w_rows[:, PASSES * e : PASSES * (e + 1), :])
-            load_ws(e)
-        load(w_pairs[1][:], w_rows[:, 4 * PASSES : 6 * PASSES, :])
-        load_planes(wbs_sb[:], wb_scales.rearrange("f s b n -> (f s) b n"))
-        load(wb_sb[:], wb_words.rearrange("f s p n -> p (f s) n"))
-        nc.sync.dma_start(gates[2][:], gate2)
-        load(w_pairs[2][:], w_rows[:, 6 * PASSES : 8 * PASSES, :])
-        load_ws(4)
+        def gather_pair(n):
+            gather_words(pair_words[n], slots(n * PAIR, (n + 1) * PAIR))
 
         def w_plane(e, s):
             g = [2 * e + s in group for group in WS_GROUPS].index(True)
             return ws_sb[g][ROWS * list(WS_GROUPS[g]).index(2 * e + s) : P, :]
 
-        def late_part(n, s):
-            return late_words[n][:, s * HALF : (s + 1) * HALF]
-
         def expert(e, bank, tiles=range(NT)):
-            if e < 2:
-                w_sb = w0_sb[:]
-                words = [(words0, words1)[e][:, s * C : (s + 1) * C] for s in range(PASSES)]
-            else:
-                w_sb = w_pairs[e // 2 - 1][:, PASSES * (e % 2) : PASSES * (e % 2 + 1), :]
-                first = (e - 2) % 3 * C
-                words = [late_part((e - 2) // 3, s)[:, first : first + C] for s in range(PASSES)]
+            planes, first = (early_planes, e * C) if e * C < EARLY else (late_planes, e * C - EARLY)
             for n, j in enumerate(tiles):
-                cols = slice(j * P, (j + 1) * P)
                 for s in range(PASSES):
                     if e == 1:
                         w_tile = w1_halves[j // 2][:, s, 4 * P * (j % 2) : 4 * P * (j % 2 + 1)]
                     else:
-                        w_tile = w_sb[:, s, 4 * P * j : 4 * P * (j + 1)]
+                        w_tile = w_sb[e][:, s, 4 * P * j : 4 * P * (j + 1)]
+                    at = s * PAIR + e % 2 * C
                     nc.tensor.matmul_mx(
                         out=bank[:, n * C : (n + 1) * C],
                         lhsT=w_tile.bitcast(FP8X4),
-                        lhsT_scale=w_plane(e, s)[:, cols],
-                        rhs=words[s].bitcast(FP8X4),
-                        rhs_scale=e_planes[ROWS * s : P, e * C : (e + 1) * C],
+                        lhsT_scale=w_plane(e, s)[:, j * P : (j + 1) * P],
+                        rhs=pair_words[e // 2][:, at : at + C].bitcast(FP8X4),
+                        rhs_scale=planes[ROWS * s : P, first : first + C],
                         start=(s == 0),
                         stop=(s == PASSES - 1),
                     )
@@ -229,16 +209,15 @@ def tile_moe_mlr_silu_kernel(
                 MULT,
             )
 
-        def scatter_on_scalar(lo, hi, tiles):
-            for j in tiles:
-                nc.scalar.activation(o_sb[j][:].indirect(slots(lo, hi)), y[:, j, lo:hi], COPY)
+        def scatter_on_scalar(j, lo, hi):
+            nc.scalar.activation(o_sb[j][:].indirect(slots(lo * C, hi * C)), y[:, j, lo * C : hi * C], COPY)
 
         def scatter_on_vector(j, lo, hi):
-            nc.vector.tensor_copy(o_sb[j][:].indirect(slots(lo, hi)), y[:, j, lo:hi])
+            nc.vector.tensor_copy(o_sb[j][:].indirect(slots(lo * C, hi * C)), y[:, j, lo * C : hi * C])
 
-        def scatter_z(parts):
-            for j, f in parts:
-                nc.scalar.activation(z_sb[j][:].indirect(a_slots(f)), z[:, j, f * D : (f + 1) * D], COPY)
+        def scatter_z(part):
+            j, f = Z_PARTS[part]
+            nc.scalar.activation(z_sb[j][:].indirect(a_slots(f)), z[:, part, :], COPY)
 
         def adapter_in(u, sums):
             f = u * P // D
@@ -265,85 +244,92 @@ def tile_moe_mlr_silu_kernel(
                 for v in range(2):
                     at = v * D + b * P
                     nc.tensor.transpose(turned[:, at : at + P], pairs[:, v * P : (v + 1) * P], ident[:])
-            nc.scalar.copy(
-                h_in[:, 4 * f * D : 4 * (f + 1) * D].bitcast(F32).rearrange("p (m v) -> p m v", v=2),
+            nc.vector.tensor_copy(
+                h_in[f][:].bitcast(F32).rearrange("p (m v) -> p m v", v=2),
                 turned[:].rearrange("p (v m) -> p m v", v=2),
             )
 
-        def multiply_h(j, f, sums):
-            cols = slice(f * D, (f + 1) * D)
-            nc.tensor.matmul_mx(
-                out=sums,
-                lhsT=wb_sb[:, f, 2 * P * j : 2 * P * (j + 1)].bitcast(FP4X4),
-                lhsT_scale=wbs_sb[:, f, j * P : (j + 1) * P],
-                rhs=h_codes[:, cols].bitcast(FP8X4),
-                rhs_scale=h_scales[:, cols],
-                start=True,
-                stop=True,
-            )
+        def quantize_h(f):
+            nc.vector.quantize_mx(out=h_codes[f][:].bitcast(FP8X4), scales=h_scales[f][:], in_=h_in[f][:])
 
-        def adapter_out(j, bank):
-            for f in range(F):
-                multiply_h(j, f, bank[:, f * D : (f + 1) * D])
-            nc.vector.tensor_tensor(z[:, j, :], bank[:], gates[2][:], MULT)
+        def adapter_out(first, bank):
+            for n in range(2):
+                j, f = Z_PARTS[first + n]
+                nc.tensor.matmul_mx(
+                    out=bank[:, n * D : (n + 1) * D],
+                    lhsT=wb_sb[:, f, 2 * P * j : 2 * P * (j + 1)].bitcast(FP4X4),
+                    lhsT_scale=wbs_sb[:, f, j * P : (j + 1) * P],
+                    rhs=h_codes[f][:].bitcast(FP8X4),
+                    rhs_scale=h_scales[f][:],
+                    start=True,
+                    stop=True,
+                )
+            if Z_PARTS[first][1] == f:
+                q = gate2_sb[:, f * D : (f + 1) * D].unsqueeze(1).to_broadcast([P, 2, D])
+            else:
+                q = gate2_sb[:].rearrange("p (f m) -> p f m", f=F)
+            nc.vector.tensor_tensor(z[:, first : first + 2, :], bank[:].rearrange("p (j m) -> p j m", j=2), q, MULT)
 
-        def adapter_out_pair(f, bank):
-            for j in range(2):
-                multiply_h(j, f, bank[:, j * D : (j + 1) * D])
-            nc.vector.tensor_tensor(
-                z[:, 0:2, f * D : (f + 1) * D],
-                bank[:].rearrange("p (j m) -> p j m", j=2),
-                gates[2][:, f * D : (f + 1) * D].unsqueeze(1).to_broadcast([P, 2, D]),
-                MULT,
-            )
+        gather_bytes(early_planes, slots(0, EARLY))
+        gather_pair(0)
+        gather_bytes(a_planes, offs2_sb[:])
 
-        def gather_late(n, s):
-            lo = EARLY + n * HALF
-            gather_words(late_part(n, s), s, slots(lo, lo + HALF))
+        for r in range(ROWS):
+            load(a_plane1[r:P:32, :], a_planes[ROWS + r : P : 32, :])
+        load_w(3)
+        load_ws(3)
+        load(w45[:], w_rows[:, 4 * PASSES : 6 * PASSES, :])
+        load_w(6)
+        load_ws(4)
+        load(wb_sb[:], wb_words.rearrange("f s p n -> p (f s) n"))
+        load_planes(wbs_sb[:], wb_scales.rearrange("f s b n -> (f s) b n"))
+        nc.sync.dma_start(gate2_sb[:], gate2)
+        load_w(7)
 
         expert(1, banks[0], range(0, 2))
-        gather_adapter(0)
-        expert(1, banks[5], range(2, NT))
-        gather_adapter(1)
-        gather_expert(words0, 0)
-        for s in range(PASSES):
-            gather_late(0, s)
-        scatter_on_scalar(C, 2 * C, range(NT))
-        for u in range(M // P):
-            adapter_in(u, banks[(6, 7, 1, 2)[u]])
+        gather_pair(1)
+        expert(1, banks[1], range(2, NT))
+        gather_words(a_words[0], a_slots(0))
         for n in range(2):
-            expert(0, banks[3 + n], range(2 * n, 2 * n + 2))
-        for s in range(PASSES):
-            gather_late(1, s)
-        scatter_on_scalar(0, C, range(NT))
-        for f in range(F):
-            turn_h(f, banks[3 + f])
-        for e in range(2, 4):
-            expert(e, banks[(0, 5)[e - 2]])
-        for j in range(1, NT - 1):
-            scatter_on_scalar(EARLY, SHARE[j], range(j, j + 1))
-        scatter_on_vector(0, EARLY, 4 * C)
-        for e in range(4, 6):
-            expert(e, banks[(6, 7)[e - 4]])
-        scatter_on_scalar(EARLY, SHARE[NT - 1], range(NT - 1, NT))
-        nc.vector.quantize_mx(out=h_codes[:].bitcast(FP8X4), scales=h_scales[:], in_=h_in[:])
-        scatter_on_vector(0, 4 * C, 6 * C)
-        for f in range(F):
-            adapter_out_pair(f, banks[1 + f])
+            expert(0, banks[2 + n], range(2 * n, 2 * n + 2))
+        gather_words(a_words[1], a_slots(1))
+        expert(2, banks[4])
+        gather_pair(2)
+        gather_bytes(late_planes, slots(EARLY, T))
+        for e in (1, 0):
+            for j in range(NT):
+                scatter_on_scalar(j, e, e + 1)
+        for j in range(2):
+            scatter_on_scalar(j, 2, 3)
         for j in range(2, NT):
-            adapter_out(j, banks[(0, 5)[j - 2]])
-        for e in range(6, E):
-            expert(e, banks[e])
-        scatter_z([(j, f) for f in range(F) for j in range(2)])
+            scatter_on_vector(j, 2, 3)
+        for u in range(M // P):
+            adapter_in(u, banks[(5, 6, 7, 1)[u]])
+        expert(3, banks[0])
+        gather_pair(3)
+        turn_h(0, banks[0])
+        for e in range(4, 6):
+            expert(e, banks[e - 2])
+        for j in (0, 3):
+            scatter_on_scalar(j, 3, 4)
+        for j in (1, 2):
+            scatter_on_scalar(j, 3, 5)
+        quantize_h(0)
+        turn_h(1, banks[2])
+        expert(6, banks[1])
+        quantize_h(1)
+        for b in range(NT):
+            adapter_out(2 * b, banks[4 + b])
+        expert(7, banks[4])
+        for part in Z_ORDER:
+            scatter_z(part)
         for j in range(NT):
-            scatter_on_vector(j, SHARE[j] if j else 6 * C, T)
-            if j >= 2:
-                scatter_z([(j, f) for f in range(F)])
+            scatter_on_vector(j, (4, 5, 5, 4)[j], E)
             if j < NT - 1:
                 nc.gpsimd.tensor_tensor(z_sb[j][:], o_sb[j][:], z_sb[j][:], ADD)
                 nc.sync.dma_start(out[j * P : (j + 1) * P, :], z_sb[j][:])
         j = NT - 1
-        for lo in range(0, T, 256):
-            cols = slice(lo, lo + 256)
+        for lo in range(0, T, LAST):
+            cols = slice(lo, lo + LAST)
             nc.vector.tensor_tensor(o_sb[j - 1][:, cols], o_sb[j][:, cols], z_sb[j][:, cols], ADD)
             nc.sync.dma_start(out[j * P : (j + 1) * P, cols], o_sb[j - 1][:, cols])

@@ -108,15 +108,18 @@ def tile_moe_mlr_silu_kernel(
         zero(a_plane1[:])
         zero(wbs_sb[:].rearrange("p a n -> p (a n)"))
         nc.scalar.activation(z_sb[0][:], zero_col[:].to_broadcast([P, T]), SILU)
-        for j in range(1, NT):
-            nc.gpsimd.memset(z_sb[j][:], 0.0)
+        nc.gpsimd.memset(z_sb[1][:], 0.0)
 
-        def load(dst, src):
-            nc.sync.dma_start(dst.bitcast(I32), src.bitcast(I32))
+        def load(dst, src, queue=nc.sync):
+            queue.dma_start(dst.bitcast(I32), src.bitcast(I32))
 
-        def load_planes(dst, src):
+        def load_planes(dst, src, queue=nc.sync):
             for r in range(ROWS):
-                load(dst[r:P:32, :, :], src[:, r :: ROWS, :].rearrange("a q n -> q a n"))
+                load(dst[r:P:32, :, :], src[:, r :: ROWS, :].rearrange("a q n -> q a n"), queue)
+
+        load_planes(was_sb[:], wa_scales.rearrange("f s b n -> (f s) b n"), nc.gpsimd)
+        for j in range(2, NT):
+            nc.gpsimd.memset(z_sb[j][:], 0.0)
 
         w_rows = w_words.rearrange("e s p n d -> p (e s) (n d)")
         ws_rows = w_scales.rearrange("e s b n -> (e s) b n")
@@ -149,7 +152,6 @@ def tile_moe_mlr_silu_kernel(
         load_ws(1)
         load_w(2)
         load_ws(2)
-        load_planes(was_sb[:], wa_scales.rearrange("f s b n -> (f s) b n"))
         load(wa_sb[:], wa_words.rearrange("f s p n -> p (f s) n"))
 
         nc.tensor.transpose(banks[7][:, 0:P], gate_rows[:], ident[:])
@@ -303,10 +305,10 @@ def tile_moe_mlr_silu_kernel(
             scatter_on_scalar(j, 2, 3)
         for j in range(2, NT):
             scatter_on_vector(j, 2, 3)
-        for u in range(M // P):
-            adapter_in(u, banks[(5, 6, 7, 1)[u]])
         expert(3, banks[0])
         gather_pair(3)
+        for u in range(M // P):
+            adapter_in(u, banks[(5, 6, 7, 1)[u]])
         turn_h(0, banks[0])
         for e in range(4, 6):
             expert(e, banks[e - 2])

@@ -31,6 +31,7 @@ KIB = 1024
 WS_GROUPS = (range(1, 5), range(0, 16, 15), range(5, 9), range(9, 13), range(13, 15))
 Z_PARTS = ((0, 0), (1, 0), (2, 0), (0, 1), (1, 1), (2, 1), (3, 0), (3, 1))
 Z_ORDER = (0, 1, 3, 2, 4, 5, 6, 7)
+LATE = (4 * C, 4 * C + 32, 5 * C, 4 * C)
 LAST = 256
 
 
@@ -59,7 +60,7 @@ def tile_moe_mlr_silu_kernel(
 
         w1_halves = [placed([P, PASSES, 2 * N], U8, "w1_half%d" % n, 2 * KIB * n) for n in range(2)]
         w_sb = {e: placed([P, PASSES, 4 * N], U8, "w_sb%d" % e, 4 * KIB * max(e, 1)) for e in (0, 2, 3)}
-        w45 = placed([P, 2 * PASSES, 4 * N], U8, "w45", 16 * KIB)
+        w45 = kept([P, 2 * PASSES, 4 * N], U8, "w45")
         for e in range(4, 6):
             w_sb[e] = w45[:, PASSES * (e - 4) : PASSES * (e - 3), :]
         for e in range(6, E):
@@ -68,10 +69,10 @@ def tile_moe_mlr_silu_kernel(
             kept([P, PASSES * PAIR], U32, "pair_words0"),
             placed([P, PASSES * PAIR], U32, "pair_words1", 0),
             placed([P, PASSES * PAIR], U32, "pair_words2", 8 * KIB),
-            placed([P, PASSES * PAIR], U32, "pair_words3", 12 * KIB),
+            placed([P, PASSES * PAIR], U32, "pair_words3", 10 * KIB),
         ]
         a_words = [placed([P, PASSES * D], U32, "a_words%d" % f, 2 * KIB * (f + 1)) for f in range(F)]
-        late_planes = placed([P, T - EARLY], U8, "late_planes", 10 * KIB)
+        late_planes = placed([P, T - EARLY], U8, "late_planes", 12 * KIB)
 
         ws_sb = [kept([P, N], U8, "ws_sb%d" % g) for g in range(len(WS_GROUPS))]
         wa_sb = kept([P, F * PASSES, 2 * H], U8, "wa_sb")
@@ -80,7 +81,7 @@ def tile_moe_mlr_silu_kernel(
         wbs_sb = kept([P, F, N], U8, "wbs_sb")
         h_rows = [kept([P, D // P, H], BF16, "h_rows%d" % f) for f in range(F)]
         h_in = [kept([P, 4 * D], BF16, "h_in%d" % f) for f in range(F)]
-        h_codes = [placed([P, D], U32, "h_codes%d" % f, (16 + f) * KIB) for f in range(F)]
+        h_codes = [kept([P, D], U32, "h_codes%d" % f) for f in range(F)]
         h_scales = [kept([P, D], U8, "h_scales%d" % f) for f in range(F)]
         gate_rows = kept([P, P], F32, "gate_rows")
         gate_wide = kept([P, E, P], F32, "gate_wide")
@@ -108,7 +109,6 @@ def tile_moe_mlr_silu_kernel(
         zero(a_plane1[:])
         zero(wbs_sb[:].rearrange("p a n -> p (a n)"))
         nc.scalar.activation(z_sb[0][:], zero_col[:].to_broadcast([P, T]), SILU)
-        nc.gpsimd.memset(z_sb[1][:], 0.0)
 
         def load(dst, src, queue=nc.sync):
             queue.dma_start(dst.bitcast(I32), src.bitcast(I32))
@@ -118,7 +118,8 @@ def tile_moe_mlr_silu_kernel(
                 load(dst[r:P:32, :, :], src[:, r :: ROWS, :].rearrange("a q n -> q a n"), queue)
 
         load_planes(was_sb[:], wa_scales.rearrange("f s b n -> (f s) b n"), nc.gpsimd)
-        for j in range(2, NT):
+        load_planes(wbs_sb[:], wb_scales.rearrange("f s b n -> (f s) b n"), nc.gpsimd)
+        for j in range(1, NT):
             nc.gpsimd.memset(z_sb[j][:], 0.0)
 
         w_rows = w_words.rearrange("e s p n d -> p (e s) (n d)")
@@ -212,10 +213,10 @@ def tile_moe_mlr_silu_kernel(
             )
 
         def scatter_on_scalar(j, lo, hi):
-            nc.scalar.activation(o_sb[j][:].indirect(slots(lo * C, hi * C)), y[:, j, lo * C : hi * C], COPY)
+            nc.scalar.activation(o_sb[j][:].indirect(slots(lo, hi)), y[:, j, lo:hi], COPY)
 
         def scatter_on_vector(j, lo, hi):
-            nc.vector.tensor_copy(o_sb[j][:].indirect(slots(lo * C, hi * C)), y[:, j, lo * C : hi * C])
+            nc.vector.tensor_copy(o_sb[j][:].indirect(slots(lo, hi)), y[:, j, lo:hi])
 
         def scatter_z(part):
             j, f = Z_PARTS[part]
@@ -284,7 +285,6 @@ def tile_moe_mlr_silu_kernel(
         load_w(6)
         load_ws(4)
         load(wb_sb[:], wb_words.rearrange("f s p n -> p (f s) n"))
-        load_planes(wbs_sb[:], wb_scales.rearrange("f s b n -> (f s) b n"))
         nc.sync.dma_start(gate2_sb[:], gate2)
         load_w(7)
 
@@ -296,37 +296,35 @@ def tile_moe_mlr_silu_kernel(
             expert(0, banks[2 + n], range(2 * n, 2 * n + 2))
         gather_words(a_words[1], a_slots(1))
         expert(2, banks[4])
-        gather_pair(2)
-        gather_bytes(late_planes, slots(EARLY, T))
+        for n in range(2, E // 2):
+            gather_pair(n)
         for e in (1, 0):
             for j in range(NT):
-                scatter_on_scalar(j, e, e + 1)
-        for j in range(2):
-            scatter_on_scalar(j, 2, 3)
-        for j in range(2, NT):
-            scatter_on_vector(j, 2, 3)
-        expert(3, banks[0])
-        gather_pair(3)
+                scatter_on_scalar(j, e * C, (e + 1) * C)
+        for n in range(2):
+            expert(3, banks[2 * n], range(2 * n, 2 * n + 2))
+        gather_bytes(late_planes, slots(EARLY, T))
         for u in range(M // P):
             adapter_in(u, banks[(5, 6, 7, 1)[u]])
-        turn_h(0, banks[0])
-        for e in range(4, 6):
-            expert(e, banks[e - 2])
-        for j in (0, 3):
-            scatter_on_scalar(j, 3, 4)
-        for j in (1, 2):
-            scatter_on_scalar(j, 3, 5)
+        scatter_on_vector(2, 2 * C, 4 * C)
+        for f in range(F):
+            turn_h(f, banks[2 * f])
         quantize_h(0)
-        turn_h(1, banks[2])
-        expert(6, banks[1])
+        expert(4, banks[3])
         quantize_h(1)
-        for b in range(NT):
-            adapter_out(2 * b, banks[4 + b])
-        expert(7, banks[4])
+        for j in (0, 3, 1):
+            scatter_on_scalar(j, 2 * C, LATE[j])
+        scatter_on_scalar(2, 4 * C, LATE[2])
+        for e in range(5, 7):
+            expert(e, banks[e - 1])
+        for b in range(NT - 1):
+            adapter_out(2 * b, banks[(6, 7, 1)[b]])
+        expert(7, banks[6])
+        adapter_out(2 * (NT - 1), banks[0])
         for part in Z_ORDER:
             scatter_z(part)
         for j in range(NT):
-            scatter_on_vector(j, (4, 5, 5, 4)[j], E)
+            scatter_on_vector(j, LATE[j], T)
             if j < NT - 1:
                 nc.gpsimd.tensor_tensor(z_sb[j][:], o_sb[j][:], z_sb[j][:], ADD)
                 nc.sync.dma_start(out[j * P : (j + 1) * P, :], z_sb[j][:])

@@ -68,7 +68,7 @@ def tile_moe_mlr_silu_kernel(
         pair_words = [
             kept([P, PASSES * PAIR], U32, "pair_words0"),
             placed([P, PASSES * PAIR], U32, "pair_words1", 0),
-            placed([P, PASSES * PAIR], U32, "pair_words2", 8 * KIB),
+            placed([P, PASSES * PAIR], U32, "pair_words2", 6 * KIB),
             placed([P, PASSES * PAIR], U32, "pair_words3", 10 * KIB),
         ]
         a_words = [placed([P, PASSES * D], U32, "a_words%d" % f, 2 * KIB * (f + 1)) for f in range(F)]
@@ -96,16 +96,15 @@ def tile_moe_mlr_silu_kernel(
         banks = [psum.tile([P, N], F32, name="bank%d" % b) for b in range(8)]
 
         def zero(tile_ap):
-            nc.gpsimd.memset(tile_ap.bitcast(I32), 0)
+            nc.vector.memset(tile_ap.bitcast(I32), 0)
 
-        zero(xs_sb[:])
+        nc.gpsimd.memset(xs_sb[:].bitcast(I32), 0)
         nc.gpsimd.memset(gate_rows[:], 0.0)
         nc.gpsimd.memset(zero_col[:], 0.0)
-        zero(ws_sb[0][:])
         make_identity(nc, ident[:])
-        for g in range(1, len(WS_GROUPS)):
-            zero(ws_sb[g][:])
         zero(was_sb[:].rearrange("p a n -> p (a n)"))
+        for g in range(len(WS_GROUPS)):
+            zero(ws_sb[g][:])
         zero(a_plane1[:])
         zero(wbs_sb[:].rearrange("p a n -> p (a n)"))
         nc.scalar.activation(z_sb[0][:], zero_col[:].to_broadcast([P, T]), SILU)
@@ -295,18 +294,19 @@ def tile_moe_mlr_silu_kernel(
         for n in range(2):
             expert(0, banks[2 + n], range(2 * n, 2 * n + 2))
         gather_words(a_words[1], a_slots(1))
+        gather_pair(2)
         expert(2, banks[4])
-        for n in range(2, E // 2):
-            gather_pair(n)
+        gather_pair(3)
         for e in (1, 0):
             for j in range(NT):
                 scatter_on_scalar(j, e * C, (e + 1) * C)
+        scatter_on_vector(2, 2 * C, 3 * C)
         for n in range(2):
             expert(3, banks[2 * n], range(2 * n, 2 * n + 2))
         gather_bytes(late_planes, slots(EARLY, T))
         for u in range(M // P):
             adapter_in(u, banks[(5, 6, 7, 1)[u]])
-        scatter_on_vector(2, 2 * C, 4 * C)
+        scatter_on_vector(2, 3 * C, 4 * C)
         for f in range(F):
             turn_h(f, banks[2 * f])
         quantize_h(0)

@@ -31,7 +31,7 @@ KIB = 1024
 WS_GROUPS = (range(1, 5), range(0, 16, 15), range(5, 9), range(9, 13), range(13, 15))
 Z_PARTS = ((0, 0), (1, 0), (2, 0), (0, 1), (1, 1), (2, 1), (3, 0), (3, 1))
 Z_ORDER = (0, 1, 3, 2, 4, 5, 6, 7)
-LATE = (4 * C, 4 * C + 32, 5 * C, 4 * C)
+LATE = (4 * C, 4 * C, 5 * C + 64, 4 * C)
 LAST = 256
 
 
@@ -314,9 +314,9 @@ def tile_moe_mlr_silu_kernel(
         quantize_h(1)
         for j in (0, 3, 1):
             scatter_on_scalar(j, 2 * C, LATE[j])
+        expert(5, banks[4])
         scatter_on_scalar(2, 4 * C, LATE[2])
-        for e in range(5, 7):
-            expert(e, banks[e - 1])
+        expert(6, banks[5])
         for b in range(NT - 1):
             adapter_out(2 * b, banks[(6, 7, 1)[b]])
         expert(7, banks[6])

from contextlib import ExitStack

import concourse.mybir as mybir
from concourse.masks import make_identity

K, T, E, C, F, D, H, N = 1024, 1024, 8, 128, 2, 256, 512, 512
FLOPS = 2 * (K * N * E * C + K * H * F * D + H * N * F * D)

F32 = mybir.dt.float32
BF16 = mybir.dt.bfloat16
I32 = mybir.dt.int32
U32 = mybir.dt.uint32
U16 = mybir.dt.uint16
U8 = mybir.dt.uint8
FP8X4 = mybir.dt.float8_e4m3fn_x4
FP4X4 = mybir.dt.float4_e2m1fn_x4
COPY = mybir.ActivationFunctionType.Copy
SILU = mybir.ActivationFunctionType.Silu
ADD = mybir.AluOpType.add
MULT = mybir.AluOpType.mult

P = 128
PASSES = K // 512
QUADS = 4
ROWS = 4
M = F * D
NT = N // P
PAIR = 2 * C
EARLY = 6 * C
KIB = 1024
WS_GROUPS = (range(1, 5), range(0, 16, 15), range(5, 9), range(9, 13), range(13, 15))
Z_PARTS = ((0, 0), (1, 0), (2, 0), (0, 1), (1, 1), (2, 1), (3, 0), (3, 1))
Z_ORDER = (0, 1, 3, 2, 4, 5, 6, 7)
LATE = (4 * C, 4 * C, 5 * C + 64, 4 * C)
LAST = 256


def tile_moe_mlr_silu_kernel(
    tc, x_words, x_scales, w_words, w_scales, wa_words, wa_scales, wb_words, wb_scales, gate, gate2, offs, offs2, out
):
    nc = tc.nc
    with ExitStack() as ctx:
        keep = ctx.enter_context(tc.tile_pool(name="keep", bufs=1))
        reuse = ctx.enter_context(tc.tile_pool(name="reuse", bufs=1))
        psum = ctx.enter_context(tc.psum_pool(name="psum", bufs=1))

        def kept(shape, dtype, name):
            return keep.tile(shape, dtype, name=name, align_bytes=64)

        def placed(shape, dtype, name, at):
            return reuse.tile(shape, dtype, name=name, align_bytes=64, offset=at)

        offs_sb = keep.tile([P, T // 16], U16, name="offs_sb")
        offs2_sb = keep.tile([P, M // 16], U16, name="offs2_sb")
        x_sb = [kept([P, T], I32, "x_sb%d" % s) for s in range(PASSES)]
        xs_sb = kept([P, T], U8, "xs_sb")
        early_planes = kept([P, EARLY], U8, "early_planes")
        a_planes = kept([P, M], U8, "a_planes")
        a_plane1 = kept([P, M], U8, "a_plane1")

        w1_halves = [placed([P, PASSES, 2 * N], U8, "w1_half%d" % n, 2 * KIB * n) for n in range(2)]
        w_sb = {e: placed([P, PASSES, 4 * N], U8, "w_sb%d" % e, 4 * KIB * max(e, 1)) for e in (0, 2, 3)}
        w45 = kept([P, 2 * PASSES, 4 * N], U8, "w45")
        for e in range(4, 6):
            w_sb[e] = w45[:, PASSES * (e - 4) : PASSES * (e - 3), :]
        for e in range(6, E):
            w_sb[e] = kept([P, PASSES, 4 * N], U8, "w_sb%d" % e)
        pair_words = [
            kept([P, PASSES * PAIR], U32, "pair_words0"),
            placed([P, PASSES * PAIR], U32, "pair_words1", 0),
            placed([P, PASSES * PAIR], U32, "pair_words2", 6 * KIB),
            placed([P, PASSES * PAIR], U32, "pair_words3", 10 * KIB),
        ]
        a_words = [placed([P, PASSES * D], U32, "a_words%d" % f, 2 * KIB * (f + 1)) for f in range(F)]
        late_planes = placed([P, T - EARLY], U8, "late_planes", 12 * KIB)

        ws_sb = [kept([P, N], U8, "ws_sb%d" % g) for g in range(len(WS_GROUPS))]
        wa_sb = kept([P, F * PASSES, 2 * H], U8, "wa_sb")
        was_sb = kept([P, F * PASSES, H], U8, "was_sb")
        wb_sb = kept([P, F, 2 * N], U8, "wb_sb")
        wbs_sb = kept([P, F, N], U8, "wbs_sb")
        h_rows = [kept([P, D // P, H], BF16, "h_rows%d" % f) for f in range(F)]
        h_in = [kept([P, 4 * D], BF16, "h_in%d" % f) for f in range(F)]
        h_codes = [kept([P, D], U32, "h_codes%d" % f) for f in range(F)]
        h_scales = [kept([P, D], U8, "h_scales%d" % f) for f in range(F)]
        gate_rows = kept([P, P], F32, "gate_rows")
        gate_wide = kept([P, E, P], F32, "gate_wide")
        gates = [kept([P, N], F32, "gates%d" % b) for b in range(2)]
        gate2_sb = kept([P, M], F32, "gate2_sb")
        zero_col = kept([P, 1], F32, "zero_col")
        ident = kept([P, P], F32, "ident")
        o_sb = [kept([P, T], F32, "o_sb%d" % j) for j in range(NT)]
        z_sb = [kept([P, T], F32, "z_sb%d" % j) for j in range(NT)]
        y = kept([P, NT, T], F32, "y")
        z = kept([P, len(Z_PARTS), D], F32, "z")
        banks = [psum.tile([P, N], F32, name="bank%d" % b) for b in range(8)]

        def zero(tile_ap):
            nc.vector.memset(tile_ap.bitcast(I32), 0)

        nc.gpsimd.memset(xs_sb[:].bitcast(I32), 0)
        nc.gpsimd.memset(gate_rows[:], 0.0)
        nc.gpsimd.memset(zero_col[:], 0.0)
        make_identity(nc, ident[:])
        zero(was_sb[:].rearrange("p a n -> p (a n)"))
        for g in range(len(WS_GROUPS)):
            zero(ws_sb[g][:])
        zero(a_plane1[:])
        zero(wbs_sb[:].rearrange("p a n -> p (a n)"))
        nc.scalar.activation(z_sb[0][:], zero_col[:].to_broadcast([P, T]), SILU)

        def load(dst, src, queue=nc.sync):
            queue.dma_start(dst.bitcast(I32), src.bitcast(I32))

        def load_planes(dst, src, queue=nc.sync):
            for r in range(ROWS):
                load(dst[r:P:32, :, :], src[:, r :: ROWS, :].rearrange("a q n -> q a n"), queue)

        load_planes(was_sb[:], wa_scales.rearrange("f s b n -> (f s) b n"), nc.gpsimd)
        load_planes(wbs_sb[:], wb_scales.rearrange("f s b n -> (f s) b n"), nc.gpsimd)
        for j in range(1, NT):
            nc.gpsimd.memset(z_sb[j][:], 0.0)

        w_rows = w_words.rearrange("e s p n d -> p (e s) (n d)")
        ws_rows = w_scales.rearrange("e s b n -> (e s) b n")

        def load_ws(g):
            group = WS_GROUPS[g]
            for q in range(QUADS):
                load(
                    ws_sb[g][32 * q : 32 * q + ROWS * len(group), :],
                    ws_rows[group.start : group.stop : group.step, ROWS * q : ROWS * (q + 1), :],
                )

        def load_w(e):
            load(w_sb[e][:], w_rows[:, PASSES * e : PASSES * (e + 1), :])

        def load_w1(n):
            load(w1_halves[n][:], w_rows[:, PASSES : 2 * PASSES, 2 * N * n : 2 * N * (n + 1)])

        nc.sync.dma_start(offs_sb[:], offs)
        for q in range(QUADS):
            load(xs_sb[32 * q : 32 * q + PASSES * ROWS, :], x_scales[:, ROWS * q : ROWS * (q + 1), :])
        nc.sync.dma_start(gate_rows[0:E, :], gate[0].rearrange("(e p) -> e p", p=P))
        for s in range(PASSES):
            load(x_sb[s][:], x_words[s].rearrange("p t d -> p (t d)"))
        nc.sync.dma_start(offs2_sb[:], offs2)
        load_w1(0)
        load_ws(0)
        load_w1(1)
        load_w(0)
        load_ws(1)
        load_w(2)
        load_ws(2)
        load(wa_sb[:], wa_words.rearrange("f s p n -> p (f s) n"))

        nc.tensor.transpose(banks[7][:, 0:P], gate_rows[:], ident[:])
        for b in range(2):
            group = slice(4 * b, 4 * (b + 1))
            nc.scalar.copy(gate_wide[:, group, :], banks[7][:, group].unsqueeze(2).to_broadcast([P, 4, P]))
        for b in range(2):
            bank = banks[5 + b]
            for u in range(4):
                nc.tensor.transpose(bank[:, u * P : (u + 1) * P], gate_wide[:, 4 * b + u, :], ident[:])
            nc.scalar.copy(gates[b][:], bank[:])

        def slots(lo, hi):
            return offs_sb[:, lo // 16 : hi // 16]

        def a_slots(f):
            return offs2_sb[:, f * D // 16 : (f + 1) * D // 16]

        def gather_words(dst, offsets):
            width = dst.shape[1] // PASSES
            for s in range(PASSES):
                nc.vector.tensor_copy(dst[:, s * width : (s + 1) * width], x_sb[s][:].bitcast(U32).indirect(offsets))

        def gather_bytes(dst, offsets):
            nc.vector.tensor_copy(dst[:], xs_sb[:].indirect(offsets))

        def gather_pair(n):
            gather_words(pair_words[n], slots(n * PAIR, (n + 1) * PAIR))

        def w_plane(e, s):
            g = [2 * e + s in group for group in WS_GROUPS].index(True)
            return ws_sb[g][ROWS * list(WS_GROUPS[g]).index(2 * e + s) : P, :]

        def expert(e, bank, tiles=range(NT)):
            planes, first = (early_planes, e * C) if e * C < EARLY else (late_planes, e * C - EARLY)
            for n, j in enumerate(tiles):
                for s in range(PASSES):
                    if e == 1:
                        w_tile = w1_halves[j // 2][:, s, 4 * P * (j % 2) : 4 * P * (j % 2 + 1)]
                    else:
                        w_tile = w_sb[e][:, s, 4 * P * j : 4 * P * (j + 1)]
                    at = s * PAIR + e % 2 * C
                    nc.tensor.matmul_mx(
                        out=bank[:, n * C : (n + 1) * C],
                        lhsT=w_tile.bitcast(FP8X4),
                        lhsT_scale=w_plane(e, s)[:, j * P : (j + 1) * P],
                        rhs=pair_words[e // 2][:, at : at + C].bitcast(FP8X4),
                        rhs_scale=planes[ROWS * s : P, first : first + C],
                        start=(s == 0),
                        stop=(s == PASSES - 1),
                    )
            g = gates[e // 4][:, e % 4 * C : (e % 4 + 1) * C]
            nc.vector.tensor_tensor(
                y[:, tiles.start : tiles.stop, e * C : (e + 1) * C],
                bank[:, 0 : len(tiles) * C].rearrange("p (j c) -> p j c", c=C),
                g.unsqueeze(1).to_broadcast([P, len(tiles), C]),
                MULT,
            )

        def scatter_on_scalar(j, lo, hi):
            nc.scalar.activation(o_sb[j][:].indirect(slots(lo, hi)), y[:, j, lo:hi], COPY)

        def scatter_on_vector(j, lo, hi):
            nc.vector.tensor_copy(o_sb[j][:].indirect(slots(lo, hi)), y[:, j, lo:hi])

        def scatter_z(part):
            j, f = Z_PARTS[part]
            nc.scalar.activation(z_sb[j][:].indirect(a_slots(f)), z[:, part, :], COPY)

        def adapter_in(u, sums):
            f = u * P // D
            cols = slice(u * P, (u + 1) * P)
            for s in range(PASSES):
                nc.tensor.matmul_mx(
                    out=sums[:],
                    lhsT=a_words[f][:, s * D + u * P % D : s * D + u * P % D + P].bitcast(FP8X4),
                    lhsT_scale=(a_planes, a_plane1)[s][:, cols],
                    rhs=wa_sb[:, f * PASSES + s, :].bitcast(FP4X4),
                    rhs_scale=was_sb[:, f * PASSES + s, :],
                    start=(s == 0),
                    stop=(s == PASSES - 1),
                )
            nc.scalar.activation(
                h_rows[f][:, u % 2, :].rearrange("m (v p e) -> m v p e", v=2, e=2),
                sums[:].rearrange("m (p v e) -> m v p e", v=2, e=2),
                SILU,
            )

        def turn_h(f, turned):
            for b in range(D // P):
                pairs = h_rows[f][:, b, :].bitcast(F32)
                for v in range(2):
                    at = v * D + b * P
                    nc.tensor.transpose(turned[:, at : at + P], pairs[:, v * P : (v + 1) * P], ident[:])
            nc.vector.tensor_copy(
                h_in[f][:].bitcast(F32).rearrange("p (m v) -> p m v", v=2),
                turned[:].rearrange("p (v m) -> p m v", v=2),
            )

        def quantize_h(f):
            nc.vector.quantize_mx(out=h_codes[f][:].bitcast(FP8X4), scales=h_scales[f][:], in_=h_in[f][:])

        def adapter_out(first, bank):
            for n in range(2):
                j, f = Z_PARTS[first + n]
                nc.tensor.matmul_mx(
                    out=bank[:, n * D : (n + 1) * D],
                    lhsT=wb_sb[:, f, 2 * P * j : 2 * P * (j + 1)].bitcast(FP4X4),
                    lhsT_scale=wbs_sb[:, f, j * P : (j + 1) * P],
                    rhs=h_codes[f][:].bitcast(FP8X4),
                    rhs_scale=h_scales[f][:],
                    start=True,
                    stop=True,
                )
            if Z_PARTS[first][1] == f:
                q = gate2_sb[:, f * D : (f + 1) * D].unsqueeze(1).to_broadcast([P, 2, D])
            else:
                q = gate2_sb[:].rearrange("p (f m) -> p f m", f=F)
            nc.vector.tensor_tensor(z[:, first : first + 2, :], bank[:].rearrange("p (j m) -> p j m", j=2), q, MULT)

        gather_bytes(early_planes, slots(0, EARLY))
        gather_pair(0)
        gather_bytes(a_planes, offs2_sb[:])

        for r in range(ROWS):
            load(a_plane1[r:P:32, :], a_planes[ROWS + r : P : 32, :])
        load_w(3)
        load_ws(3)
        load(w45[:], w_rows[:, 4 * PASSES : 6 * PASSES, :])
        load_w(6)
        load_ws(4)
        load(wb_sb[:], wb_words.rearrange("f s p n -> p (f s) n"))
        nc.sync.dma_start(gate2_sb[:], gate2)
        load_w(7)

        expert(1, banks[0], range(0, 2))
        gather_pair(1)
        expert(1, banks[1], range(2, NT))
        gather_words(a_words[0], a_slots(0))
        for n in range(2):
            expert(0, banks[2 + n], range(2 * n, 2 * n + 2))
        gather_words(a_words[1], a_slots(1))
        gather_pair(2)
        expert(2, banks[4])
        gather_pair(3)
        for e in (1, 0):
            for j in range(NT):
                scatter_on_scalar(j, e * C, (e + 1) * C)
        scatter_on_vector(2, 2 * C, 3 * C)
        for n in range(2):
            expert(3, banks[2 * n], range(2 * n, 2 * n + 2))
        gather_bytes(late_planes, slots(EARLY, T))
        for u in range(M // P):
            adapter_in(u, banks[(5, 6, 7, 1)[u]])
        scatter_on_vector(2, 3 * C, 4 * C)
        for f in range(F):
            turn_h(f, banks[2 * f])
        quantize_h(0)
        expert(4, banks[3])
        quantize_h(1)
        for j in (0, 3, 1):
            scatter_on_scalar(j, 2 * C, LATE[j])
        expert(5, banks[4])
        scatter_on_scalar(2, 4 * C, LATE[2])
        expert(6, banks[5])
        for b in range(NT - 1):
            adapter_out(2 * b, banks[(6, 7, 1)[b]])
        expert(7, banks[6])
        adapter_out(2 * (NT - 1), banks[0])
        for part in Z_ORDER:
            scatter_z(part)
        for j in range(NT):
            scatter_on_vector(j, LATE[j], T)
            if j < NT - 1:
                nc.gpsimd.tensor_tensor(z_sb[j][:], o_sb[j][:], z_sb[j][:], ADD)
                nc.sync.dma_start(out[j * P : (j + 1) * P, :], z_sb[j][:])
        j = NT - 1
        for lo in range(0, T, LAST):
            cols = slice(lo, lo + LAST)
            nc.vector.tensor_tensor(o_sb[j - 1][:, cols], o_sb[j][:, cols], z_sb[j][:, cols], ADD)
            nc.sync.dma_start(out[j * P : (j + 1) * P, cols], o_sb[j - 1][:, cols])
